import numpy as np
import ml_dtypes


def mxq(x, axis, fmt="e4m3"):
    dtype, down = {"e4m3": (ml_dtypes.float8_e4m3fn, 7), "e5m2": (ml_dtypes.float8_e5m2, 14)}[fmt]
    v = np.moveaxis(np.asarray(x, np.float32).astype(ml_dtypes.bfloat16).astype(np.float64), axis, -1)
    blocks = v.reshape(v.shape[:-1] + (-1, 32))
    amax = np.abs(blocks).max(-1, keepdims=True)
    byte = np.maximum(np.where(amax > 0, np.frexp(amax)[1] - 1 + 127, 0) - down, 1)
    scale = np.exp2(byte - 127.0)
    codes = (blocks / scale).astype(np.float32).astype(dtype).astype(np.float64)
    return np.moveaxis((codes * scale).reshape(v.shape), -1, axis)


WIDE = False


def mx_kscale(k):
    if not WIDE:
        return np.ones(k)
    levels = np.array([10, -10, 5, -5, 0])
    if k % 512:
        return np.exp2(np.random.permutation(np.resize(levels, k // 32))).repeat(32)
    a = np.empty((k // 512, 16))
    for p in range(k // 512):
        a[p, :8] = np.random.permutation(np.resize(levels, 8))
        for g in range(8):
            far = levels[np.abs(levels - a[p, g]) >= 10]
            a[p, g + 8] = far[np.random.randint(len(far))]
    return np.exp2(a.ravel()).repeat(32)


def f64(x):
    return np.asarray(x).astype(np.float64)


def striped(idx):
    return np.tile(idx.reshape(-1, 16).T, (8, 1)).astype(np.uint16)


def unstriped(offs):
    return offs[:16].T.reshape(-1).astype(np.int64)


E2M1 = np.array([0.0, 0.5, 1.0, 1.5, 2.0, 3.0, 4.0, 6.0, -0.0, -0.5, -1.0, -1.5, -2.0, -3.0, -4.0, -6.0])


def pack_weight(w, fmt):
    k, n = w.shape
    w = f64(np.asarray(w, np.float32).astype(ml_dtypes.bfloat16)).reshape(k // 32, 32, n)
    amax = np.abs(w).max(1)
    if fmt == "e4m3":
        byte = np.frexp(amax)[1] - 1 + 127 - 7
    else:
        mant, ex = np.frexp(amax / 6.0)
        byte = np.where(mant > 0.5, ex, ex - 1) + 127
    byte = np.clip(np.where(amax > 0, byte, 1), 1, 254)
    scaled = (w * np.exp2(127.0 - byte)[:, None, :]).reshape(k, n).astype(np.float32)
    by_word = np.ascontiguousarray(scaled.reshape(k // 512, 128, 4, n).transpose(0, 1, 3, 2))
    if fmt == "e4m3":
        words = by_word.astype(ml_dtypes.float8_e4m3fn).view(np.uint8)
    else:
        c = by_word.astype(ml_dtypes.float4_e2m1fn).view(np.uint8) & 0xF
        words = (c[..., 0::2] | (c[..., 1::2] << 4)).reshape(k // 512, 128, 2 * n)
    return np.ascontiguousarray(words), np.ascontiguousarray(byte.astype(np.uint8).reshape(k // 512, 16, n))


def unpack_weight(words, scales, fmt):
    g, _, n = scales.shape
    words = np.ascontiguousarray(words).reshape(g, 128, n, -1)
    if fmt == "e4m3":
        vals = words.view(ml_dtypes.float8_e4m3fn).astype(np.float64)
    else:
        nib = np.empty((g, 128, n, 4), np.uint8)
        nib[..., 0::2] = words & 0xF
        nib[..., 1::2] = words >> 4
        vals = E2M1[nib]
    vals = vals * np.repeat(np.exp2(scales.astype(np.float64) - 127.0), 8, axis=1)[..., None]
    return vals.transpose(0, 1, 3, 2).reshape(g * 512, n)


def gelu(v):
    return 0.5 * v * (1.0 + np.tanh(np.sqrt(2.0 / np.pi) * (v + 0.044715 * v**3)))


def striped8(idx):
    return np.concatenate([v.reshape(-1, 16).T for v in idx]).astype(np.uint16)


def unstriped8(offs):
    return np.stack([offs[16 * g:16 * g + 16].T.reshape(-1) for g in range(8)]).astype(np.int64)


def runs(v, idx8):
    k = np.arange(v.shape[0])
    return v[k[:, None], idx8[k % 512 // 64]]


K, K2, H, N, T, S, G = 1024, 512, 1024, 512, 2048, 1024, 8

def setup_inputs():
    n = np.random.standard_normal
    s = mx_kscale(K)[:, None]
    s2 = mx_kscale(K2)[:, None]
    u = mx_kscale(H)[:, None]
    tab_words, tab_scales = pack_weight(n((K, T)) * s, "e4m3")
    tab2_words, tab2_scales = pack_weight(n((K2, T)) * s2, "e4m3")
    w1_words, w1_scales = pack_weight(n((K, H)) / np.sqrt(K) / s * u.T, "e2m1")
    offs = striped8(np.stack([np.random.permutation(T)[:S] for _ in range(G)]))
    return {
        "tab_words": tab_words, "tab_scales": tab_scales, "offs": offs,
        "tab2_words": tab2_words, "tab2_scales": tab2_scales,
        "offs2": striped(np.random.permutation(T)[:S]),
        "w1_words": w1_words, "w1_scales": w1_scales,
        "w2": (n((K2, H)) / np.sqrt(K2) / s2).astype(np.float32),
        "w3": (n((H, N)) / np.sqrt(H) / u).astype(np.float32),
        "bias": (0.5 * n(N)).astype(np.float32),
    }

def reference(tab_words, tab_scales, offs, tab2_words, tab2_scales, offs2,
              w1_words, w1_scales, w2, w3, bias):
    v = runs(unpack_weight(tab_words, tab_scales, "e4m3"), unstriped8(offs))
    v2 = unpack_weight(tab2_words, tab2_scales, "e4m3")[:, unstriped(offs2)]
    w1 = unpack_weight(w1_words, w1_scales, "e2m1")
    site = w1.T @ v
    window = mxq(f64(w2), 0, "e4m3").T @ v2
    h = site * window
    y = mxq(f64(w3), 0, "e4m3").T @ mxq(h, 0, "e4m3")
    return y + f64(bias)[:, None]

@@ -1,0 +1,266 @@
+from contextlib import ExitStack
+
+import concourse.mybir as mybir
+
+K, K2, H, N, T, S = 1024, 512, 1024, 512, 2048, 1024
+FLOPS = 2 * S * (K * H + K2 * H + H * N)
+
+F32 = mybir.dt.float32
+BF16 = mybir.dt.bfloat16
+I32 = mybir.dt.int32
+U32 = mybir.dt.uint32
+U16 = mybir.dt.uint16
+U8 = mybir.dt.uint8
+FP8X4 = mybir.dt.float8_e4m3fn_x4
+FP4X4 = mybir.dt.float4_e2m1fn_x4
+MULT = mybir.AluOpType.mult
+ADD = mybir.AluOpType.add
+IDENT = mybir.ActivationFunctionType.Identity
+
+P = 128
+HALF = 512
+CHUNK = 128
+PAIR = 256
+
+
+def tile_list_guide_cleavage_scores_kernel(
+    tc, tab_words, tab_scales, offs, tab2_words, tab2_scales, offs2, w1_words, w1_scales, w2, w3, bias, out
+):
+    nc = tc.nc
+    with ExitStack() as ctx:
+        keep = ctx.enter_context(tc.tile_pool(name="keep", bufs=1))
+        ring = ctx.enter_context(tc.tile_pool(name="ring", bufs=6))
+        psum = ctx.enter_context(tc.psum_pool(name="psum", bufs=1))
+
+        def held(shape, dtype, name, tag=None):
+            return keep.tile(shape, dtype, name=name, tag=tag or name, align_bytes=64)
+
+        def load_w2(b, tag):
+            raw = held([P, 4, HALF], F32, f"w2_raw{b}", tag)
+            nc.sync.dma_start(raw[:], w2.rearrange("(p s) n -> p s n", s=4)[:, :, b * HALF : (b + 1) * HALF])
+            return raw
+
+        def load_w3(b, tag):
+            raw = held([P, 4, N], F32, f"w3_raw{b}", tag)
+            rows = w3[b * HALF : (b + 1) * HALF, :].rearrange("(u t i) n -> t u i n", t=4, i=8)
+            for t in range(4):
+                nc.sync.dma_start(raw[:, t, :], rows[t])
+            return raw
+
+        list1 = keep.tile([P, S // 16], U16, name="list1")
+        list2 = keep.tile([P, S // 16], U16, name="list2")
+        nc.sync.dma_start(list1[:], offs)
+        bias_raw = held([P, N // P], F32, "bias_raw")
+        with nc.allow_non_contiguous_dma(reason="bias onto partitions"):
+            nc.scalar.dma_start(bias_raw[:], bias.rearrange("(c p) -> p c", p=P))
+
+        scale_win = held([P, T], U8, "scale_win", "slotA")
+        for a in range(2):
+            for r in range(2):
+                rows = tab_scales[a, r::2, :].bitcast(I32)
+                nc.sync.dma_start(
+                    scale_win[2 * a + r :: 4, :].bitcast(I32), rows.unsqueeze(1).to_broadcast([8, 4, T // 4])
+                )
+        table = [held([P, T], I32, "table0", "slotC")]
+        nc.sync.dma_start(table[0][:], tab_words[0].rearrange("p t i -> p (t i)").bitcast(I32))
+        nc.sync.dma_start(list2[:], offs2)
+
+        w1s_raw = held([P, 2, H // 4], I32, "w1s_raw", "slotD")
+        scale_win2 = held([P, T // 4], I32, "scale_win2", "slotF")
+        plane = [held([P, S // 4], I32, f"plane{a}") for a in range(2)]
+        nc.gpsimd.memset(w1s_raw[:], 0)
+        nc.vector.memset(scale_win2[:], 0)
+        nc.vector.memset(plane[0][:], 0)
+        nc.vector.memset(plane[1][:], 0)
+        for e in range(4):
+            nc.sync.dma_start(w1s_raw[e::32], w1_scales[:, e::4, :].rearrange("a d n -> d a n").bitcast(I32))
+        w1_raw = held([P, 2, H // 2], I32, "w1_raw", "slotB")
+        nc.sync.dma_start(w1_raw[:], w1_words.rearrange("a p n -> p a n").bitcast(I32))
+        table.append(held([P, T], I32, "table1", "slotG"))
+        nc.sync.dma_start(table[1][:], tab_words[1].rearrange("p t i -> p (t i)").bitcast(I32))
+        for e in range(4):
+            nc.gpsimd.dma_start(scale_win2[e::32], tab2_scales[0, e::4, :].bitcast(I32))
+        bias_col = held([P, N // P], F32, "bias_col")
+        nc.scalar.activation(bias_col[:], bias_raw[:], IDENT)
+
+        picked_scales = held([P, S], U8, "picked_scales")
+        nc.vector.tensor_copy(picked_scales[:], scale_win[:].indirect(list1[:]))
+        picked32 = picked_scales[:].bitcast(I32)
+
+        def move_plane(a):
+            for odd in range(2):
+                for r in range(2):
+                    nc.sync.dma_start(plane[a][2 * odd + r :: 32], picked32[16 * odd + 2 * a + r :: 32])
+
+        move_plane(0)
+        w2_raw = [load_w2(0, "slotA")]
+        move_plane(1)
+
+
+        def gather_words(window, lst, half, name, tag=None):
+            picked = held([P, HALF], U32, name, tag)
+            cols = slice(half * HALF // 16, (half + 1) * HALF // 16)
+            nc.vector.tensor_copy(picked[:], window[:].bitcast(U32).indirect(lst[:, cols]))
+            return picked
+
+        picked = [[gather_words(table[0], list1, half, f"picked0{half}") for half in range(2)]]
+        table2 = held([P, T], I32, "table2", "slotC")
+        nc.sync.dma_start(table2[:], tab2_words[0].rearrange("p t i -> p (t i)").bitcast(I32))
+
+        w1_ord = held([P, 2 * H // 2], I32, "w1_ord")
+        nc.vector.tensor_copy(
+            w1_ord[:].rearrange("p (g t u i) -> p g t u i", g=4, t=4, i=4),
+            w1_raw[:].rearrange("p a (b u t i) -> p (a b) t u i", b=2, t=4, i=4),
+        )
+        w2_raw.append(load_w2(1, "slotB"))
+        w1s_ord = held([P, 2 * H // 4], I32, "w1s_ord")
+        nc.vector.tensor_copy(
+            w1s_ord[:].rearrange("p (g t u i) -> p g t u i", g=4, t=4, i=2),
+            w1s_raw[:].rearrange("p a (b u t i) -> p (a b) t u i", b=2, t=4, i=2),
+        )
+        w3_raw = [load_w3(0, "slotD")]
+        picked.append([gather_words(table[1], list1, half, f"picked1{half}") for half in range(2)])
+
+        w2_bf, w3_bf = {}, {}
+
+        def cast_w2(b):
+            wb = held([P, HALF * 4], BF16, f"w2_bf{b}")
+            dst = wb[:].rearrange("p (t u x i s) -> p t u x s i", t=4, x=2, i=4, s=4)
+            src = w2_raw[b][:].rearrange("p s (u t x i) -> p t u x s i", t=4, x=2, i=4)
+            for t in range(4):
+                nc.scalar.copy(dst[:, t], src[:, t])
+            w2_bf[b] = wb
+
+        def cast_w3(b):
+            wb = held([P, N * 4], BF16, f"w3_bf{b}", f"slotH{b}")
+            dst = wb[:].rearrange("p (c n t) -> p c n t", c=4, t=4)
+            src = w3_raw[b][:].rearrange("p t (c n) -> p c n t", c=4)
+            for c in range(4):
+                nc.gpsimd.tensor_scalar(dst[:, c], src[:, c], 1.0, 0.0, MULT, ADD)
+            w3_bf[b] = wb
+
+        def quantize(values, width, name):
+            codes = held([P, width], U32, name + "_codes")
+            scales = held([P, width], U8, name + "_scales")
+            nc.vector.quantize_mx(out=codes[:].bitcast(FP8X4), scales=scales[:], in_=values)
+            return codes, scales
+
+        site = {}
+
+        def site_product(b, half):
+            sb = held([P, 4, HALF], F32, f"site{b}{half}")
+            for t in range(4):
+                bank = psum.tile([P, HALF], F32, name="site_bank", tag="bank", bufs=8)
+                for a in range(2):
+                    col = (2 * a + b) * HALF + t * P
+                    nc.tensor.matmul_mx(
+                        out=bank[:],
+                        lhsT=w1_ord[:].bitcast(U8)[:, 2 * col : 2 * (col + P)].bitcast(FP4X4),
+                        lhsT_scale=w1s_ord[:].bitcast(U8)[:, col : col + P],
+                        rhs=picked[a][half][:].bitcast(FP8X4),
+                        rhs_scale=plane[a][:].bitcast(U8)[:, half * HALF : (half + 1) * HALF],
+                        start=(a == 0),
+                        stop=(a == 1),
+                    )
+                nc.scalar.copy(sb[:, t, :], bank[:])
+            site[b, half] = sb
+
+        cast_w2(0)
+        site_product(0, 0)
+        picked_scales2 = held([P, S], U8, "picked_scales2", "slotG")
+        nc.vector.tensor_copy(picked_scales2[:], scale_win2[:].bitcast(U8).indirect(list2[:]))
+        w3_raw.append(load_w3(1, "slotF"))
+        picked2 = [gather_words(table2, list2, 0, "picked20")]
+        w2_q = [quantize(w2_bf[0][:], HALF, "w2q0")]
+        site_product(0, 1)
+
+        h_q = {}
+
+        def match(b, chunk, dst):
+            j0 = chunk * CHUNK
+            half, c0 = divmod(j0, HALF)
+            bank = psum.tile([P, 4, CHUNK], F32, name="window_bank", tag="bank", bufs=8)
+            for t in range(4):
+                nc.tensor.matmul_mx(
+                    out=bank[:, t, :],
+                    lhsT=w2_q[b][0][:, t * P : (t + 1) * P].bitcast(FP8X4),
+                    lhsT_scale=w2_q[b][1][:, t * P : (t + 1) * P],
+                    rhs=picked2[half][:, c0 : c0 + CHUNK].bitcast(FP8X4),
+                    rhs_scale=picked_scales2[:, j0 : j0 + CHUNK],
+                    start=True,
+                    stop=True,
+                )
+            nc.vector.tensor_tensor(
+                dst.rearrange("p (x i t) -> p x t i", i=2, t=4),
+                bank[:].rearrange("p t (x i) -> p x t i", i=2),
+                site[b, half][:, :, c0 : c0 + CHUNK].rearrange("p t (x i) -> p x t i", i=2),
+                MULT,
+            )
+
+        def score(j0, width, last):
+            pair, c0 = divmod(j0, PAIR)
+            for cc in range(2):
+                res = ring.tile([P, 2, width], F32, name="res")
+                bank = psum.tile([P, 2, width], F32, name="score_bank", tag="bank", bufs=8)
+                for k in range(2):
+                    c = 2 * cc + k
+                    for b in range(2):
+                        codes, scales = h_q[b, j0] if b else h_q[b, pair * PAIR]
+                        cols = slice(0, width) if b else slice(c0, c0 + width)
+                        nc.tensor.matmul_mx(
+                            out=bank[:, k, :],
+                            lhsT=w3_q[b][0][:, c * P : (c + 1) * P].bitcast(FP8X4),
+                            lhsT_scale=w3_q[b][1][:, c * P : (c + 1) * P],
+                            rhs=codes[:, cols].bitcast(FP8X4),
+                            rhs_scale=scales[:, cols],
+                            start=(b == 0),
+                            stop=(b == 1),
+                        )
+                for k in range(2):
+                    c = 2 * cc + k
+                    if last and cc == 1:
+                        nc.vector.tensor_scalar_add(res[:, k, :], bank[:, k, :], bias_col[:, c : c + 1])
+                    else:
+                        nc.scalar.activation(res[:, k, :], bank[:, k, :], IDENT, bias=bias_col[:, c : c + 1])
+                rows = out.rearrange("(c p) j -> p c j", p=P)
+                nc.sync.dma_start(rows[:, 2 * cc : 2 * cc + 2, j0 : j0 + width], res[:])
+
+        def finish(b, j0, width, values):
+            h_q[b, j0] = quantize(values, width, f"hq{b}_{j0}")
+            if b == 1:
+                score(j0, width, j0 + width == S)
+
+        w3_q = []
+        waiting = []
+        for b in range(2):
+            for pair in range(4):
+                if (b, pair) == (0, 1):
+                    cast_w2(1)
+                    site_product(1, 0)
+                    cast_w3(0)
+                    cast_w3(1)
+                if (b, pair) == (0, 2):
+                    picked2.append(gather_words(table2, list2, 1, "picked21"))
+                if (b, pair) == (0, 3):
+                    site_product(1, 1)
+                    w2_q.append(quantize(w2_bf[1][:], HALF, "w2q1"))
+                if (b, pair) == (1, 0):
+                    w3_q.append(quantize(w3_bf[0][:], N, "w3q0"))
+                if (b, pair) == (1, 1):
+                    w3_q.append(quantize(w3_bf[1][:], N, "w3q1"))
+                split = (b, pair) == (1, 3)
+                if not split:
+                    hb = held([P, PAIR * 4], BF16, f"h_bf{b}{pair}", f"slotH{pair}" if b == 1 and pair < 2 else None)
+                for sub in range(2):
+                    if split:
+                        part = held([P, CHUNK * 4], BF16, f"h_last{sub}")[:]
+                    else:
+                        part = hb[:, sub * CHUNK * 4 : (sub + 1) * CHUNK * 4]
+                    match(b, 2 * pair + sub, part)
+                    while waiting:
+                        finish(*waiting.pop(0))
+                    if split:
+                        waiting.append((b, pair * PAIR + sub * CHUNK, CHUNK, part))
+                if not split:
+                    waiting.append((b, pair * PAIR, PAIR, hb[:]))
+        finish(*waiting.pop(0))

@@ -148,22 +148,25 @@ def tile_list_guide_cleavage_scores_kernel(
         site = {}
 
         def site_product(b, half):
-            sb = held([P, 4, HALF], F32, f"site{b}{half}")
-            for t in range(4):
-                bank = psum.tile([P, HALF], F32, name="site_bank", tag="bank", bufs=8)
+            for chunk in range(4 * half, 4 * half + 4):
+                j0 = chunk * CHUNK
+                c0 = j0 % HALF
+                bank = psum.tile([P, 4, CHUNK], F32, name="site_bank", tag="bank", bufs=8)
                 for a in range(2):
-                    col = (2 * a + b) * HALF + t * P
-                    nc.tensor.matmul_mx(
-                        out=bank[:],
-                        lhsT=w1_ord[:].bitcast(U8)[:, 2 * col : 2 * (col + P)].bitcast(FP4X4),
-                        lhsT_scale=w1s_ord[:].bitcast(U8)[:, col : col + P],
-                        rhs=picked[a][half][:].bitcast(FP8X4),
-                        rhs_scale=plane[a][:].bitcast(U8)[:, half * HALF : (half + 1) * HALF],
-                        start=(a == 0),
-                        stop=(a == 1),
-                    )
-                nc.scalar.copy(sb[:, t, :], bank[:])
-            site[b, half] = sb
+                    for t in range(4):
+                        col = (2 * a + b) * HALF + t * P
+                        nc.tensor.matmul_mx(
+                            out=bank[:, t, :],
+                            lhsT=w1_ord[:].bitcast(U8)[:, 2 * col : 2 * (col + P)].bitcast(FP4X4),
+                            lhsT_scale=w1s_ord[:].bitcast(U8)[:, col : col + P],
+                            rhs=picked[a][half][:, c0 : c0 + CHUNK].bitcast(FP8X4),
+                            rhs_scale=plane[a][:].bitcast(U8)[:, j0 : j0 + CHUNK],
+                            start=(a == 0 and t == 0),
+                            stop=(a == 1 and t == 3),
+                        )
+                sb = held([P, CHUNK, 4], F32, f"site{b}{chunk}")
+                nc.scalar.copy(sb[:], bank[:].rearrange("p t j -> p j t"))
+                site[b, chunk] = sb
 
         cast_w2(0)
         site_product(0, 0)
@@ -191,9 +194,9 @@ def tile_list_guide_cleavage_scores_kernel(
                     stop=True,
                 )
             nc.vector.tensor_tensor(
-                dst.rearrange("p (x i t) -> p x t i", i=2, t=4),
-                bank[:].rearrange("p t (x i) -> p x t i", i=2),
-                site[b, half][:, :, c0 : c0 + CHUNK].rearrange("p t (x i) -> p x t i", i=2),
+                dst.rearrange("p (j t) -> p j t", t=4),
+                bank[:].rearrange("p t j -> p j t"),
+                site[b, chunk][:],
                 MULT,
             )
 

@@ -29,7 +29,6 @@ def tile_list_guide_cleavage_scores_kernel(
     nc = tc.nc
     with ExitStack() as ctx:
         keep = ctx.enter_context(tc.tile_pool(name="keep", bufs=1))
-        ring = ctx.enter_context(tc.tile_pool(name="ring", bufs=6))
         psum = ctx.enter_context(tc.psum_pool(name="psum", bufs=1))
 
         def held(shape, dtype, name, tag=None):
@@ -56,11 +55,9 @@ def tile_list_guide_cleavage_scores_kernel(
 
         scale_win = held([P, T], U8, "scale_win", "slotA")
         for a in range(2):
-            for r in range(2):
-                rows = tab_scales[a, r::2, :].bitcast(I32)
-                nc.sync.dma_start(
-                    scale_win[2 * a + r :: 4, :].bitcast(I32), rows.unsqueeze(1).to_broadcast([8, 4, T // 4])
-                )
+            for cols in (slice(0, T // 2), slice(T // 2, T)):
+                rows = tab_scales[a, :, cols].bitcast(I32)
+                nc.sync.dma_start(scale_win[a::2, cols].bitcast(I32), rows.unsqueeze(1).to_broadcast([16, 4, T // 8]))
         table = [held([P, T], I32, "table0", "slotC")]
         nc.sync.dma_start(table[0][:], tab_words[0].rearrange("p t i -> p (t i)").bitcast(I32))
         nc.sync.dma_start(list2[:], offs2)
@@ -79,7 +76,7 @@ def tile_list_guide_cleavage_scores_kernel(
         table.append(held([P, T], I32, "table1", "slotG"))
         nc.sync.dma_start(table[1][:], tab_words[1].rearrange("p t i -> p (t i)").bitcast(I32))
         for e in range(4):
-            nc.gpsimd.dma_start(scale_win2[e::32], tab2_scales[0, e::4, :].bitcast(I32))
+            nc.gpsimd.dma_start(scale_win2[4 + e :: 32], tab2_scales[0, e::4, :].bitcast(I32))
         bias_col = held([P, N // P], F32, "bias_col")
         nc.scalar.activation(bias_col[:], bias_raw[:], IDENT)
 
@@ -88,9 +85,8 @@ def tile_list_guide_cleavage_scores_kernel(
         picked32 = picked_scales[:].bitcast(I32)
 
         def move_plane(a):
-            for odd in range(2):
-                for r in range(2):
-                    nc.sync.dma_start(plane[a][2 * odd + r :: 32], picked32[16 * odd + 2 * a + r :: 32])
+            for e in range(4):
+                nc.sync.dma_start(plane[a][e::32], picked32[8 * e + a :: 32])
 
         move_plane(0)
         w2_raw = [load_w2(0, "slotA")]
@@ -103,7 +99,9 @@ def tile_list_guide_cleavage_scores_kernel(
             nc.vector.tensor_copy(picked[:], window[:].bitcast(U32).indirect(lst[:, cols]))
             return picked
 
-        picked = [[gather_words(table[0], list1, half, f"picked0{half}") for half in range(2)]]
+        picked0 = held([P, S], U32, "picked0")
+        nc.vector.tensor_copy(picked0[:], table[0][:].bitcast(U32).indirect(list1[:]))
+        picked = [[picked0[:, :HALF], picked0[:, HALF:]]]
         table2 = held([P, T], I32, "table2", "slotC")
         nc.sync.dma_start(table2[:], tab2_words[0].rearrange("p t i -> p (t i)").bitcast(I32))
 
@@ -125,10 +123,9 @@ def tile_list_guide_cleavage_scores_kernel(
 
         def cast_w2(b):
             wb = held([P, HALF * 4], BF16, f"w2_bf{b}")
-            dst = wb[:].rearrange("p (t u x i s) -> p t u x s i", t=4, x=2, i=4, s=4)
-            src = w2_raw[b][:].rearrange("p s (u t x i) -> p t u x s i", t=4, x=2, i=4)
-            for t in range(4):
-                nc.scalar.copy(dst[:, t], src[:, t])
+            dst = wb[:].rearrange("p (t u i s) -> p t u i s", t=4, i=8, s=4)
+            src = w2_raw[b][:].rearrange("p s (u t i) -> p t u i s", t=4, i=8)
+            nc.scalar.copy(dst, src)
             w2_bf[b] = wb
 
         def cast_w3(b):
@@ -177,8 +174,6 @@ def tile_list_guide_cleavage_scores_kernel(
         w2_q = [quantize(w2_bf[0][:], HALF, "w2q0")]
         site_product(0, 1)
 
-        h_q = {}
-
         def match(b, chunk, dst):
             j0 = chunk * CHUNK
             half, c0 = divmod(j0, HALF)
@@ -189,7 +184,7 @@ def tile_list_guide_cleavage_scores_kernel(
                     lhsT=w2_q[b][0][:, t * P : (t + 1) * P].bitcast(FP8X4),
                     lhsT_scale=w2_q[b][1][:, t * P : (t + 1) * P],
                     rhs=picked2[half][:, c0 : c0 + CHUNK].bitcast(FP8X4),
-                    rhs_scale=picked_scales2[:, j0 : j0 + CHUNK],
+                    rhs_scale=picked_scales2[4:, j0 : j0 + CHUNK],
                     start=True,
                     stop=True,
                 )
@@ -200,38 +195,41 @@ def tile_list_guide_cleavage_scores_kernel(
                 MULT,
             )
 
-        def score(j0, width, last):
-            pair, c0 = divmod(j0, PAIR)
-            for cc in range(2):
-                res = ring.tile([P, 2, width], F32, name="res")
-                bank = psum.tile([P, 2, width], F32, name="score_bank", tag="bank", bufs=8)
-                for k in range(2):
-                    c = 2 * cc + k
+        h_codes = [held([P, S], U32, f"h_codes{b}") for b in range(2)]
+        h_scales = [held([P, S], U8, f"h_scales{b}") for b in range(2)]
+        out_rows = out.rearrange("(c p) j -> p c j", p=P)
+
+        def score(j0, width):
+            cols = slice(j0, j0 + width)
+            per_bank = 2
+            for c0 in range(0, N // P, per_bank):
+                res = held([P, per_bank, width], F32, f"res{j0}_{c0}")
+                bank = psum.tile([P, per_bank, width], F32, name="score_bank", tag="bank", bufs=8)
+                for k in range(per_bank):
+                    c = c0 + k
                     for b in range(2):
-                        codes, scales = h_q[b, j0] if b else h_q[b, pair * PAIR]
-                        cols = slice(0, width) if b else slice(c0, c0 + width)
                         nc.tensor.matmul_mx(
                             out=bank[:, k, :],
                             lhsT=w3_q[b][0][:, c * P : (c + 1) * P].bitcast(FP8X4),
                             lhsT_scale=w3_q[b][1][:, c * P : (c + 1) * P],
-                            rhs=codes[:, cols].bitcast(FP8X4),
-                            rhs_scale=scales[:, cols],
+                            rhs=h_codes[b][:, cols].bitcast(FP8X4),
+                            rhs_scale=h_scales[b][:, cols],
                             start=(b == 0),
                             stop=(b == 1),
                         )
-                for k in range(2):
-                    c = 2 * cc + k
-                    if last and cc == 1:
+                for k in range(per_bank):
+                    c = c0 + k
+                    if width == CHUNK and c0:
                         nc.vector.tensor_scalar_add(res[:, k, :], bank[:, k, :], bias_col[:, c : c + 1])
                     else:
                         nc.scalar.activation(res[:, k, :], bank[:, k, :], IDENT, bias=bias_col[:, c : c + 1])
-                rows = out.rearrange("(c p) j -> p c j", p=P)
-                nc.sync.dma_start(rows[:, 2 * cc : 2 * cc + 2, j0 : j0 + width], res[:])
+                nc.sync.dma_start(out_rows[:, c0 : c0 + per_bank, cols], res[:])
 
         def finish(b, j0, width, values):
-            h_q[b, j0] = quantize(values, width, f"hq{b}_{j0}")
+            cols = slice(j0, j0 + width)
+            nc.vector.quantize_mx(out=h_codes[b][:, cols].bitcast(FP8X4), scales=h_scales[b][:, cols], in_=values)
             if b == 1:
-                score(j0, width, j0 + width == S)
+                score(j0, width)
 
         w3_q = []
         waiting = []
@@ -247,10 +245,8 @@ def tile_list_guide_cleavage_scores_kernel(
                 if (b, pair) == (0, 3):
                     site_product(1, 1)
                     w2_q.append(quantize(w2_bf[1][:], HALF, "w2q1"))
-                if (b, pair) == (1, 0):
-                    w3_q.append(quantize(w3_bf[0][:], N, "w3q0"))
-                if (b, pair) == (1, 1):
-                    w3_q.append(quantize(w3_bf[1][:], N, "w3q1"))
+                if b == 1 and pair < 2:
+                    w3_q.append(quantize(w3_bf[pair][:], N, f"w3q{pair}"))
                 split = (b, pair) == (1, 3)
                 if not split:
                     hb = held([P, PAIR * 4], BF16, f"h_bf{b}{pair}", f"slotH{pair}" if b == 1 and pair < 2 else None)

@@ -21,6 +21,7 @@ P = 128
 HALF = 512
 CHUNK = 128
 PAIR = 256
+LAP = 64
 
 
 def tile_list_guide_cleavage_scores_kernel(
@@ -29,95 +30,88 @@ def tile_list_guide_cleavage_scores_kernel(
     nc = tc.nc
     with ExitStack() as ctx:
         keep = ctx.enter_context(tc.tile_pool(name="keep", bufs=1))
+        placed = ctx.enter_context(tc.tile_pool(name="placed", bufs=1))
         psum = ctx.enter_context(tc.psum_pool(name="psum", bufs=1))
 
         def held(shape, dtype, name, tag=None):
             return keep.tile(shape, dtype, name=name, tag=tag or name, align_bytes=64)
 
-        def load_w2(b, tag):
-            raw = held([P, 4, HALF], F32, f"w2_raw{b}", tag)
+        raw_bytes = 4 * HALF * 4
+        w1_at = 0
+        scale_at = w1_at + 2 * H * 2
+        picked_at = scale_at + T
+        w2a_at = picked_at + S - LAP
+        table1_at = w2a_at + raw_bytes
+
+        def at(shape, dtype, name, offset):
+            return placed.tile(shape, dtype, name=name, offset=offset, align_bytes=64)
+
+        def load_w2(b, raw):
             nc.sync.dma_start(raw[:], w2.rearrange("(p s) n -> p s n", s=4)[:, :, b * HALF : (b + 1) * HALF])
             return raw
 
-        def load_w3(b, tag):
-            raw = held([P, 4, N], F32, f"w3_raw{b}", tag)
+        def load_w3(b, raw):
             rows = w3[b * HALF : (b + 1) * HALF, :].rearrange("(u t i) n -> t u i n", t=4, i=8)
             for t in range(4):
                 nc.sync.dma_start(raw[:, t, :], rows[t])
             return raw
 
+        def load_table(words, tile):
+            nc.sync.dma_start(tile[:], words.rearrange("p t i -> p (t i)").bitcast(I32))
+            return tile
+
         list1 = keep.tile([P, S // 16], U16, name="list1")
         list2 = keep.tile([P, S // 16], U16, name="list2")
-        nc.sync.dma_start(list1[:], offs)
-        bias_raw = held([P, N // P], F32, "bias_raw")
-        with nc.allow_non_contiguous_dma(reason="bias onto partitions"):
-            nc.scalar.dma_start(bias_raw[:], bias.rearrange("(c p) -> p c", p=P))
-
-        scale_win = held([P, T], U8, "scale_win", "slotA")
-        for a in range(2):
-            for cols in (slice(0, T // 2), slice(T // 2, T)):
-                rows = tab_scales[a, :, cols].bitcast(I32)
-                nc.sync.dma_start(scale_win[a::2, cols].bitcast(I32), rows.unsqueeze(1).to_broadcast([16, 4, T // 8]))
-        table = [held([P, T], I32, "table0", "slotC")]
-        nc.sync.dma_start(table[0][:], tab_words[0].rearrange("p t i -> p (t i)").bitcast(I32))
-        nc.sync.dma_start(list2[:], offs2)
-
-        w1s_raw = held([P, 2, H // 4], I32, "w1s_raw", "slotD")
-        scale_win2 = held([P, T // 4], I32, "scale_win2", "slotF")
-        plane = [held([P, S // 4], I32, f"plane{a}") for a in range(2)]
-        nc.gpsimd.memset(w1s_raw[:], 0)
+        scale_win = at([P, T], U8, "scale_win", scale_at)
+        w1s_raw = held([P, H // 4], I32, "w1s_raw")
+        scale_win2 = held([P, T // 4], I32, "scale_win2", "slot_scale2")
+        planes = held([P, 2, (S + H) // 4], I32, "planes")
+        nc.gpsimd.memset(scale_win[:].bitcast(I32), 0)
+        nc.vector.memset(w1s_raw[:], 0)
         nc.vector.memset(scale_win2[:], 0)
-        nc.vector.memset(plane[0][:], 0)
-        nc.vector.memset(plane[1][:], 0)
-        for e in range(4):
-            nc.sync.dma_start(w1s_raw[e::32], w1_scales[:, e::4, :].rearrange("a d n -> d a n").bitcast(I32))
-        w1_raw = held([P, 2, H // 2], I32, "w1_raw", "slotB")
+        nc.vector.memset(planes[:], 0)
+        nc.sync.dma_start(list1[:], offs)
+        nc.sync.dma_start(list2[:], offs2)
+        nc.sync.dma_start(scale_win[::4].bitcast(I32), tab_scales.rearrange("a q t -> q a t").bitcast(I32))
+        nc.sync.dma_start(w1s_raw[::4], w1_scales.rearrange("a q n -> q a n").bitcast(I32))
+        table = [load_table(tab_words[0], held([P, T], I32, "table0", "slot_table0"))]
+        table.append(load_table(tab_words[1], at([P, T], I32, "table1", table1_at)))
+        w1_raw = at([P, 2, H // 2], I32, "w1_raw", w1_at)
         nc.sync.dma_start(w1_raw[:], w1_words.rearrange("a p n -> p a n").bitcast(I32))
-        table.append(held([P, T], I32, "table1", "slotG"))
-        nc.sync.dma_start(table[1][:], tab_words[1].rearrange("p t i -> p (t i)").bitcast(I32))
         for e in range(4):
             nc.gpsimd.dma_start(scale_win2[4 + e :: 32], tab2_scales[0, e::4, :].bitcast(I32))
-        bias_col = held([P, N // P], F32, "bias_col")
-        nc.scalar.activation(bias_col[:], bias_raw[:], IDENT)
 
-        picked_scales = held([P, S], U8, "picked_scales")
+        rows = held([P, (S + H) // 4], I32, "rows", "slot_rows")
+        picked_scales = at([P, S], U8, "picked_scales", picked_at)
         nc.vector.tensor_copy(picked_scales[:], scale_win[:].indirect(list1[:]))
-        picked32 = picked_scales[:].bitcast(I32)
+        nc.vector.tensor_copy(
+            rows[:, S // 4 :].rearrange("p (b t u i) -> p b t u i", b=2, t=4, i=2),
+            w1s_raw[:].rearrange("p (b u t i) -> p b t u i", b=2, t=4, i=2),
+        )
+        nc.vector.tensor_copy(rows[:, : S // 4], picked_scales[:].bitcast(I32))
+        for d in range(4):
+            nc.sync.dma_start(planes[32 * d : 32 * d + 4], rows[32 * d : 32 * d + 32 : 4])
 
-        def move_plane(a):
-            for e in range(4):
-                nc.sync.dma_start(plane[a][e::32], picked32[8 * e + a :: 32])
+        w2_raw = [load_w2(0, at([P, 4, HALF], F32, "w2_raw0", w2a_at))]
+        table2 = load_table(tab2_words[0], held([P, T], I32, "table2", "slot_rows"))
 
-        move_plane(0)
-        w2_raw = [load_w2(0, "slotA")]
-        move_plane(1)
-
-
-        def gather_words(window, lst, half, name, tag=None):
-            picked = held([P, HALF], U32, name, tag)
+        def gather_words(window, lst, half, picked):
             cols = slice(half * HALF // 16, (half + 1) * HALF // 16)
             nc.vector.tensor_copy(picked[:], window[:].bitcast(U32).indirect(lst[:, cols]))
             return picked
 
-        picked0 = held([P, S], U32, "picked0")
-        nc.vector.tensor_copy(picked0[:], table[0][:].bitcast(U32).indirect(list1[:]))
-        picked = [[picked0[:, :HALF], picked0[:, HALF:]]]
-        table2 = held([P, T], I32, "table2", "slotC")
-        nc.sync.dma_start(table2[:], tab2_words[0].rearrange("p t i -> p (t i)").bitcast(I32))
+        picked = {(0, 0): gather_words(table[0], list1, 0, at([P, HALF], U32, "picked00", scale_at))}
+        picked[1, 0] = gather_words(table[1], list1, 0, held([P, HALF], U32, "picked10"))
 
         w1_ord = held([P, 2 * H // 2], I32, "w1_ord")
         nc.vector.tensor_copy(
             w1_ord[:].rearrange("p (g t u i) -> p g t u i", g=4, t=4, i=4),
             w1_raw[:].rearrange("p a (b u t i) -> p (a b) t u i", b=2, t=4, i=4),
         )
-        w2_raw.append(load_w2(1, "slotB"))
-        w1s_ord = held([P, 2 * H // 4], I32, "w1s_ord")
-        nc.vector.tensor_copy(
-            w1s_ord[:].rearrange("p (g t u i) -> p g t u i", g=4, t=4, i=2),
-            w1s_raw[:].rearrange("p a (b u t i) -> p (a b) t u i", b=2, t=4, i=2),
-        )
-        w3_raw = [load_w3(0, "slotD")]
-        picked.append([gather_words(table[1], list1, half, f"picked1{half}") for half in range(2)])
+        for a in range(2):
+            picked[a, 1] = gather_words(table[a], list1, 1, at([P, HALF], U32, f"picked{a}1", w1_at + a * HALF * 4))
+        w2_raw.append(load_w2(1, held([P, 4, HALF], F32, "w2_raw1", "slot_table0")))
+        w3_raw = [load_w3(0, at([P, 4, N], F32, "w3_raw0", table1_at + S))]
 
         w2_bf, w3_bf = {}, {}
 
@@ -125,11 +119,12 @@ def tile_list_guide_cleavage_scores_kernel(
             wb = held([P, HALF * 4], BF16, f"w2_bf{b}")
             dst = wb[:].rearrange("p (t u i s) -> p t u i s", t=4, i=8, s=4)
             src = w2_raw[b][:].rearrange("p s (u t i) -> p t u i s", t=4, i=8)
-            nc.scalar.copy(dst, src)
+            for t in range(4):
+                nc.scalar.activation(dst[:, t], src[:, t], IDENT)
             w2_bf[b] = wb
 
         def cast_w3(b):
-            wb = held([P, N * 4], BF16, f"w3_bf{b}", f"slotH{b}")
+            wb = held([P, N * 4], BF16, f"w3_bf{b}")
             dst = wb[:].rearrange("p (c n t) -> p c n t", c=4, t=4)
             src = w3_raw[b][:].rearrange("p t (c n) -> p c n t", c=4)
             for c in range(4):
@@ -144,46 +139,50 @@ def tile_list_guide_cleavage_scores_kernel(
 
         site = {}
 
-        def site_product(b, half):
-            for chunk in range(4 * half, 4 * half + 4):
+        def site_product(b, first, count):
+            for chunk in range(first, first + count):
                 j0 = chunk * CHUNK
-                c0 = j0 % HALF
-                bank = psum.tile([P, 4, CHUNK], F32, name="site_bank", tag="bank", bufs=8)
+                half, c0 = divmod(j0, HALF)
+                bank = psum.tile([P, 4, CHUNK], F32, name="site_bank", tag="site_bank", bufs=5)
                 for a in range(2):
                     for t in range(4):
                         col = (2 * a + b) * HALF + t * P
                         nc.tensor.matmul_mx(
                             out=bank[:, t, :],
                             lhsT=w1_ord[:].bitcast(U8)[:, 2 * col : 2 * (col + P)].bitcast(FP4X4),
-                            lhsT_scale=w1s_ord[:].bitcast(U8)[:, col : col + P],
-                            rhs=picked[a][half][:, c0 : c0 + CHUNK].bitcast(FP8X4),
-                            rhs_scale=plane[a][:].bitcast(U8)[:, j0 : j0 + CHUNK],
+                            lhsT_scale=planes[:, a, :].bitcast(U8)[:, S + b * HALF + t * P : S + b * HALF + (t + 1) * P],
+                            rhs=picked[a, half][:, c0 : c0 + CHUNK].bitcast(FP8X4),
+                            rhs_scale=planes[:, a, :].bitcast(U8)[:, j0 : j0 + CHUNK],
                             start=(a == 0 and t == 0),
                             stop=(a == 1 and t == 3),
                         )
                 sb = held([P, CHUNK, 4], F32, f"site{b}{chunk}")
-                nc.scalar.copy(sb[:], bank[:].rearrange("p t j -> p j t"))
+                nc.scalar.activation(sb[:], bank[:].rearrange("p t j -> p j t"), IDENT)
                 site[b, chunk] = sb
 
         cast_w2(0)
-        site_product(0, 0)
-        picked_scales2 = held([P, S], U8, "picked_scales2", "slotG")
+        site_product(0, 0, 4)
+        picked2 = held([P, S], U32, "picked2")
+        nc.vector.tensor_copy(picked2[:], table2[:].bitcast(U32).indirect(list2[:]))
+        w3_raw.append(load_w3(1, held([P, 4, N], F32, "w3_raw1", "slot_rows")))
+        picked_scales2 = at([P, S], U8, "picked_scales2", table1_at)
         nc.vector.tensor_copy(picked_scales2[:], scale_win2[:].bitcast(U8).indirect(list2[:]))
-        w3_raw.append(load_w3(1, "slotF"))
-        picked2 = [gather_words(table2, list2, 0, "picked20")]
+        bias_col = held([P, N // P], F32, "bias_col", "slot_scale2")
+        with nc.allow_non_contiguous_dma(reason="bias onto partitions"):
+            nc.sync.dma_start(bias_col[:], bias.rearrange("(c p) -> p c", p=P))
         w2_q = [quantize(w2_bf[0][:], HALF, "w2q0")]
-        site_product(0, 1)
+        cast_w2(1)
+        site_product(1, 0, 4)
 
         def match(b, chunk, dst):
             j0 = chunk * CHUNK
-            half, c0 = divmod(j0, HALF)
-            bank = psum.tile([P, 4, CHUNK], F32, name="window_bank", tag="bank", bufs=8)
+            bank = psum.tile([P, 4, CHUNK], F32, name="window_bank", tag="window_bank", bufs=3)
             for t in range(4):
                 nc.tensor.matmul_mx(
                     out=bank[:, t, :],
                     lhsT=w2_q[b][0][:, t * P : (t + 1) * P].bitcast(FP8X4),
                     lhsT_scale=w2_q[b][1][:, t * P : (t + 1) * P],
-                    rhs=picked2[half][:, c0 : c0 + CHUNK].bitcast(FP8X4),
+                    rhs=picked2[:, j0 : j0 + CHUNK].bitcast(FP8X4),
                     rhs_scale=picked_scales2[4:, j0 : j0 + CHUNK],
                     start=True,
                     stop=True,
@@ -201,10 +200,10 @@ def tile_list_guide_cleavage_scores_kernel(
 
         def score(j0, width):
             cols = slice(j0, j0 + width)
-            per_bank = 2
+            per_bank = min(2, HALF // width)
             for c0 in range(0, N // P, per_bank):
                 res = held([P, per_bank, width], F32, f"res{j0}_{c0}")
-                bank = psum.tile([P, per_bank, width], F32, name="score_bank", tag="bank", bufs=8)
+                bank = psum.tile([P, per_bank, width], F32, name="score_bank", tag="site_bank", bufs=5)
                 for k in range(per_bank):
                     c = c0 + k
                     for b in range(2):
@@ -225,41 +224,39 @@ def tile_list_guide_cleavage_scores_kernel(
                         nc.scalar.activation(res[:, k, :], bank[:, k, :], IDENT, bias=bias_col[:, c : c + 1])
                 nc.sync.dma_start(out_rows[:, c0 : c0 + per_bank, cols], res[:])
 
-        def finish(b, j0, width, values):
-            cols = slice(j0, j0 + width)
-            nc.vector.quantize_mx(out=h_codes[b][:, cols].bitcast(FP8X4), scales=h_scales[b][:, cols], in_=values)
-            if b == 1:
-                score(j0, width)
+        def matched(b, j0, width):
+            hb = held([P, width * 4], BF16, f"h_bf{b}_{j0}")
+            for k in range(width // CHUNK):
+                match(b, j0 // CHUNK + k, hb[:, k * CHUNK * 4 : (k + 1) * CHUNK * 4])
+            return hb
 
-        w3_q = []
-        waiting = []
-        for b in range(2):
-            for pair in range(4):
-                if (b, pair) == (0, 1):
-                    cast_w2(1)
-                    site_product(1, 0)
-                    cast_w3(0)
-                    cast_w3(1)
-                if (b, pair) == (0, 2):
-                    picked2.append(gather_words(table2, list2, 1, "picked21"))
-                if (b, pair) == (0, 3):
-                    site_product(1, 1)
-                    w2_q.append(quantize(w2_bf[1][:], HALF, "w2q1"))
-                if b == 1 and pair < 2:
-                    w3_q.append(quantize(w3_bf[pair][:], N, f"w3q{pair}"))
-                split = (b, pair) == (1, 3)
-                if not split:
-                    hb = held([P, PAIR * 4], BF16, f"h_bf{b}{pair}", f"slotH{pair}" if b == 1 and pair < 2 else None)
-                for sub in range(2):
-                    if split:
-                        part = held([P, CHUNK * 4], BF16, f"h_last{sub}")[:]
-                    else:
-                        part = hb[:, sub * CHUNK * 4 : (sub + 1) * CHUNK * 4]
-                    match(b, 2 * pair + sub, part)
-                    while waiting:
-                        finish(*waiting.pop(0))
-                    if split:
-                        waiting.append((b, pair * PAIR + sub * CHUNK, CHUNK, part))
-                if not split:
-                    waiting.append((b, pair * PAIR, PAIR, hb[:]))
-        finish(*waiting.pop(0))
+        def quantize_h(b, j0, width, hb):
+            cols = slice(j0, j0 + width)
+            nc.vector.quantize_mx(out=h_codes[b][:, cols].bitcast(FP8X4), scales=h_scales[b][:, cols], in_=hb[:])
+
+        first = matched(0, 0, HALF)
+        w2_q.append(quantize(w2_bf[1][:], HALF, "w2q1"))
+        quantize_h(0, 0, HALF, first)
+        site_product(0, 4, 2)
+        site_product(1, 4, 2)
+        cast_w3(0)
+        cast_w3(1)
+        second = matched(1, 0, HALF)
+        w3_q = [quantize(w3_bf[b][:], N, f"w3q{b}") for b in range(2)]
+        site_product(0, 6, 2)
+        site_product(1, 6, 2)
+        waiting = (1, 0, HALF, second)
+        for b, j0, width in (
+            (0, HALF, PAIR),
+            (1, HALF, PAIR),
+            (0, HALF + PAIR, PAIR),
+            (1, HALF + PAIR, CHUNK),
+            (1, S - CHUNK, CHUNK),
+        ):
+            hb = matched(b, j0, width)
+            quantize_h(*waiting)
+            if waiting[0] == 1:
+                score(*waiting[1:3])
+            waiting = (b, j0, width, hb)
+        quantize_h(*waiting)
+        score(*waiting[1:3])

@@ -38,8 +38,9 @@ def tile_list_guide_cleavage_scores_kernel(
 
         raw_bytes = 4 * HALF * 4
         w1_at = 0
-        scale_at = w1_at + 2 * H * 2
-        picked_at = scale_at + T
+        scale_at = w1_at + 2 * H * 2 + LAP
+        rows_at = scale_at + T - LAP
+        picked_at = rows_at + raw_bytes
         w2a_at = picked_at + S - LAP
         table1_at = w2a_at + raw_bytes
 
@@ -72,7 +73,7 @@ def tile_list_guide_cleavage_scores_kernel(
         nc.vector.memset(planes[:], 0)
         nc.sync.dma_start(list1[:], offs)
         nc.sync.dma_start(list2[:], offs2)
-        nc.sync.dma_start(scale_win[::4].bitcast(I32), tab_scales.rearrange("a q t -> q a t").bitcast(I32))
+        nc.scalar.dma_start(scale_win[::4].bitcast(I32), tab_scales.rearrange("a q t -> q a t").bitcast(I32))
         nc.sync.dma_start(w1s_raw[::4], w1_scales.rearrange("a q n -> q a n").bitcast(I32))
         table = [load_table(tab_words[0], held([P, T], I32, "table0", "slot_table0"))]
         table.append(load_table(tab_words[1], at([P, T], I32, "table1", table1_at)))
@@ -81,7 +82,7 @@ def tile_list_guide_cleavage_scores_kernel(
         for e in range(4):
             nc.gpsimd.dma_start(scale_win2[4 + e :: 32], tab2_scales[0, e::4, :].bitcast(I32))
 
-        rows = held([P, (S + H) // 4], I32, "rows", "slot_rows")
+        rows = at([P, (S + H) // 4], I32, "rows", rows_at)
         picked_scales = at([P, S], U8, "picked_scales", picked_at)
         nc.vector.tensor_copy(picked_scales[:], scale_win[:].indirect(list1[:]))
         nc.vector.tensor_copy(
@@ -93,14 +94,14 @@ def tile_list_guide_cleavage_scores_kernel(
             nc.sync.dma_start(planes[32 * d : 32 * d + 4], rows[32 * d : 32 * d + 32 : 4])
 
         w2_raw = [load_w2(0, at([P, 4, HALF], F32, "w2_raw0", w2a_at))]
-        table2 = load_table(tab2_words[0], held([P, T], I32, "table2", "slot_rows"))
+        table2 = load_table(tab2_words[0], at([P, T], I32, "table2", rows_at))
 
         def gather_words(window, lst, half, picked):
             cols = slice(half * HALF // 16, (half + 1) * HALF // 16)
             nc.vector.tensor_copy(picked[:], window[:].bitcast(U32).indirect(lst[:, cols]))
             return picked
 
-        picked = {(0, 0): gather_words(table[0], list1, 0, at([P, HALF], U32, "picked00", scale_at))}
+        picked = {(0, 0): gather_words(table[0], list1, 0, at([P, HALF], U32, "picked00", scale_at - LAP))}
         picked[1, 0] = gather_words(table[1], list1, 0, held([P, HALF], U32, "picked10"))
 
         w1_ord = held([P, 2 * H // 2], I32, "w1_ord")
@@ -131,8 +132,8 @@ def tile_list_guide_cleavage_scores_kernel(
                 nc.gpsimd.tensor_scalar(dst[:, c], src[:, c], 1.0, 0.0, MULT, ADD)
             w3_bf[b] = wb
 
-        def quantize(values, width, name):
-            codes = held([P, width], U32, name + "_codes")
+        def quantize(values, width, name, tag=None):
+            codes = held([P, width], U32, name + "_codes", tag)
             scales = held([P, width], U8, name + "_scales")
             nc.vector.quantize_mx(out=codes[:].bitcast(FP8X4), scales=scales[:], in_=values)
             return codes, scales
@@ -156,7 +157,7 @@ def tile_list_guide_cleavage_scores_kernel(
                             start=(a == 0 and t == 0),
                             stop=(a == 1 and t == 3),
                         )
-                sb = held([P, CHUNK, 4], F32, f"site{b}{chunk}")
+                sb = held([P, CHUNK, 4], F32, f"site{b}{chunk}", f"slot_site{b}{chunk}")
                 nc.scalar.activation(sb[:], bank[:].rearrange("p t j -> p j t"), IDENT)
                 site[b, chunk] = sb
 
@@ -164,7 +165,7 @@ def tile_list_guide_cleavage_scores_kernel(
         site_product(0, 0, 4)
         picked2 = held([P, S], U32, "picked2")
         nc.vector.tensor_copy(picked2[:], table2[:].bitcast(U32).indirect(list2[:]))
-        w3_raw.append(load_w3(1, held([P, 4, N], F32, "w3_raw1", "slot_rows")))
+        w3_raw.append(load_w3(1, at([P, 4, N], F32, "w3_raw1", rows_at)))
         picked_scales2 = at([P, S], U8, "picked_scales2", table1_at)
         nc.vector.tensor_copy(picked_scales2[:], scale_win2[:].bitcast(U8).indirect(list2[:]))
         bias_col = held([P, N // P], F32, "bias_col", "slot_scale2")
@@ -194,8 +195,7 @@ def tile_list_guide_cleavage_scores_kernel(
                 MULT,
             )
 
-        h_codes = [held([P, S], U32, f"h_codes{b}") for b in range(2)]
-        h_scales = [held([P, S], U8, f"h_scales{b}") for b in range(2)]
+        h_q = {}
         out_rows = out.rearrange("(c p) j -> p c j", p=P)
 
         def score(j0, width):
@@ -204,17 +204,17 @@ def tile_list_guide_cleavage_scores_kernel(
             for c0 in range(0, N // P, per_bank):
                 res = held([P, per_bank, width], F32, f"res{j0}_{c0}")
                 bank = psum.tile([P, per_bank, width], F32, name="score_bank", tag="site_bank", bufs=5)
-                for k in range(per_bank):
-                    c = c0 + k
-                    for b in range(2):
+                for b in range(2):
+                    for k in range(per_bank):
+                        c = c0 + k
                         nc.tensor.matmul_mx(
                             out=bank[:, k, :],
                             lhsT=w3_q[b][0][:, c * P : (c + 1) * P].bitcast(FP8X4),
                             lhsT_scale=w3_q[b][1][:, c * P : (c + 1) * P],
-                            rhs=h_codes[b][:, cols].bitcast(FP8X4),
-                            rhs_scale=h_scales[b][:, cols],
-                            start=(b == 0),
-                            stop=(b == 1),
+                            rhs=h_q[b, j0][0][:, :width].bitcast(FP8X4),
+                            rhs_scale=h_q[b, j0][1][:, :width],
+                            start=(b == 0 and k == 0),
+                            stop=(b == 1 and k == per_bank - 1),
                         )
                 for k in range(per_bank):
                     c = c0 + k
@@ -230,18 +230,19 @@ def tile_list_guide_cleavage_scores_kernel(
                 match(b, j0 // CHUNK + k, hb[:, k * CHUNK * 4 : (k + 1) * CHUNK * 4])
             return hb
 
-        def quantize_h(b, j0, width, hb):
-            cols = slice(j0, j0 + width)
-            nc.vector.quantize_mx(out=h_codes[b][:, cols].bitcast(FP8X4), scales=h_scales[b][:, cols], in_=hb[:])
+        def quantize_h(b, j0, width, hb, after=None):
+            codes, scales = quantize(hb[:], width, f"h{b}_{j0}", after)
+            for c0 in range(0, width, CHUNK):
+                h_q[b, j0 + c0] = (codes[:, c0:], scales[:, c0:])
 
         first = matched(0, 0, HALF)
-        w2_q.append(quantize(w2_bf[1][:], HALF, "w2q1"))
-        quantize_h(0, 0, HALF, first)
+        w2_q.append(quantize(w2_bf[1][:], HALF, "w2q1", "slot_site03"))
         site_product(0, 4, 2)
         site_product(1, 4, 2)
         cast_w3(0)
         cast_w3(1)
         second = matched(1, 0, HALF)
+        quantize_h(0, 0, HALF, first, "slot_site10")
         w3_q = [quantize(w3_bf[b][:], N, f"w3q{b}") for b in range(2)]
         site_product(0, 6, 2)
         site_product(1, 6, 2)
@@ -254,7 +255,7 @@ def tile_list_guide_cleavage_scores_kernel(
             (1, S - CHUNK, CHUNK),
         ):
             hb = matched(b, j0, width)
-            quantize_h(*waiting)
+            quantize_h(*waiting, f"slot_site{b}{j0 // CHUNK}")
             if waiting[0] == 1:
                 score(*waiting[1:3])
             waiting = (b, j0, width, hb)

@@ -42,7 +42,8 @@ def tile_list_guide_cleavage_scores_kernel(
         rows_at = scale_at + T - LAP
         picked_at = rows_at + raw_bytes
         w2a_at = picked_at + S - LAP
-        table1_at = w2a_at + raw_bytes
+        w3b_at = w2a_at + raw_bytes
+        table1_at = w3b_at + raw_bytes - LAP
 
         def at(shape, dtype, name, offset):
             return placed.tile(shape, dtype, name=name, offset=offset, align_bytes=64)
@@ -112,12 +113,13 @@ def tile_list_guide_cleavage_scores_kernel(
         for a in range(2):
             picked[a, 1] = gather_words(table[a], list1, 1, at([P, HALF], U32, f"picked{a}1", w1_at + a * HALF * 4))
         w2_raw.append(load_w2(1, held([P, 4, HALF], F32, "w2_raw1", "slot_table0")))
-        w3_raw = [load_w3(0, at([P, 4, N], F32, "w3_raw0", table1_at + S))]
+        w3_raw = [load_w3(0, at([P, 4, N], F32, "w3_raw0", table1_at + LAP + S))]
+        w3_raw.append(load_w3(1, at([P, 4, N], F32, "w3_raw1", w3b_at)))
 
         w2_bf, w3_bf = {}, {}
 
         def cast_w2(b):
-            wb = held([P, HALF * 4], BF16, f"w2_bf{b}")
+            wb = held([P, HALF * 4], BF16, f"w2_bf{b}", f"slot_w2{b}")
             dst = wb[:].rearrange("p (t u i s) -> p t u i s", t=4, i=8, s=4)
             src = w2_raw[b][:].rearrange("p s (u t i) -> p t u i s", t=4, i=8)
             for t in range(4):
@@ -129,7 +131,10 @@ def tile_list_guide_cleavage_scores_kernel(
             dst = wb[:].rearrange("p (c n t) -> p c n t", c=4, t=4)
             src = w3_raw[b][:].rearrange("p t (c n) -> p c n t", c=4)
             for c in range(4):
-                nc.gpsimd.tensor_scalar(dst[:, c], src[:, c], 1.0, 0.0, MULT, ADD)
+                if b == 0:
+                    nc.gpsimd.tensor_scalar(dst[:, c], src[:, c], 1.0, 0.0, MULT, ADD)
+                else:
+                    nc.scalar.activation(dst[:, c], src[:, c], IDENT)
             w3_bf[b] = wb
 
         def quantize(values, width, name, tag=None):
@@ -165,15 +170,13 @@ def tile_list_guide_cleavage_scores_kernel(
         site_product(0, 0, 4)
         picked2 = held([P, S], U32, "picked2")
         nc.vector.tensor_copy(picked2[:], table2[:].bitcast(U32).indirect(list2[:]))
-        w3_raw.append(load_w3(1, at([P, 4, N], F32, "w3_raw1", rows_at)))
-        picked_scales2 = at([P, S], U8, "picked_scales2", table1_at)
+        picked_scales2 = at([P, S], U8, "picked_scales2", table1_at + LAP)
         nc.vector.tensor_copy(picked_scales2[:], scale_win2[:].bitcast(U8).indirect(list2[:]))
         bias_col = held([P, N // P], F32, "bias_col", "slot_scale2")
         with nc.allow_non_contiguous_dma(reason="bias onto partitions"):
             nc.sync.dma_start(bias_col[:], bias.rearrange("(c p) -> p c", p=P))
         w2_q = [quantize(w2_bf[0][:], HALF, "w2q0")]
-        cast_w2(1)
-        site_product(1, 0, 4)
+        site_product(0, 4, 4)
 
         def match(b, chunk, dst):
             j0 = chunk * CHUNK
@@ -224,8 +227,8 @@ def tile_list_guide_cleavage_scores_kernel(
                         nc.scalar.activation(res[:, k, :], bank[:, k, :], IDENT, bias=bias_col[:, c : c + 1])
                 nc.sync.dma_start(out_rows[:, c0 : c0 + per_bank, cols], res[:])
 
-        def matched(b, j0, width):
-            hb = held([P, width * 4], BF16, f"h_bf{b}_{j0}")
+        def matched(b, j0, width, tag=None):
+            hb = held([P, width * 4], BF16, f"h_bf{b}_{j0}", tag)
             for k in range(width // CHUNK):
                 match(b, j0 // CHUNK + k, hb[:, k * CHUNK * 4 : (k + 1) * CHUNK * 4])
             return hb
@@ -236,28 +239,23 @@ def tile_list_guide_cleavage_scores_kernel(
                 h_q[b, j0 + c0] = (codes[:, c0:], scales[:, c0:])
 
         first = matched(0, 0, HALF)
-        w2_q.append(quantize(w2_bf[1][:], HALF, "w2q1", "slot_site03"))
-        site_product(0, 4, 2)
-        site_product(1, 4, 2)
+        cast_w2(1)
+        site_product(1, 0, 4)
         cast_w3(0)
+        second = matched(0, HALF, PAIR)
+        quantize_h(0, 0, HALF, first, "slot_site04")
+        w2_q.append(quantize(w2_bf[1][:], HALF, "w2q1"))
+        third = matched(0, HALF + PAIR, PAIR, "slot_w21")
+        quantize_h(0, HALF, PAIR, second, "slot_site06")
         cast_w3(1)
-        second = matched(1, 0, HALF)
-        quantize_h(0, 0, HALF, first, "slot_site10")
-        w3_q = [quantize(w3_bf[b][:], N, f"w3q{b}") for b in range(2)]
-        site_product(0, 6, 2)
-        site_product(1, 6, 2)
-        waiting = (1, 0, HALF, second)
-        for b, j0, width in (
-            (0, HALF, PAIR),
-            (1, HALF, PAIR),
-            (0, HALF + PAIR, PAIR),
-            (1, HALF + PAIR, CHUNK),
-            (1, S - CHUNK, CHUNK),
-        ):
-            hb = matched(b, j0, width)
-            quantize_h(*waiting, f"slot_site{b}{j0 // CHUNK}")
-            if waiting[0] == 1:
-                score(*waiting[1:3])
-            waiting = (b, j0, width, hb)
-        quantize_h(*waiting)
-        score(*waiting[1:3])
+        site_product(1, 4, 4)
+        waiting = (0, PAIR, matched(1, 0, PAIR))
+        quantize_h(0, HALF + PAIR, PAIR, third, "slot_site10")
+        w3_q = [quantize(w3_bf[0][:], N, "w3q0", "slot_site11"), quantize(w3_bf[1][:], N, "w3q1", "slot_after")]
+        for j0, width in ((PAIR, PAIR), (HALF, PAIR), (HALF + PAIR, CHUNK), (S - CHUNK, CHUNK)):
+            hb = matched(1, j0, width)
+            quantize_h(1, *waiting, f"slot_site1{j0 // CHUNK}")
+            score(*waiting[:2])
+            waiting = (j0, width, hb)
+        quantize_h(1, *waiting)
+        score(*waiting[:2])

@@ -14,7 +14,6 @@ U8 = mybir.dt.uint8
 FP8X4 = mybir.dt.float8_e4m3fn_x4
 FP4X4 = mybir.dt.float4_e2m1fn_x4
 MULT = mybir.AluOpType.mult
-ADD = mybir.AluOpType.add
 IDENT = mybir.ActivationFunctionType.Identity
 
 P = 128
@@ -122,19 +121,21 @@ def tile_list_guide_cleavage_scores_kernel(
             wb = held([P, HALF * 4], BF16, f"w2_bf{b}", f"slot_w2{b}")
             dst = wb[:].rearrange("p (t u i s) -> p t u i s", t=4, i=8, s=4)
             src = w2_raw[b][:].rearrange("p s (u t i) -> p t u i s", t=4, i=8)
+            walk_dst = wb[:].rearrange("p (t u h i s) -> p t u h s i", t=4, h=2, i=4, s=4)
+            walk_src = w2_raw[b][:].rearrange("p s (u t h i) -> p t u h s i", t=4, h=2, i=4)
             for t in range(4):
-                nc.scalar.activation(dst[:, t], src[:, t], IDENT)
+                if (b, t) == (0, 0):
+                    nc.scalar.activation(dst[:, t], src[:, t], IDENT)
+                else:
+                    nc.scalar.copy(walk_dst[:, t], walk_src[:, t])
             w2_bf[b] = wb
 
         def cast_w3(b):
             wb = held([P, N * 4], BF16, f"w3_bf{b}")
-            dst = wb[:].rearrange("p (c n t) -> p c n t", c=4, t=4)
-            src = w3_raw[b][:].rearrange("p t (c n) -> p c n t", c=4)
-            for c in range(4):
-                if b == 0:
-                    nc.gpsimd.tensor_scalar(dst[:, c], src[:, c], 1.0, 0.0, MULT, ADD)
-                else:
-                    nc.scalar.activation(dst[:, c], src[:, c], IDENT)
+            dst = wb[:].rearrange("p (c g i t) -> p c g t i", c=2, i=4, t=4)
+            src = w3_raw[b][:].rearrange("p t (c g i) -> p c g t i", c=2, i=4)
+            for c in range(2):
+                nc.scalar.copy(dst[:, c], src[:, c])
             w3_bf[b] = wb
 
         def quantize(values, width, name, tag=None):

@@ -19,8 +19,10 @@ IDENT = mybir.ActivationFunctionType.Identity
 P = 128
 HALF = 512
 CHUNK = 128
-PAIR = 256
+PAIR = 2 * CHUNK
 LAP = 64
+SUM_BANKS = 5
+WINDOW_BANKS = 3
 
 
 def tile_list_guide_cleavage_scores_kernel(
@@ -35,14 +37,16 @@ def tile_list_guide_cleavage_scores_kernel(
         def held(shape, dtype, name, tag=None):
             return keep.tile(shape, dtype, name=name, tag=tag or name, align_bytes=64)
 
-        raw_bytes = 4 * HALF * 4
+        big_bytes = 4 * HALF * 4
         w1_at = 0
-        scale_at = w1_at + 2 * H * 2 + LAP
+        w2b_at = w1_at + 2 * H * 2 - LAP
+        picked0_at = w2b_at + big_bytes
+        scale_at = picked0_at + S * 4 - LAP
         rows_at = scale_at + T - LAP
-        picked_at = rows_at + raw_bytes
+        picked_at = rows_at + big_bytes
         w2a_at = picked_at + S - LAP
-        w3b_at = w2a_at + raw_bytes
-        table1_at = w3b_at + raw_bytes - LAP
+        w3b_at = w2a_at + big_bytes
+        table1_at = w3b_at + big_bytes - LAP
 
         def at(shape, dtype, name, offset):
             return placed.tile(shape, dtype, name=name, offset=offset, align_bytes=64)
@@ -52,9 +56,9 @@ def tile_list_guide_cleavage_scores_kernel(
             return raw
 
         def load_w3(b, raw):
-            rows = w3[b * HALF : (b + 1) * HALF, :].rearrange("(u t i) n -> t u i n", t=4, i=8)
+            by_t = w3[b * HALF : (b + 1) * HALF, :].rearrange("(u t i) n -> t u i n", t=4, i=8)
             for t in range(4):
-                nc.sync.dma_start(raw[:, t, :], rows[t])
+                nc.sync.dma_start(raw[:, t, :], by_t[t])
             return raw
 
         def load_table(words, tile):
@@ -75,68 +79,71 @@ def tile_list_guide_cleavage_scores_kernel(
         nc.sync.dma_start(list2[:], offs2)
         nc.scalar.dma_start(scale_win[::4].bitcast(I32), tab_scales.rearrange("a q t -> q a t").bitcast(I32))
         nc.sync.dma_start(w1s_raw[::4], w1_scales.rearrange("a q n -> q a n").bitcast(I32))
-        table = [load_table(tab_words[0], held([P, T], I32, "table0", "slot_table0"))]
+        table = [load_table(tab_words[0], held([P, T], I32, "table0"))]
         table.append(load_table(tab_words[1], at([P, T], I32, "table1", table1_at)))
         w1_raw = at([P, 2, H // 2], I32, "w1_raw", w1_at)
         nc.sync.dma_start(w1_raw[:], w1_words.rearrange("a p n -> p a n").bitcast(I32))
         for e in range(4):
             nc.gpsimd.dma_start(scale_win2[4 + e :: 32], tab2_scales[0, e::4, :].bitcast(I32))
 
-        rows = at([P, (S + H) // 4], I32, "rows", rows_at)
+        scale_rows = at([P, (S + H) // 4], I32, "scale_rows", rows_at)
         picked_scales = at([P, S], U8, "picked_scales", picked_at)
         nc.vector.tensor_copy(picked_scales[:], scale_win[:].indirect(list1[:]))
         nc.vector.tensor_copy(
-            rows[:, S // 4 :].rearrange("p (b t u i) -> p b t u i", b=2, t=4, i=2),
+            scale_rows[:, S // 4 :].rearrange("p (b t u i) -> p b t u i", b=2, t=4, i=2),
             w1s_raw[:].rearrange("p (b u t i) -> p b t u i", b=2, t=4, i=2),
         )
-        nc.vector.tensor_copy(rows[:, : S // 4], picked_scales[:].bitcast(I32))
+        nc.vector.tensor_copy(scale_rows[:, : S // 4], picked_scales[:].bitcast(I32))
         for d in range(4):
-            nc.sync.dma_start(planes[32 * d : 32 * d + 4], rows[32 * d : 32 * d + 32 : 4])
+            nc.sync.dma_start(planes[32 * d : 32 * d + 4], scale_rows[32 * d : 32 * d + 32 : 4])
 
         w2_raw = [load_w2(0, at([P, 4, HALF], F32, "w2_raw0", w2a_at))]
         table2 = load_table(tab2_words[0], at([P, T], I32, "table2", rows_at))
 
-        def gather_words(window, lst, half, picked):
+        def gather_half(window, half, picked_half):
             cols = slice(half * HALF // 16, (half + 1) * HALF // 16)
-            nc.vector.tensor_copy(picked[:], window[:].bitcast(U32).indirect(lst[:, cols]))
-            return picked
+            nc.vector.tensor_copy(picked_half[:], window[:].bitcast(U32).indirect(list1[:, cols]))
+            return picked_half
 
-        picked = {(0, 0): gather_words(table[0], list1, 0, at([P, HALF], U32, "picked00", scale_at - LAP))}
-        picked[1, 0] = gather_words(table[1], list1, 0, held([P, HALF], U32, "picked10"))
+        picked0 = at([P, S], U32, "picked0", picked0_at)
+        nc.vector.tensor_copy(picked0[:], table[0][:].bitcast(U32).indirect(list1[:]))
+        picked = {(0, 0): picked0[:, :HALF], (0, 1): picked0[:, HALF:]}
+        picked[1, 0] = gather_half(table[1], 0, held([P, HALF], U32, "picked10"))
 
         w1_ord = held([P, 2 * H // 2], I32, "w1_ord")
         nc.vector.tensor_copy(
             w1_ord[:].rearrange("p (g t u i) -> p g t u i", g=4, t=4, i=4),
             w1_raw[:].rearrange("p a (b u t i) -> p (a b) t u i", b=2, t=4, i=4),
         )
-        for a in range(2):
-            picked[a, 1] = gather_words(table[a], list1, 1, at([P, HALF], U32, f"picked{a}1", w1_at + a * HALF * 4))
-        w2_raw.append(load_w2(1, held([P, 4, HALF], F32, "w2_raw1", "slot_table0")))
+        w2_raw.append(load_w2(1, at([P, 4, HALF], F32, "w2_raw1", w2b_at)))
+        picked[1, 1] = gather_half(table[1], 1, at([P, HALF], U32, "picked11", w1_at))
         w3_raw = [load_w3(0, at([P, 4, N], F32, "w3_raw0", table1_at + LAP + S))]
         w3_raw.append(load_w3(1, at([P, 4, N], F32, "w3_raw1", w3b_at)))
 
         w2_bf, w3_bf = {}, {}
 
-        def cast_w2(b):
-            wb = held([P, HALF * 4], BF16, f"w2_bf{b}", f"slot_w2{b}")
-            dst = wb[:].rearrange("p (t u i s) -> p t u i s", t=4, i=8, s=4)
-            src = w2_raw[b][:].rearrange("p s (u t i) -> p t u i s", t=4, i=8)
-            walk_dst = wb[:].rearrange("p (t u h i s) -> p t u h s i", t=4, h=2, i=4, s=4)
-            walk_src = w2_raw[b][:].rearrange("p s (u t h i) -> p t u h s i", t=4, h=2, i=4)
+        def round_w2(b):
+            rounded = held([P, HALF * 4], BF16, f"w2_bf{b}", f"slot_w2{b}")
+            dst = rounded[:].rearrange("p (t u h i s) -> p t u h s i", t=4, h=2, i=4, s=4)
+            src = w2_raw[b][:].rearrange("p s (u t h i) -> p t u h s i", t=4, h=2, i=4)
             for t in range(4):
                 if (b, t) == (0, 0):
-                    nc.scalar.activation(dst[:, t], src[:, t], IDENT)
+                    nc.scalar.activation(
+                        rounded[:].rearrange("p (t u i s) -> p t u i s", t=4, i=8, s=4)[:, t],
+                        w2_raw[b][:].rearrange("p s (u t i) -> p t u i s", t=4, i=8)[:, t],
+                        IDENT,
+                    )
                 else:
-                    nc.scalar.copy(walk_dst[:, t], walk_src[:, t])
-            w2_bf[b] = wb
+                    nc.scalar.copy(dst[:, t], src[:, t])
+            w2_bf[b] = rounded
 
-        def cast_w3(b):
-            wb = held([P, N * 4], BF16, f"w3_bf{b}")
-            dst = wb[:].rearrange("p (c g i t) -> p c g t i", c=2, i=4, t=4)
+        def round_w3(b):
+            rounded = held([P, N * 4], BF16, f"w3_bf{b}")
+            dst = rounded[:].rearrange("p (c g i t) -> p c g t i", c=2, i=4, t=4)
             src = w3_raw[b][:].rearrange("p t (c g i) -> p c g t i", c=2, i=4)
             for c in range(2):
                 nc.scalar.copy(dst[:, c], src[:, c])
-            w3_bf[b] = wb
+            w3_bf[b] = rounded
 
         def quantize(values, width, name, tag=None):
             codes = held([P, width], U32, name + "_codes", tag)
@@ -146,29 +153,33 @@ def tile_list_guide_cleavage_scores_kernel(
 
         site = {}
 
-        def site_product(b, first, count):
-            for chunk in range(first, first + count):
+        def site_slot(b, chunk):
+            return f"slot_site{b}{chunk}"
+
+        def site_sums(b, half):
+            for chunk in range(half * HALF // CHUNK, (half + 1) * HALF // CHUNK):
                 j0 = chunk * CHUNK
-                half, c0 = divmod(j0, HALF)
-                bank = psum.tile([P, 4, CHUNK], F32, name="site_bank", tag="site_bank", bufs=5)
+                c0 = j0 % HALF
+                bank = psum.tile([P, 4, CHUNK], F32, name="site_bank", tag="sum_bank", bufs=SUM_BANKS)
                 for a in range(2):
                     for t in range(4):
-                        col = (2 * a + b) * HALF + t * P
+                        col = b * HALF + t * P
+                        word = a * H + col
                         nc.tensor.matmul_mx(
                             out=bank[:, t, :],
-                            lhsT=w1_ord[:].bitcast(U8)[:, 2 * col : 2 * (col + P)].bitcast(FP4X4),
-                            lhsT_scale=planes[:, a, :].bitcast(U8)[:, S + b * HALF + t * P : S + b * HALF + (t + 1) * P],
+                            lhsT=w1_ord[:].bitcast(U8)[:, 2 * word : 2 * (word + P)].bitcast(FP4X4),
+                            lhsT_scale=planes[:, a, :].bitcast(U8)[:, S + col : S + col + P],
                             rhs=picked[a, half][:, c0 : c0 + CHUNK].bitcast(FP8X4),
                             rhs_scale=planes[:, a, :].bitcast(U8)[:, j0 : j0 + CHUNK],
                             start=(a == 0 and t == 0),
                             stop=(a == 1 and t == 3),
                         )
-                sb = held([P, CHUNK, 4], F32, f"site{b}{chunk}", f"slot_site{b}{chunk}")
-                nc.scalar.activation(sb[:], bank[:].rearrange("p t j -> p j t"), IDENT)
-                site[b, chunk] = sb
+                sums = held([P, CHUNK, 4], F32, f"site{b}{chunk}", site_slot(b, chunk))
+                nc.scalar.activation(sums[:], bank[:].rearrange("p t j -> p j t"), IDENT)
+                site[b, chunk] = sums
 
-        cast_w2(0)
-        site_product(0, 0, 4)
+        round_w2(0)
+        site_sums(0, 0)
         picked2 = held([P, S], U32, "picked2")
         nc.vector.tensor_copy(picked2[:], table2[:].bitcast(U32).indirect(list2[:]))
         picked_scales2 = at([P, S], U8, "picked_scales2", table1_at + LAP)
@@ -177,11 +188,11 @@ def tile_list_guide_cleavage_scores_kernel(
         with nc.allow_non_contiguous_dma(reason="bias onto partitions"):
             nc.sync.dma_start(bias_col[:], bias.rearrange("(c p) -> p c", p=P))
         w2_q = [quantize(w2_bf[0][:], HALF, "w2q0")]
-        site_product(0, 4, 4)
+        site_sums(0, 1)
 
         def match(b, chunk, dst):
             j0 = chunk * CHUNK
-            bank = psum.tile([P, 4, CHUNK], F32, name="window_bank", tag="window_bank", bufs=3)
+            bank = psum.tile([P, 4, CHUNK], F32, name="window_bank", tag="window_bank", bufs=WINDOW_BANKS)
             for t in range(4):
                 nc.tensor.matmul_mx(
                     out=bank[:, t, :],
@@ -203,13 +214,11 @@ def tile_list_guide_cleavage_scores_kernel(
         out_rows = out.rearrange("(c p) j -> p c j", p=P)
 
         def score(j0, width):
-            cols = slice(j0, j0 + width)
-            per_bank = min(2, HALF // width)
-            for c0 in range(0, N // P, per_bank):
-                res = held([P, per_bank, width], F32, f"res{j0}_{c0}")
-                bank = psum.tile([P, per_bank, width], F32, name="score_bank", tag="site_bank", bufs=5)
+            for c0 in range(0, N // P, 2):
+                res = held([P, 2, width], F32, f"res{j0}_{c0}")
+                bank = psum.tile([P, 2, width], F32, name="score_bank", tag="sum_bank", bufs=SUM_BANKS)
                 for b in range(2):
-                    for k in range(per_bank):
+                    for k in range(2):
                         c = c0 + k
                         nc.tensor.matmul_mx(
                             out=bank[:, k, :],
@@ -218,45 +227,46 @@ def tile_list_guide_cleavage_scores_kernel(
                             rhs=h_q[b, j0][0][:, :width].bitcast(FP8X4),
                             rhs_scale=h_q[b, j0][1][:, :width],
                             start=(b == 0 and k == 0),
-                            stop=(b == 1 and k == per_bank - 1),
+                            stop=(b == 1 and k == 1),
                         )
-                for k in range(per_bank):
+                for k in range(2):
                     c = c0 + k
                     if width == CHUNK and c0:
                         nc.vector.tensor_scalar_add(res[:, k, :], bank[:, k, :], bias_col[:, c : c + 1])
                     else:
                         nc.scalar.activation(res[:, k, :], bank[:, k, :], IDENT, bias=bias_col[:, c : c + 1])
-                nc.sync.dma_start(out_rows[:, c0 : c0 + per_bank, cols], res[:])
+                nc.sync.dma_start(out_rows[:, c0 : c0 + 2, j0 : j0 + width], res[:])
 
         def matched(b, j0, width, tag=None):
-            hb = held([P, width * 4], BF16, f"h_bf{b}_{j0}", tag)
+            h_bf = held([P, width * 4], BF16, f"h_bf{b}_{j0}", tag)
             for k in range(width // CHUNK):
-                match(b, j0 // CHUNK + k, hb[:, k * CHUNK * 4 : (k + 1) * CHUNK * 4])
-            return hb
+                match(b, j0 // CHUNK + k, h_bf[:, k * CHUNK * 4 : (k + 1) * CHUNK * 4])
+            return h_bf
 
-        def quantize_h(b, j0, width, hb, after=None):
-            codes, scales = quantize(hb[:], width, f"h{b}_{j0}", after)
+        def quantize_h(b, j0, width, h_bf, tag=None):
+            codes, scales = quantize(h_bf[:], width, f"h{b}_{j0}", tag)
             for c0 in range(0, width, CHUNK):
                 h_q[b, j0 + c0] = (codes[:, c0:], scales[:, c0:])
 
         first = matched(0, 0, HALF)
-        cast_w2(1)
-        site_product(1, 0, 4)
-        cast_w3(0)
+        round_w2(1)
+        site_sums(1, 0)
+        round_w3(0)
         second = matched(0, HALF, PAIR)
-        quantize_h(0, 0, HALF, first, "slot_site04")
+        quantize_h(0, 0, HALF, first, site_slot(0, HALF // CHUNK))
         w2_q.append(quantize(w2_bf[1][:], HALF, "w2q1"))
         third = matched(0, HALF + PAIR, PAIR, "slot_w21")
-        quantize_h(0, HALF, PAIR, second, "slot_site06")
-        cast_w3(1)
-        site_product(1, 4, 4)
+        quantize_h(0, HALF, PAIR, second, site_slot(0, (HALF + PAIR) // CHUNK))
+        round_w3(1)
+        site_sums(1, 1)
+
         waiting = (0, PAIR, matched(1, 0, PAIR))
-        quantize_h(0, HALF + PAIR, PAIR, third, "slot_site10")
-        w3_q = [quantize(w3_bf[0][:], N, "w3q0", "slot_site11"), quantize(w3_bf[1][:], N, "w3q1", "slot_after")]
+        quantize_h(0, HALF + PAIR, PAIR, third, site_slot(1, 0))
+        w3_q = [quantize(w3_bf[0][:], N, "w3q0", site_slot(1, 1)), quantize(w3_bf[1][:], N, "w3q1")]
         for j0, width in ((PAIR, PAIR), (HALF, PAIR), (HALF + PAIR, CHUNK), (S - CHUNK, CHUNK)):
-            hb = matched(1, j0, width)
-            quantize_h(1, *waiting, f"slot_site1{j0 // CHUNK}")
+            h_bf = matched(1, j0, width)
+            quantize_h(1, *waiting, site_slot(1, j0 // CHUNK))
             score(*waiting[:2])
-            waiting = (j0, width, hb)
+            waiting = (j0, width, h_bf)
         quantize_h(1, *waiting)
         score(*waiting[:2])

@@ -21,8 +21,8 @@ HALF = 512
 CHUNK = 128
 PAIR = 2 * CHUNK
 LAP = 64
-SUM_BANKS = 5
-WINDOW_BANKS = 3
+BANKS = 8
+BANK_BYTES = 2048
 
 
 def tile_list_guide_cleavage_scores_kernel(
@@ -38,18 +38,23 @@ def tile_list_guide_cleavage_scores_kernel(
             return keep.tile(shape, dtype, name=name, tag=tag or name, align_bytes=64)
 
         big_bytes = 4 * HALF * 4
-        w1_at = 0
-        w2b_at = w1_at + 2 * H * 2 - LAP
-        picked0_at = w2b_at + big_bytes
-        scale_at = picked0_at + S * 4 - LAP
-        rows_at = scale_at + T - LAP
-        picked_at = rows_at + big_bytes
-        w2a_at = picked_at + S - LAP
+        rows_at = big_bytes - LAP
+        scale_at = rows_at - T + LAP
+        w2b_at = 0
+        picked_at = rows_at + T
+        table2_at = picked_at + S - LAP
+        w2a_at = table2_at + big_bytes
         w3b_at = w2a_at + big_bytes
         table1_at = w3b_at + big_bytes - LAP
 
         def at(shape, dtype, name, offset):
             return placed.tile(shape, dtype, name=name, offset=offset, align_bytes=64)
+
+        taken = []
+
+        def next_bank(shape, name):
+            taken.append(name)
+            return psum.tile(shape, F32, name=name, offset=(len(taken) - 1) % BANKS * BANK_BYTES)
 
         def load_w2(b, raw):
             nc.sync.dma_start(raw[:], w2.rearrange("(p s) n -> p s n", s=4)[:, :, b * HALF : (b + 1) * HALF])
@@ -68,23 +73,31 @@ def tile_list_guide_cleavage_scores_kernel(
         list1 = keep.tile([P, S // 16], U16, name="list1")
         list2 = keep.tile([P, S // 16], U16, name="list2")
         scale_win = at([P, T], U8, "scale_win", scale_at)
-        w1s_raw = held([P, H // 4], I32, "w1s_raw")
+        w1s_raw = held([P, H // 4], I32, "w1s_raw", "slot_w1s")
         scale_win2 = held([P, T // 4], I32, "scale_win2", "slot_scale2")
         planes = held([P, 2, (S + H) // 4], I32, "planes")
-        nc.gpsimd.memset(scale_win[:].bitcast(I32), 0)
+        nc.vector.memset(scale_win[:, : T // 2].bitcast(I32), 0)
+        nc.gpsimd.memset(scale_win[:, T // 2 :].bitcast(I32), 0)
         nc.vector.memset(w1s_raw[:], 0)
         nc.vector.memset(scale_win2[:], 0)
         nc.vector.memset(planes[:], 0)
         nc.sync.dma_start(list1[:], offs)
         nc.sync.dma_start(list2[:], offs2)
-        nc.scalar.dma_start(scale_win[::4].bitcast(I32), tab_scales.rearrange("a q t -> q a t").bitcast(I32))
+        w1_raw = held([P, 2, H // 2], I32, "w1_raw")
+        nc.sync.dma_start(w1_raw[:], w1_words.rearrange("a p n -> p a n").bitcast(I32))
+        nc.sync.dma_start(scale_win[::4].bitcast(I32), tab_scales.rearrange("a q t -> q a t").bitcast(I32))
         nc.sync.dma_start(w1s_raw[::4], w1_scales.rearrange("a q n -> q a n").bitcast(I32))
         table = [load_table(tab_words[0], held([P, T], I32, "table0"))]
         table.append(load_table(tab_words[1], at([P, T], I32, "table1", table1_at)))
-        w1_raw = at([P, 2, H // 2], I32, "w1_raw", w1_at)
-        nc.sync.dma_start(w1_raw[:], w1_words.rearrange("a p n -> p a n").bitcast(I32))
+        w2_raw = [load_w2(0, at([P, 4, HALF], F32, "w2_raw0", w2a_at))]
         for e in range(4):
             nc.gpsimd.dma_start(scale_win2[4 + e :: 32], tab2_scales[0, e::4, :].bitcast(I32))
+
+        w1_ord = held([P, 2 * H // 2], I32, "w1_ord")
+        nc.vector.tensor_copy(
+            w1_ord[:].rearrange("p (g t u i) -> p g t u i", g=4, t=4, i=4),
+            w1_raw[:].rearrange("p a (b u t i) -> p (a b) t u i", b=2, t=4, i=4),
+        )
 
         scale_rows = at([P, (S + H) // 4], I32, "scale_rows", rows_at)
         picked_scales = at([P, S], U8, "picked_scales", picked_at)
@@ -97,33 +110,26 @@ def tile_list_guide_cleavage_scores_kernel(
         for d in range(4):
             nc.sync.dma_start(planes[32 * d : 32 * d + 4], scale_rows[32 * d : 32 * d + 32 : 4])
 
-        w2_raw = [load_w2(0, at([P, 4, HALF], F32, "w2_raw0", w2a_at))]
-        table2 = load_table(tab2_words[0], at([P, T], I32, "table2", rows_at))
+        table2 = load_table(tab2_words[0], at([P, T], I32, "table2", table2_at))
+        w2_raw.append(load_w2(1, at([P, 4, HALF], F32, "w2_raw1", w2b_at)))
 
-        def gather_half(window, half, picked_half):
+        def gather_half(window, offsets, half, picked_half):
             cols = slice(half * HALF // 16, (half + 1) * HALF // 16)
-            nc.vector.tensor_copy(picked_half[:], window[:].bitcast(U32).indirect(list1[:, cols]))
+            nc.vector.tensor_copy(picked_half[:], window[:].bitcast(U32).indirect(offsets[:, cols]))
             return picked_half
 
-        picked0 = at([P, S], U32, "picked0", picked0_at)
+        picked0 = held([P, S], U32, "picked0", "slot_w1s")
         nc.vector.tensor_copy(picked0[:], table[0][:].bitcast(U32).indirect(list1[:]))
         picked = {(0, 0): picked0[:, :HALF], (0, 1): picked0[:, HALF:]}
-        picked[1, 0] = gather_half(table[1], 0, held([P, HALF], U32, "picked10"))
+        picked[1, 0] = gather_half(table[1], list1, 0, held([P, HALF], U32, "picked10"))
 
-        w1_ord = held([P, 2 * H // 2], I32, "w1_ord")
-        nc.vector.tensor_copy(
-            w1_ord[:].rearrange("p (g t u i) -> p g t u i", g=4, t=4, i=4),
-            w1_raw[:].rearrange("p a (b u t i) -> p (a b) t u i", b=2, t=4, i=4),
-        )
-        w2_raw.append(load_w2(1, at([P, 4, HALF], F32, "w2_raw1", w2b_at)))
-        picked[1, 1] = gather_half(table[1], 1, at([P, HALF], U32, "picked11", w1_at))
+        picked[1, 1] = gather_half(table[1], list1, 1, held([P, HALF], U32, "picked11"))
         w3_raw = [load_w3(0, at([P, 4, N], F32, "w3_raw0", table1_at + LAP + S))]
         w3_raw.append(load_w3(1, at([P, 4, N], F32, "w3_raw1", w3b_at)))
 
         w2_bf, w3_bf = {}, {}
 
-        def round_w2(b):
-            rounded = held([P, HALF * 4], BF16, f"w2_bf{b}", f"slot_w2{b}")
+        def round_w2(b, rounded):
             dst = rounded[:].rearrange("p (t u h i s) -> p t u h s i", t=4, h=2, i=4, s=4)
             src = w2_raw[b][:].rearrange("p s (u t h i) -> p t u h s i", t=4, h=2, i=4)
             for t in range(4):
@@ -137,30 +143,34 @@ def tile_list_guide_cleavage_scores_kernel(
                     nc.scalar.copy(dst[:, t], src[:, t])
             w2_bf[b] = rounded
 
-        def round_w3(b):
-            rounded = held([P, N * 4], BF16, f"w3_bf{b}")
-            dst = rounded[:].rearrange("p (c g i t) -> p c g t i", c=2, i=4, t=4)
-            src = w3_raw[b][:].rearrange("p t (c g i) -> p c g t i", c=2, i=4)
-            for c in range(2):
-                nc.scalar.copy(dst[:, c], src[:, c])
+        def round_w3(b, copy, pieces, tag=None):
+            rounded = held([P, N * 4], BF16, f"w3_bf{b}", tag)
+            dst = rounded[:].rearrange("p (c g i t) -> p c g t i", c=pieces, i=4, t=4)
+            src = w3_raw[b][:].rearrange("p t (c g i) -> p c g t i", c=pieces, i=4)
+            for c in range(pieces):
+                copy(dst[:, c], src[:, c])
             w3_bf[b] = rounded
 
-        def quantize(values, width, name, tag=None):
-            codes = held([P, width], U32, name + "_codes", tag)
+        def quantize(values, width, name, tag=None, offset=None):
+            if offset is None:
+                codes = held([P, width], U32, name + "_codes", tag)
+            else:
+                codes = at([P, width], U32, name + "_codes", offset)
             scales = held([P, width], U8, name + "_scales")
             nc.vector.quantize_mx(out=codes[:].bitcast(FP8X4), scales=scales[:], in_=values)
             return codes, scales
 
         site = {}
+        after_rounding = {(0, 0): w2a_at, (0, 4): w2b_at, (0, 6): w3b_at}
 
         def site_slot(b, chunk):
             return f"slot_site{b}{chunk}"
 
-        def site_sums(b, half):
-            for chunk in range(half * HALF // CHUNK, (half + 1) * HALF // CHUNK):
+        def site_sums(b, chunks):
+            for chunk in chunks:
                 j0 = chunk * CHUNK
-                c0 = j0 % HALF
-                bank = psum.tile([P, 4, CHUNK], F32, name="site_bank", tag="sum_bank", bufs=SUM_BANKS)
+                half, c0 = divmod(j0, HALF)
+                bank = next_bank([P, 4, CHUNK], f"site_bank{b}{chunk}")
                 for a in range(2):
                     for t in range(4):
                         col = b * HALF + t * P
@@ -174,38 +184,48 @@ def tile_list_guide_cleavage_scores_kernel(
                             start=(a == 0 and t == 0),
                             stop=(a == 1 and t == 3),
                         )
-                sums = held([P, CHUNK, 4], F32, f"site{b}{chunk}", site_slot(b, chunk))
+                if (b, chunk) in after_rounding:
+                    sums = at([P, CHUNK, 4], F32, f"site{b}{chunk}", after_rounding[b, chunk])
+                else:
+                    sums = held([P, CHUNK, 4], F32, f"site{b}{chunk}", site_slot(b, chunk))
                 nc.scalar.activation(sums[:], bank[:].rearrange("p t j -> p j t"), IDENT)
                 site[b, chunk] = sums
 
-        round_w2(0)
-        site_sums(0, 0)
-        picked2 = held([P, S], U32, "picked2")
-        nc.vector.tensor_copy(picked2[:], table2[:].bitcast(U32).indirect(list2[:]))
+        round_w2(0, held([P, HALF * 4], BF16, "w2_bf0", "slot_w20"))
+        site_sums(0, range(4))
+        site_sums(1, range(4))
         picked_scales2 = at([P, S], U8, "picked_scales2", table1_at + LAP)
         nc.vector.tensor_copy(picked_scales2[:], scale_win2[:].bitcast(U8).indirect(list2[:]))
+        picked2 = [gather_half(table2, list2, 0, held([P, HALF], U32, "picked20"))]
+        w2_q = [quantize(w2_bf[0][:], HALF, "w2q0")]
+        picked2.append(gather_half(table2, list2, 1, held([P, HALF], U32, "picked21", "slot_w20")))
         bias_col = held([P, N // P], F32, "bias_col", "slot_scale2")
         with nc.allow_non_contiguous_dma(reason="bias onto partitions"):
             nc.sync.dma_start(bias_col[:], bias.rearrange("(c p) -> p c", p=P))
-        w2_q = [quantize(w2_bf[0][:], HALF, "w2q0")]
-        site_sums(0, 1)
+
+        window = {}
+
+        def window_sums(pieces):
+            for b, chunk in pieces:
+                j0 = chunk * CHUNK
+                half, c0 = divmod(j0, HALF)
+                bank = next_bank([P, 4, CHUNK], f"window_bank{b}{chunk}")
+                for t in range(4):
+                    nc.tensor.matmul_mx(
+                        out=bank[:, t, :],
+                        lhsT=w2_q[b][0][:, t * P : (t + 1) * P].bitcast(FP8X4),
+                        lhsT_scale=w2_q[b][1][:, t * P : (t + 1) * P],
+                        rhs=picked2[half][:, c0 : c0 + CHUNK].bitcast(FP8X4),
+                        rhs_scale=picked_scales2[4:, j0 : j0 + CHUNK],
+                        start=True,
+                        stop=True,
+                    )
+                window[b, chunk] = bank
 
         def match(b, chunk, dst):
-            j0 = chunk * CHUNK
-            bank = psum.tile([P, 4, CHUNK], F32, name="window_bank", tag="window_bank", bufs=WINDOW_BANKS)
-            for t in range(4):
-                nc.tensor.matmul_mx(
-                    out=bank[:, t, :],
-                    lhsT=w2_q[b][0][:, t * P : (t + 1) * P].bitcast(FP8X4),
-                    lhsT_scale=w2_q[b][1][:, t * P : (t + 1) * P],
-                    rhs=picked2[:, j0 : j0 + CHUNK].bitcast(FP8X4),
-                    rhs_scale=picked_scales2[4:, j0 : j0 + CHUNK],
-                    start=True,
-                    stop=True,
-                )
             nc.vector.tensor_tensor(
                 dst.rearrange("p (j t) -> p j t", t=4),
-                bank[:].rearrange("p t j -> p j t"),
+                window[b, chunk][:].rearrange("p t j -> p j t"),
                 site[b, chunk][:],
                 MULT,
             )
@@ -214,11 +234,12 @@ def tile_list_guide_cleavage_scores_kernel(
         out_rows = out.rearrange("(c p) j -> p c j", p=P)
 
         def score(j0, width):
-            for c0 in range(0, N // P, 2):
-                res = held([P, 2, width], F32, f"res{j0}_{c0}")
-                bank = psum.tile([P, 2, width], F32, name="score_bank", tag="sum_bank", bufs=SUM_BANKS)
+            blocks = 1 if width == HALF else 2
+            for c0 in range(0, N // P, blocks):
+                res = held([P, blocks, width], F32, f"res{j0}_{c0}")
+                bank = next_bank([P, blocks, width], f"score_bank{j0}_{c0}")
                 for b in range(2):
-                    for k in range(2):
+                    for k in range(blocks):
                         c = c0 + k
                         nc.tensor.matmul_mx(
                             out=bank[:, k, :],
@@ -227,46 +248,68 @@ def tile_list_guide_cleavage_scores_kernel(
                             rhs=h_q[b, j0][0][:, :width].bitcast(FP8X4),
                             rhs_scale=h_q[b, j0][1][:, :width],
                             start=(b == 0 and k == 0),
-                            stop=(b == 1 and k == 1),
+                            stop=(b == 1 and k == blocks - 1),
                         )
-                for k in range(2):
+                for k in range(blocks):
                     c = c0 + k
-                    if width == CHUNK and c0:
+                    if j0 == S - CHUNK and c0:
                         nc.vector.tensor_scalar_add(res[:, k, :], bank[:, k, :], bias_col[:, c : c + 1])
                     else:
                         nc.scalar.activation(res[:, k, :], bank[:, k, :], IDENT, bias=bias_col[:, c : c + 1])
-                nc.sync.dma_start(out_rows[:, c0 : c0 + 2, j0 : j0 + width], res[:])
+                nc.sync.dma_start(out_rows[:, c0 : c0 + blocks, j0 : j0 + width], res[:])
 
-        def matched(b, j0, width, tag=None):
-            h_bf = held([P, width * 4], BF16, f"h_bf{b}_{j0}", tag)
-            for k in range(width // CHUNK):
-                match(b, j0 // CHUNK + k, h_bf[:, k * CHUNK * 4 : (k + 1) * CHUNK * 4])
-            return h_bf
+        def h_tile(name, entries, tag=None):
+            return held([P, entries * 4], BF16, name, tag)
 
-        def quantize_h(b, j0, width, h_bf, tag=None):
-            codes, scales = quantize(h_bf[:], width, f"h{b}_{j0}", tag)
-            for c0 in range(0, width, CHUNK):
-                h_q[b, j0 + c0] = (codes[:, c0:], scales[:, c0:])
+        def part(h_bf, k):
+            return h_bf[:, k * CHUNK * 4 : (k + 1) * CHUNK * 4]
 
-        first = matched(0, 0, HALF)
-        round_w2(1)
-        site_sums(1, 0)
-        round_w3(0)
-        second = matched(0, HALF, PAIR)
-        quantize_h(0, 0, HALF, first, site_slot(0, HALF // CHUNK))
-        w2_q.append(quantize(w2_bf[1][:], HALF, "w2q1"))
-        third = matched(0, HALF + PAIR, PAIR, "slot_w21")
-        quantize_h(0, HALF, PAIR, second, site_slot(0, (HALF + PAIR) // CHUNK))
-        round_w3(1)
-        site_sums(1, 1)
+        def quantize_h(h_bf, pieces, tag=None, offset=None):
+            width = h_bf.shape[1] // 4
+            codes, scales = quantize(h_bf[:], width, "h%d_%d" % pieces[0], tag, offset)
+            for k, key in enumerate(pieces):
+                c0 = k * width // len(pieces)
+                h_q[key] = (codes[:, c0:], scales[:, c0:])
 
-        waiting = (0, PAIR, matched(1, 0, PAIR))
-        quantize_h(0, HALF + PAIR, PAIR, third, site_slot(1, 0))
-        w3_q = [quantize(w3_bf[0][:], N, "w3q0", site_slot(1, 1)), quantize(w3_bf[1][:], N, "w3q1")]
-        for j0, width in ((PAIR, PAIR), (HALF, PAIR), (HALF + PAIR, CHUNK), (S - CHUNK, CHUNK)):
-            h_bf = matched(1, j0, width)
-            quantize_h(1, *waiting, site_slot(1, j0 // CHUNK))
-            score(*waiting[:2])
-            waiting = (j0, width, h_bf)
-        quantize_h(1, *waiting)
-        score(*waiting[:2])
+        third_pieces = [(0, 4), (0, 5), (1, 4), (1, 5)]
+        last_pieces = [(0, 6), (1, 6), (0, 7), (1, 7)]
+
+        first = [h_tile(f"h_first{b}", HALF) for b in range(2)]
+        window_sums([(0, k) for k in range(4)])
+        for k in range(4):
+            match(0, k, part(first[0], k))
+        round_w2(1, at([P, HALF * 4], BF16, "w2_bf1", after_rounding[0, 0]))
+        for b, chunk in third_pieces:
+            site_sums(b, [chunk])
+        round_w3(0, nc.vector.tensor_copy, 1, site_slot(0, 2))
+        w2_q.append(quantize(w2_bf[1][:], HALF, "w2q1", site_slot(0, 3)))
+        quantize_h(first[0], [(0, 0)])
+        window_sums([(1, k) for k in range(4)])
+        round_w3(1, nc.scalar.copy, 4, "slot_w31")
+        for b, chunk in last_pieces:
+            site_sums(b, [chunk])
+        for k in range(4):
+            match(1, k, part(first[1], k))
+        w3_q = [quantize(w3_bf[0][:], N, "w3q0", site_slot(1, 2))]
+        quantize_h(first[1], [(1, 0)])
+        w3_q.append(quantize(w3_bf[1][:], N, "w3q1", site_slot(1, 3)))
+        window_sums(third_pieces)
+        score(0, HALF)
+
+        third = h_tile("h_third", 2 * PAIR, "slot_w31")
+        for k, (b, chunk) in enumerate(third_pieces):
+            match(b, chunk, part(third, k))
+        window_sums(last_pieces)
+        sixth = h_tile("h_sixth", 2 * CHUNK)
+        match(0, 6, part(sixth, 0))
+        quantize_h(third, [(0, HALF), (1, HALF)], None, after_rounding[0, 6])
+        score(HALF, PAIR)
+        match(1, 6, part(sixth, 1))
+        last = [h_tile(f"h_last{b}", CHUNK) for b in range(2)]
+        match(0, 7, part(last[0], 0))
+        quantize_h(sixth, [(0, 6 * CHUNK), (1, 6 * CHUNK)], site_slot(0, 7))
+        score(6 * CHUNK, CHUNK)
+        quantize_h(last[0], [(0, 7 * CHUNK)])
+        match(1, 7, part(last[1], 0))
+        quantize_h(last[1], [(1, 7 * CHUNK)])
+        score(7 * CHUNK, CHUNK)

@@ -143,8 +143,7 @@ def tile_list_guide_cleavage_scores_kernel(
                     nc.scalar.copy(dst[:, t], src[:, t])
             w2_bf[b] = rounded
 
-        def round_w3(b, copy, pieces, tag=None):
-            rounded = held([P, N * 4], BF16, f"w3_bf{b}", tag)
+        def round_w3(b, copy, pieces, rounded):
             dst = rounded[:].rearrange("p (c g i t) -> p c g t i", c=pieces, i=4, t=4)
             src = w3_raw[b][:].rearrange("p t (c g i) -> p c g t i", c=pieces, i=4)
             for c in range(pieces):
@@ -161,42 +160,36 @@ def tile_list_guide_cleavage_scores_kernel(
             return codes, scales
 
         site = {}
-        after_rounding = {(0, 0): w2a_at, (0, 4): w2b_at, (0, 6): w3b_at}
+        site_at = {(0, 0): w2a_at, (1, 0): None, (0, 1): w2b_at, (1, 1): w3b_at}
 
-        def site_slot(b, chunk):
-            return f"slot_site{b}{chunk}"
-
-        def site_sums(b, chunks):
-            for chunk in chunks:
-                j0 = chunk * CHUNK
-                half, c0 = divmod(j0, HALF)
-                bank = next_bank([P, 4, CHUNK], f"site_bank{b}{chunk}")
+        def site_sums(b, half):
+            if site_at[b, half] is None:
+                sums = held([P, 4, HALF], F32, f"site{b}{half}")
+            else:
+                sums = at([P, 4, HALF], F32, f"site{b}{half}", site_at[b, half])
+            for t in range(4):
+                bank = next_bank([P, HALF], f"site_bank{b}{half}{t}")
+                col = b * HALF + t * P
                 for a in range(2):
-                    for t in range(4):
-                        col = b * HALF + t * P
-                        word = a * H + col
-                        nc.tensor.matmul_mx(
-                            out=bank[:, t, :],
-                            lhsT=w1_ord[:].bitcast(U8)[:, 2 * word : 2 * (word + P)].bitcast(FP4X4),
-                            lhsT_scale=planes[:, a, :].bitcast(U8)[:, S + col : S + col + P],
-                            rhs=picked[a, half][:, c0 : c0 + CHUNK].bitcast(FP8X4),
-                            rhs_scale=planes[:, a, :].bitcast(U8)[:, j0 : j0 + CHUNK],
-                            start=(a == 0 and t == 0),
-                            stop=(a == 1 and t == 3),
-                        )
-                if (b, chunk) in after_rounding:
-                    sums = at([P, CHUNK, 4], F32, f"site{b}{chunk}", after_rounding[b, chunk])
-                else:
-                    sums = held([P, CHUNK, 4], F32, f"site{b}{chunk}", site_slot(b, chunk))
-                nc.scalar.activation(sums[:], bank[:].rearrange("p t j -> p j t"), IDENT)
-                site[b, chunk] = sums
+                    word = a * H + col
+                    nc.tensor.matmul_mx(
+                        out=bank[:],
+                        lhsT=w1_ord[:].bitcast(U8)[:, 2 * word : 2 * (word + P)].bitcast(FP4X4),
+                        lhsT_scale=planes[:, a, :].bitcast(U8)[:, S + col : S + col + P],
+                        rhs=picked[a, half][:, :].bitcast(FP8X4),
+                        rhs_scale=planes[:, a, :].bitcast(U8)[:, half * HALF : (half + 1) * HALF],
+                        start=(a == 0),
+                        stop=(a == 1),
+                    )
+                nc.scalar.activation(sums[:, t, :], bank[:], IDENT)
+            site[b, half] = sums
 
         round_w2(0, held([P, HALF * 4], BF16, "w2_bf0", "slot_w20"))
-        site_sums(0, range(4))
-        site_sums(1, range(4))
+        site_sums(0, 0)
+        site_sums(1, 0)
         picked_scales2 = at([P, S], U8, "picked_scales2", table1_at + LAP)
         nc.vector.tensor_copy(picked_scales2[:], scale_win2[:].bitcast(U8).indirect(list2[:]))
-        picked2 = [gather_half(table2, list2, 0, held([P, HALF], U32, "picked20"))]
+        picked2 = [gather_half(table2, list2, 0, held([P, HALF], U32, "picked20", "slot_picked20"))]
         w2_q = [quantize(w2_bf[0][:], HALF, "w2q0")]
         picked2.append(gather_half(table2, list2, 1, held([P, HALF], U32, "picked21", "slot_w20")))
         bias_col = held([P, N // P], F32, "bias_col", "slot_scale2")
@@ -223,10 +216,11 @@ def tile_list_guide_cleavage_scores_kernel(
                 window[b, chunk] = bank
 
         def match(b, chunk, dst):
+            half, c0 = divmod(chunk * CHUNK, HALF)
             nc.vector.tensor_tensor(
-                dst.rearrange("p (j t) -> p j t", t=4),
-                window[b, chunk][:].rearrange("p t j -> p j t"),
-                site[b, chunk][:],
+                dst.rearrange("p (g i t) -> p g t i", i=2, t=4),
+                window[b, chunk][:].rearrange("p t (g i) -> p g t i", i=2),
+                site[b, half][:, :, c0 : c0 + CHUNK].rearrange("p t (g i) -> p g t i", i=2),
                 MULT,
             )
 
@@ -278,21 +272,19 @@ def tile_list_guide_cleavage_scores_kernel(
         window_sums([(0, k) for k in range(4)])
         for k in range(4):
             match(0, k, part(first[0], k))
-        round_w2(1, at([P, HALF * 4], BF16, "w2_bf1", after_rounding[0, 0]))
-        for b, chunk in third_pieces:
-            site_sums(b, [chunk])
-        round_w3(0, nc.vector.tensor_copy, 1, site_slot(0, 2))
-        w2_q.append(quantize(w2_bf[1][:], HALF, "w2q1", site_slot(0, 3)))
+        round_w2(1, held([P, HALF * 4], BF16, "w2_bf1"))
+        site_sums(0, 1)
+        round_w3(0, nc.vector.tensor_copy, 1, at([P, N * 4], BF16, "w3_bf0", w2a_at))
+        w2_q.append(quantize(w2_bf[1][:], HALF, "w2q1", None, w2a_at + N * 8))
         quantize_h(first[0], [(0, 0)])
         window_sums([(1, k) for k in range(4)])
-        round_w3(1, nc.scalar.copy, 4, "slot_w31")
-        for b, chunk in last_pieces:
-            site_sums(b, [chunk])
+        round_w3(1, nc.scalar.copy, 4, held([P, N * 4], BF16, "w3_bf1", "slot_w31"))
+        site_sums(1, 1)
         for k in range(4):
             match(1, k, part(first[1], k))
-        w3_q = [quantize(w3_bf[0][:], N, "w3q0", site_slot(1, 2))]
+        w3_q = [quantize(w3_bf[0][:], N, "w3q0", "slot_picked20")]
         quantize_h(first[1], [(1, 0)])
-        w3_q.append(quantize(w3_bf[1][:], N, "w3q1", site_slot(1, 3)))
+        w3_q.append(quantize(w3_bf[1][:], N, "w3q1"))
         window_sums(third_pieces)
         score(0, HALF)
 
@@ -302,12 +294,12 @@ def tile_list_guide_cleavage_scores_kernel(
         window_sums(last_pieces)
         sixth = h_tile("h_sixth", 2 * CHUNK)
         match(0, 6, part(sixth, 0))
-        quantize_h(third, [(0, HALF), (1, HALF)], None, after_rounding[0, 6])
+        quantize_h(third, [(0, HALF), (1, HALF)])
         score(HALF, PAIR)
         match(1, 6, part(sixth, 1))
         last = [h_tile(f"h_last{b}", CHUNK) for b in range(2)]
         match(0, 7, part(last[0], 0))
-        quantize_h(sixth, [(0, 6 * CHUNK), (1, 6 * CHUNK)], site_slot(0, 7))
+        quantize_h(sixth, [(0, 6 * CHUNK), (1, 6 * CHUNK)])
         score(6 * CHUNK, CHUNK)
         quantize_h(last[0], [(0, 7 * CHUNK)])
         match(1, 7, part(last[1], 0))

@@ -14,6 +14,7 @@ U8 = mybir.dt.uint8
 FP8X4 = mybir.dt.float8_e4m3fn_x4
 FP4X4 = mybir.dt.float4_e2m1fn_x4
 MULT = mybir.AluOpType.mult
+ADD = mybir.AluOpType.add
 IDENT = mybir.ActivationFunctionType.Identity
 
 P = 128
@@ -150,6 +151,13 @@ def tile_list_guide_cleavage_scores_kernel(
                 copy(dst[:, c], src[:, c])
             w3_bf[b] = rounded
 
+        def round_on_gpsimd(raw, rounded, pieces):
+            dst = rounded[:].rearrange("p (c n t) -> p c n t", c=pieces, t=4)
+            src = raw[:].rearrange("p t (c n) -> p c n t", c=pieces)
+            for c in range(pieces):
+                nc.gpsimd.tensor_scalar(dst[:, c], src[:, c], 1.0, 0.0, MULT, ADD)
+            return rounded
+
         def quantize(values, width, name, tag=None, offset=None):
             if offset is None:
                 codes = held([P, width], U32, name + "_codes", tag)
@@ -274,7 +282,7 @@ def tile_list_guide_cleavage_scores_kernel(
             match(0, k, part(first[0], k))
         round_w2(1, held([P, HALF * 4], BF16, "w2_bf1"))
         site_sums(0, 1)
-        round_w3(0, nc.vector.tensor_copy, 1, at([P, N * 4], BF16, "w3_bf0", w2a_at))
+        w3_bf[0] = round_on_gpsimd(w3_raw[0], held([P, N * 4], BF16, "w3_bf0"), 4)
         w2_q.append(quantize(w2_bf[1][:], HALF, "w2q1", None, w2a_at + N * 8))
         quantize_h(first[0], [(0, 0)])
         window_sums([(1, k) for k in range(4)])

@@ -22,7 +22,7 @@ HALF = 512
 CHUNK = 128
 PAIR = 2 * CHUNK
 LAP = 64
-BANKS = 8
+LOW, HIGH = 0, 4
 BANK_BYTES = 2048
 
 
@@ -39,10 +39,10 @@ def tile_list_guide_cleavage_scores_kernel(
             return keep.tile(shape, dtype, name=name, tag=tag or name, align_bytes=64)
 
         big_bytes = 4 * HALF * 4
-        rows_at = big_bytes - LAP
-        scale_at = rows_at - T + LAP
-        w2b_at = 0
-        picked_at = rows_at + T
+        scale_at = 0
+        rows_at = T - LAP
+        w2b_at = rows_at + T
+        picked_at = w2b_at + big_bytes
         table2_at = picked_at + S - LAP
         w2a_at = table2_at + big_bytes
         w3b_at = w2a_at + big_bytes
@@ -51,11 +51,8 @@ def tile_list_guide_cleavage_scores_kernel(
         def at(shape, dtype, name, offset):
             return placed.tile(shape, dtype, name=name, offset=offset, align_bytes=64)
 
-        taken = []
-
-        def next_bank(shape, name):
-            taken.append(name)
-            return psum.tile(shape, F32, name=name, offset=(len(taken) - 1) % BANKS * BANK_BYTES)
+        def bank_tile(shape, name, bank):
+            return psum.tile(shape, F32, name=name, offset=bank * BANK_BYTES)
 
         def load_w2(b, raw):
             nc.sync.dma_start(raw[:], w2.rearrange("(p s) n -> p s n", s=4)[:, :, b * HALF : (b + 1) * HALF])
@@ -76,19 +73,20 @@ def tile_list_guide_cleavage_scores_kernel(
         scale_win = at([P, T], U8, "scale_win", scale_at)
         w1s_raw = held([P, H // 4], I32, "w1s_raw", "slot_w1s")
         scale_win2 = held([P, T // 4], I32, "scale_win2", "slot_scale2")
-        planes = held([P, 2, (S + H) // 4], I32, "planes")
+        planes = [held([P, 2, 2 * HALF // 4], I32, f"planes{k}") for k in range(2)]
         nc.vector.memset(scale_win[:, : T // 2].bitcast(I32), 0)
         nc.gpsimd.memset(scale_win[:, T // 2 :].bitcast(I32), 0)
         nc.vector.memset(w1s_raw[:], 0)
         nc.vector.memset(scale_win2[:], 0)
-        nc.vector.memset(planes[:], 0)
+        for k in range(2):
+            nc.vector.memset(planes[k][:], 0)
         nc.sync.dma_start(list1[:], offs)
         nc.sync.dma_start(list2[:], offs2)
         w1_raw = held([P, 2, H // 2], I32, "w1_raw")
         nc.sync.dma_start(w1_raw[:], w1_words.rearrange("a p n -> p a n").bitcast(I32))
         nc.sync.dma_start(scale_win[::4].bitcast(I32), tab_scales.rearrange("a q t -> q a t").bitcast(I32))
         nc.sync.dma_start(w1s_raw[::4], w1_scales.rearrange("a q n -> q a n").bitcast(I32))
-        table = [load_table(tab_words[0], held([P, T], I32, "table0"))]
+        table = [load_table(tab_words[0], at([P, T], I32, "table0", w2b_at))]
         table.append(load_table(tab_words[1], at([P, T], I32, "table1", table1_at)))
         w2_raw = [load_w2(0, at([P, 4, HALF], F32, "w2_raw0", w2a_at))]
         for e in range(4):
@@ -100,18 +98,23 @@ def tile_list_guide_cleavage_scores_kernel(
             w1_raw[:].rearrange("p a (b u t i) -> p (a b) t u i", b=2, t=4, i=4),
         )
 
-        scale_rows = at([P, (S + H) // 4], I32, "scale_rows", rows_at)
+        scale_rows = at([P, 2, 2, HALF // 4], I32, "scale_rows", rows_at)
         picked_scales = at([P, S], U8, "picked_scales", picked_at)
         nc.vector.tensor_copy(picked_scales[:], scale_win[:].indirect(list1[:]))
         nc.vector.tensor_copy(
-            scale_rows[:, S // 4 :].rearrange("p (b t u i) -> p b t u i", b=2, t=4, i=2),
+            scale_rows[:, :, 1, :].rearrange("p b (t u i) -> p b t u i", t=4, i=2),
             w1s_raw[:].rearrange("p (b u t i) -> p b t u i", b=2, t=4, i=2),
         )
-        nc.vector.tensor_copy(scale_rows[:, : S // 4], picked_scales[:].bitcast(I32))
-        for d in range(4):
-            nc.sync.dma_start(planes[32 * d : 32 * d + 4], scale_rows[32 * d : 32 * d + 32 : 4])
+        nc.vector.tensor_copy(scale_rows[:, :, 0, :], picked_scales[:].bitcast(I32).rearrange("p (k n) -> p k n", k=2))
 
+        def move_planes(k):
+            for d in (0, 2, 1, 3):
+                rows = scale_rows[32 * d : 32 * d + 32 : 4, k].rearrange("p s n -> p (s n)")
+                nc.sync.dma_start(planes[k][32 * d : 32 * d + 4], rows)
+
+        move_planes(0)
         table2 = load_table(tab2_words[0], at([P, T], I32, "table2", table2_at))
+        move_planes(1)
         w2_raw.append(load_w2(1, at([P, 4, HALF], F32, "w2_raw1", w2b_at)))
 
         def gather_half(window, offsets, half, picked_half):
@@ -170,22 +173,22 @@ def tile_list_guide_cleavage_scores_kernel(
         site = {}
         site_at = {(0, 0): w2a_at, (1, 0): None, (0, 1): w2b_at, (1, 1): w3b_at}
 
-        def site_sums(b, half):
+        def site_sums(b, half, first_bank):
             if site_at[b, half] is None:
                 sums = held([P, 4, HALF], F32, f"site{b}{half}")
             else:
                 sums = at([P, 4, HALF], F32, f"site{b}{half}", site_at[b, half])
             for t in range(4):
-                bank = next_bank([P, HALF], f"site_bank{b}{half}{t}")
+                bank = bank_tile([P, HALF], f"site_bank{b}{half}{t}", first_bank + t)
                 col = b * HALF + t * P
                 for a in range(2):
                     word = a * H + col
                     nc.tensor.matmul_mx(
                         out=bank[:],
                         lhsT=w1_ord[:].bitcast(U8)[:, 2 * word : 2 * (word + P)].bitcast(FP4X4),
-                        lhsT_scale=planes[:, a, :].bitcast(U8)[:, S + col : S + col + P],
+                        lhsT_scale=planes[b][:, a, :].bitcast(U8)[:, HALF + t * P : HALF + (t + 1) * P],
                         rhs=picked[a, half][:, :].bitcast(FP8X4),
-                        rhs_scale=planes[:, a, :].bitcast(U8)[:, half * HALF : (half + 1) * HALF],
+                        rhs_scale=planes[half][:, a, :].bitcast(U8)[:, :HALF],
                         start=(a == 0),
                         stop=(a == 1),
                     )
@@ -193,8 +196,8 @@ def tile_list_guide_cleavage_scores_kernel(
             site[b, half] = sums
 
         round_w2(0, held([P, HALF * 4], BF16, "w2_bf0", "slot_w20"))
-        site_sums(0, 0)
-        site_sums(1, 0)
+        site_sums(0, 0, LOW)
+        site_sums(1, 0, HIGH)
         picked_scales2 = at([P, S], U8, "picked_scales2", table1_at + LAP)
         nc.vector.tensor_copy(picked_scales2[:], scale_win2[:].bitcast(U8).indirect(list2[:]))
         picked2 = [gather_half(table2, list2, 0, held([P, HALF], U32, "picked20", "slot_picked20"))]
@@ -206,11 +209,11 @@ def tile_list_guide_cleavage_scores_kernel(
 
         window = {}
 
-        def window_sums(pieces):
-            for b, chunk in pieces:
+        def window_sums(pieces, first_bank):
+            for k, (b, chunk) in enumerate(pieces):
                 j0 = chunk * CHUNK
                 half, c0 = divmod(j0, HALF)
-                bank = next_bank([P, 4, CHUNK], f"window_bank{b}{chunk}")
+                bank = bank_tile([P, 4, CHUNK], f"window_bank{b}{chunk}", first_bank + k)
                 for t in range(4):
                     nc.tensor.matmul_mx(
                         out=bank[:, t, :],
@@ -235,11 +238,11 @@ def tile_list_guide_cleavage_scores_kernel(
         h_q = {}
         out_rows = out.rearrange("(c p) j -> p c j", p=P)
 
-        def score(j0, width):
+        def score(j0, width, first_bank):
             blocks = 1 if width == HALF else 2
             for c0 in range(0, N // P, blocks):
                 res = held([P, blocks, width], F32, f"res{j0}_{c0}")
-                bank = next_bank([P, blocks, width], f"score_bank{j0}_{c0}")
+                bank = bank_tile([P, blocks, width], f"score_bank{j0}_{c0}", first_bank + c0 // blocks)
                 for b in range(2):
                     for k in range(blocks):
                         c = c0 + k
@@ -277,39 +280,39 @@ def tile_list_guide_cleavage_scores_kernel(
         last_pieces = [(0, 6), (1, 6), (0, 7), (1, 7)]
 
         first = [h_tile(f"h_first{b}", HALF) for b in range(2)]
-        window_sums([(0, k) for k in range(4)])
+        window_sums([(0, k) for k in range(4)], HIGH)
         for k in range(4):
             match(0, k, part(first[0], k))
         round_w2(1, held([P, HALF * 4], BF16, "w2_bf1"))
-        site_sums(0, 1)
+        site_sums(0, 1, HIGH)
         w3_bf[0] = round_on_gpsimd(w3_raw[0], held([P, N * 4], BF16, "w3_bf0"), 4)
         w2_q.append(quantize(w2_bf[1][:], HALF, "w2q1", None, w2a_at + N * 8))
         quantize_h(first[0], [(0, 0)])
-        window_sums([(1, k) for k in range(4)])
+        window_sums([(1, k) for k in range(4)], LOW)
         round_w3(1, nc.scalar.copy, 4, held([P, N * 4], BF16, "w3_bf1", "slot_w31"))
-        site_sums(1, 1)
+        site_sums(1, 1, LOW)
         for k in range(4):
             match(1, k, part(first[1], k))
         w3_q = [quantize(w3_bf[0][:], N, "w3q0", "slot_picked20")]
         quantize_h(first[1], [(1, 0)])
         w3_q.append(quantize(w3_bf[1][:], N, "w3q1"))
-        window_sums(third_pieces)
-        score(0, HALF)
+        window_sums(third_pieces, HIGH)
+        score(0, HALF, LOW)
 
         third = h_tile("h_third", 2 * PAIR, "slot_w31")
         for k, (b, chunk) in enumerate(third_pieces):
             match(b, chunk, part(third, k))
-        window_sums(last_pieces)
+        window_sums(last_pieces, HIGH)
         sixth = h_tile("h_sixth", 2 * CHUNK)
         match(0, 6, part(sixth, 0))
         quantize_h(third, [(0, HALF), (1, HALF)])
-        score(HALF, PAIR)
+        score(HALF, PAIR, LOW)
         match(1, 6, part(sixth, 1))
         last = [h_tile(f"h_last{b}", CHUNK) for b in range(2)]
         match(0, 7, part(last[0], 0))
         quantize_h(sixth, [(0, 6 * CHUNK), (1, 6 * CHUNK)])
-        score(6 * CHUNK, CHUNK)
+        score(6 * CHUNK, CHUNK, LOW + 2)
         quantize_h(last[0], [(0, 7 * CHUNK)])
         match(1, 7, part(last[1], 0))
         quantize_h(last[1], [(1, 7 * CHUNK)])
-        score(7 * CHUNK, CHUNK)
+        score(7 * CHUNK, CHUNK, HIGH)

@@ -21,9 +21,8 @@ P = 128
 HALF = 512
 CHUNK = 128
 PAIR = 2 * CHUNK
-LAP = 64
-LOW, HIGH = 0, 4
 BANK_BYTES = 2048
+QUADRANTS = (0, 2, 1, 3)
 
 
 def tile_list_guide_cleavage_scores_kernel(
@@ -35,18 +34,8 @@ def tile_list_guide_cleavage_scores_kernel(
         placed = ctx.enter_context(tc.tile_pool(name="placed", bufs=1))
         psum = ctx.enter_context(tc.psum_pool(name="psum", bufs=1))
 
-        def held(shape, dtype, name, tag=None):
-            return keep.tile(shape, dtype, name=name, tag=tag or name, align_bytes=64)
-
-        big_bytes = 4 * HALF * 4
-        scale_at = 0
-        rows_at = T - LAP
-        w2b_at = rows_at + T
-        picked_at = w2b_at + big_bytes
-        table2_at = picked_at + S - LAP
-        w2a_at = table2_at + big_bytes
-        w3b_at = w2a_at + big_bytes
-        table1_at = w3b_at + big_bytes - LAP
+        def held(shape, dtype, name):
+            return keep.tile(shape, dtype, name=name, align_bytes=64)
 
         def at(shape, dtype, name, offset):
             return placed.tile(shape, dtype, name=name, offset=offset, align_bytes=64)
@@ -54,195 +43,246 @@ def tile_list_guide_cleavage_scores_kernel(
         def bank_tile(shape, name, bank):
             return psum.tile(shape, F32, name=name, offset=bank * BANK_BYTES)
 
-        def load_w2(b, raw):
-            nc.sync.dma_start(raw[:], w2.rearrange("(p s) n -> p s n", s=4)[:, :, b * HALF : (b + 1) * HALF])
-            return raw
-
-        def load_w3(b, raw):
-            by_t = w3[b * HALF : (b + 1) * HALF, :].rearrange("(u t i) n -> t u i n", t=4, i=8)
-            for t in range(4):
-                nc.sync.dma_start(raw[:, t, :], by_t[t])
-            return raw
+        big_bytes = 4 * T
+        table1_at = 0
+        w2b_at = table1_at + big_bytes
+        w3_bf_at = [w2b_at + big_bytes + b * big_bytes // 2 for b in range(2)]
+        site00_at = w3_bf_at[1] + big_bytes // 2
+        w1a_at = site00_at + big_bytes // 2
+        site_at = {(0, 0): site00_at, (1, 0): w2b_at, (1, 1): w2b_at + big_bytes // 2}
+        h_at = {(1, 2): w3_bf_at[1] - big_bytes // 8}
 
         def load_table(words, tile):
             nc.sync.dma_start(tile[:], words.rearrange("p t i -> p (t i)").bitcast(I32))
             return tile
 
+        def load_w1(b, raw):
+            nc.sync.dma_start(raw[:], w1_words.rearrange("a p n -> p a n")[:, :, b * H : (b + 1) * H].bitcast(I32))
+            return raw
+
+        def load_w2(b, raw):
+            nc.sync.dma_start(raw[:], w2.rearrange("(p s) n -> p s n", s=4)[:, :, b * HALF : (b + 1) * HALF])
+            return raw
+
+        def load_w3(b):
+            raw = held([P, 4, N], F32, f"w3_raw{b}")
+            by_t = w3[b * HALF : (b + 1) * HALF, :].rearrange("(u t i) n -> t u i n", t=4, i=8)
+            for t in range(4):
+                nc.sync.dma_start(raw[:, t, :], by_t[t])
+            return raw
+
         list1 = keep.tile([P, S // 16], U16, name="list1")
         list2 = keep.tile([P, S // 16], U16, name="list2")
-        scale_win = at([P, T], U8, "scale_win", scale_at)
-        w1s_raw = held([P, H // 4], I32, "w1s_raw", "slot_w1s")
-        scale_win2 = held([P, T // 4], I32, "scale_win2", "slot_scale2")
-        planes = [held([P, 2, 2 * HALF // 4], I32, f"planes{k}") for k in range(2)]
-        nc.vector.memset(scale_win[:, : T // 2].bitcast(I32), 0)
-        nc.gpsimd.memset(scale_win[:, T // 2 :].bitcast(I32), 0)
-        nc.vector.memset(w1s_raw[:], 0)
-        nc.vector.memset(scale_win2[:], 0)
-        for k in range(2):
-            nc.vector.memset(planes[k][:], 0)
+        scale_win = held([P, T // 4], I32, "scale_win")
+        scale_win2 = held([P, T // 4], I32, "scale_win2")
+        w1s_raw = held([P, 2, H // 4], I32, "w1s_raw")
+        planes = held([P, 2, S // 4], I32, "planes")
+        plane2 = held([P, S // 4], I32, "plane2")
+        nc.gpsimd.memset(scale_win[:], 0)
+        w1_planes = held([P, 2 * H // 4], I32, "w1_planes")
+        for tile in (scale_win2, w1_planes, planes, plane2):
+            nc.vector.memset(tile[:], 0)
         nc.sync.dma_start(list1[:], offs)
         nc.sync.dma_start(list2[:], offs2)
-        w1_raw = held([P, 2, H // 2], I32, "w1_raw")
-        nc.sync.dma_start(w1_raw[:], w1_words.rearrange("a p n -> p a n").bitcast(I32))
-        nc.sync.dma_start(scale_win[::4].bitcast(I32), tab_scales.rearrange("a q t -> q a t").bitcast(I32))
-        nc.sync.dma_start(w1s_raw[::4], w1_scales.rearrange("a q n -> q a n").bitcast(I32))
-        table = [load_table(tab_words[0], at([P, T], I32, "table0", w2b_at))]
-        table.append(load_table(tab_words[1], at([P, T], I32, "table1", table1_at)))
-        w2_raw = [load_w2(0, at([P, 4, HALF], F32, "w2_raw0", w2a_at))]
-        for e in range(4):
-            nc.gpsimd.dma_start(scale_win2[4 + e :: 32], tab2_scales[0, e::4, :].bitcast(I32))
+        for d in QUADRANTS:
+            rows = w1_scales[:, 4 * d : 4 * d + 4, :].rearrange("a e n -> e a n")
+            nc.scalar.dma_start(w1s_raw[32 * d : 32 * d + 4], rows.bitcast(I32))
+        nc.sync.dma_start(scale_win[::4], tab_scales.rearrange("a q t -> q a t").bitcast(I32))
+        table0 = load_table(tab_words[0], held([P, T], I32, "table0"))
+        nc.sync.dma_start(scale_win2[::8], tab2_scales[0].bitcast(I32))
+        w2_raw = [load_w2(0, held([P, 4, HALF], F32, "w2_raw0"))]
+        w1_raw = [load_w1(0, at([P, 2, HALF // 2], I32, "w1_raw0", w1a_at))]
 
-        w1_ord = held([P, 2 * H // 2], I32, "w1_ord")
-        nc.vector.tensor_copy(
-            w1_ord[:].rearrange("p (g t u i) -> p g t u i", g=4, t=4, i=4),
-            w1_raw[:].rearrange("p a (b u t i) -> p (a b) t u i", b=2, t=4, i=4),
-        )
+        picked_scales = held([P, S], U8, "picked_scales")
+        nc.vector.tensor_copy(picked_scales[:], scale_win[:].bitcast(U8).indirect(list1[:]))
+        for d in QUADRANTS:
+            nc.sync.dma_start(planes[32 * d : 32 * d + 4], picked_scales[32 * d : 32 * d + 32 : 4].bitcast(I32))
+        table1 = load_table(tab_words[1], at([P, T], I32, "table1", table1_at))
+        w1_raw.append(load_w1(1, at([P, 2, HALF // 2], I32, "w1_raw1", site00_at)))
+        table2 = load_table(tab2_words[0], held([P, T], I32, "table2"))
 
-        scale_rows = at([P, 2, 2, HALF // 4], I32, "scale_rows", rows_at)
-        picked_scales = at([P, S], U8, "picked_scales", picked_at)
-        nc.vector.tensor_copy(picked_scales[:], scale_win[:].indirect(list1[:]))
-        nc.vector.tensor_copy(
-            scale_rows[:, :, 1, :].rearrange("p b (t u i) -> p b t u i", t=4, i=2),
-            w1s_raw[:].rearrange("p (b u t i) -> p b t u i", b=2, t=4, i=2),
-        )
-        nc.vector.tensor_copy(scale_rows[:, :, 0, :], picked_scales[:].bitcast(I32).rearrange("p (k n) -> p k n", k=2))
-
-        def move_planes(k):
-            for d in (0, 2, 1, 3):
-                rows = scale_rows[32 * d : 32 * d + 32 : 4, k].rearrange("p s n -> p (s n)")
-                nc.sync.dma_start(planes[k][32 * d : 32 * d + 4], rows)
-
-        move_planes(0)
-        table2 = load_table(tab2_words[0], at([P, T], I32, "table2", table2_at))
-        move_planes(1)
+        picked0 = held([P, S], U32, "picked0")
+        nc.vector.tensor_copy(picked0[:], table0[:].bitcast(U32).indirect(list1[:]))
+        picked_scales2 = held([P, S], U8, "picked_scales2")
+        nc.vector.tensor_copy(picked_scales2[:], scale_win2[:].bitcast(U8).indirect(list2[:]))
+        for d in QUADRANTS:
+            nc.sync.dma_start(plane2[32 * d + 4 : 32 * d + 8], picked_scales2[32 * d : 32 * d + 32 : 8].bitcast(I32))
         w2_raw.append(load_w2(1, at([P, 4, HALF], F32, "w2_raw1", w2b_at)))
+        w3_raw = [load_w3(b) for b in range(2)]
+        bias_col = held([P, N // P], F32, "bias_col")
+        with nc.allow_non_contiguous_dma(reason="bias onto partitions"):
+            nc.sync.dma_start(bias_col[:], bias.rearrange("(c p) -> p c", p=P))
 
-        def gather_half(window, offsets, half, picked_half):
-            cols = slice(half * HALF // 16, (half + 1) * HALF // 16)
-            nc.vector.tensor_copy(picked_half[:], window[:].bitcast(U32).indirect(offsets[:, cols]))
-            return picked_half
+        def gather_pieces(window, offsets, widths, name):
+            picked = held([P, S], U32, name)
+            j0 = 0
+            for width in widths:
+                cols = slice(j0 // 16, (j0 + width) // 16)
+                nc.vector.tensor_copy(picked[:, j0 : j0 + width], window[:].bitcast(U32).indirect(offsets[:, cols]))
+                j0 = j0 + width
+            return picked
 
-        picked0 = held([P, S], U32, "picked0", "slot_w1s")
-        nc.vector.tensor_copy(picked0[:], table[0][:].bitcast(U32).indirect(list1[:]))
-        picked = {(0, 0): picked0[:, :HALF], (0, 1): picked0[:, HALF:]}
-        picked[1, 0] = gather_half(table[1], list1, 0, held([P, HALF], U32, "picked10"))
+        for d in QUADRANTS:
+            rows = slice(32 * d, 32 * d + 4)
+            nc.scalar.copy(
+                w1_planes[rows].bitcast(U32).rearrange("p (g t u i) -> p g t u i", g=4, t=4, i=2),
+                w1s_raw[rows].bitcast(U32).rearrange("p a (b u t i) -> p (a b) t u i", b=2, t=4, i=2),
+            )
 
-        picked[1, 1] = gather_half(table[1], list1, 1, held([P, HALF], U32, "picked11"))
-        w3_raw = [load_w3(0, at([P, 4, N], F32, "w3_raw0", table1_at + LAP + S))]
-        w3_raw.append(load_w3(1, at([P, 4, N], F32, "w3_raw1", w3b_at)))
+        def order_w1(b, copy, ordered):
+            copy(
+                ordered[:].rearrange("p (a t u i) -> p a t u i", a=2, t=4, i=4),
+                w1_raw[b][:].bitcast(U32).rearrange("p a (u t i) -> p a t u i", t=4, i=4),
+            )
+            return ordered
 
-        w2_bf, w3_bf = {}, {}
-
-        def round_w2(b, rounded):
-            dst = rounded[:].rearrange("p (t u h i s) -> p t u h s i", t=4, h=2, i=4, s=4)
+        def round_w2(b, first, count, rounded):
+            dst = rounded[:].rearrange("p (t u h i s) -> p t u h s i", t=count, h=2, i=4, s=4)
             src = w2_raw[b][:].rearrange("p s (u t h i) -> p t u h s i", t=4, h=2, i=4)
-            for t in range(4):
+            for k in range(count):
+                t = first + k
                 if (b, t) == (0, 0):
                     nc.scalar.activation(
-                        rounded[:].rearrange("p (t u i s) -> p t u i s", t=4, i=8, s=4)[:, t],
+                        rounded[:].rearrange("p (t u i s) -> p t u i s", t=count, i=8, s=4)[:, k],
                         w2_raw[b][:].rearrange("p s (u t i) -> p t u i s", t=4, i=8)[:, t],
                         IDENT,
                     )
                 else:
-                    nc.scalar.copy(dst[:, t], src[:, t])
-            w2_bf[b] = rounded
-
-        def round_w3(b, copy, pieces, rounded):
-            dst = rounded[:].rearrange("p (c g i t) -> p c g t i", c=pieces, i=4, t=4)
-            src = w3_raw[b][:].rearrange("p t (c g i) -> p c g t i", c=pieces, i=4)
-            for c in range(pieces):
-                copy(dst[:, c], src[:, c])
-            w3_bf[b] = rounded
-
-        def round_on_gpsimd(raw, rounded, pieces):
-            dst = rounded[:].rearrange("p (c n t) -> p c n t", c=pieces, t=4)
-            src = raw[:].rearrange("p t (c n) -> p c n t", c=pieces)
-            for c in range(pieces):
-                nc.gpsimd.tensor_scalar(dst[:, c], src[:, c], 1.0, 0.0, MULT, ADD)
+                    nc.scalar.copy(dst[:, k], src[:, t])
             return rounded
 
-        def quantize(values, width, name, tag=None, offset=None):
-            if offset is None:
-                codes = held([P, width], U32, name + "_codes", tag)
-            else:
-                codes = at([P, width], U32, name + "_codes", offset)
-            scales = held([P, width], U8, name + "_scales")
-            nc.vector.quantize_mx(out=codes[:].bitcast(FP8X4), scales=scales[:], in_=values)
+        def round_w3(raw, rounded, on_gpsimd):
+            for c in range(4):
+                if c < on_gpsimd:
+                    dst = rounded[:].rearrange("p (c n t) -> p c n t", c=4, t=4)[:, c]
+                    src = raw[:].rearrange("p t (c n) -> p c n t", c=4)[:, c]
+                    nc.gpsimd.tensor_scalar(dst, src, 1.0, 0.0, MULT, ADD)
+                else:
+                    dst = rounded[:].rearrange("p (c g i t) -> p c g t i", c=4, i=4, t=4)[:, c]
+                    src = raw[:].rearrange("p t (c g i) -> p c g t i", c=4, i=4)[:, c]
+                    nc.scalar.copy(dst, src)
+            return rounded
+
+        def quantize(values, codes, scales):
+            nc.vector.quantize_mx(out=codes.bitcast(FP8X4), scales=scales, in_=values)
+
+        def quantize_weight(rounded, codes, name):
+            scales = held([P, HALF], U8, name + "_scales")
+            quantize(rounded[:], codes[:], scales[:])
             return codes, scales
 
-        site = {}
-        site_at = {(0, 0): w2a_at, (1, 0): None, (0, 1): w2b_at, (1, 1): w3b_at}
+        w1_ord = [order_w1(0, nc.scalar.copy, held([P, HALF], U32, "w1_ord0"))]
+        w2_bf = {(0, 0): round_w2(0, 0, 2, held([P, 2 * HALF], BF16, "w2_bf00"))}
+        w2_bf[0, 2] = round_w2(0, 2, 2, at([P, 2 * HALF], BF16, "w2_bf02", w1a_at))
+        picked = [picked0, gather_pieces(table1, list1, (PAIR, PAIR, HALF), "picked1")]
+        w1_ord.append(order_w1(1, nc.scalar.copy, held([P, HALF], U32, "w1_ord1")))
 
-        def site_sums(b, half, first_bank):
-            if site_at[b, half] is None:
-                sums = held([P, 4, HALF], F32, f"site{b}{half}")
-            else:
-                sums = at([P, 4, HALF], F32, f"site{b}{half}", site_at[b, half])
+        def site_passes(banks, a, b, pair, opens):
             for t in range(4):
-                bank = bank_tile([P, HALF], f"site_bank{b}{half}{t}", first_bank + t)
-                col = b * HALF + t * P
-                for a in range(2):
-                    word = a * H + col
-                    nc.tensor.matmul_mx(
-                        out=bank[:],
-                        lhsT=w1_ord[:].bitcast(U8)[:, 2 * word : 2 * (word + P)].bitcast(FP4X4),
-                        lhsT_scale=planes[b][:, a, :].bitcast(U8)[:, HALF + t * P : HALF + (t + 1) * P],
-                        rhs=picked[a, half][:, :].bitcast(FP8X4),
-                        rhs_scale=planes[half][:, a, :].bitcast(U8)[:, :HALF],
-                        start=(a == 0),
-                        stop=(a == 1),
-                    )
-                nc.scalar.activation(sums[:, t, :], bank[:], IDENT)
-            site[b, half] = sums
+                word = a * HALF + t * P
+                col = a * H + b * HALF + t * P
+                nc.tensor.matmul_mx(
+                    out=banks[t // 2][:, t % 2, :],
+                    lhsT=w1_ord[b][:].bitcast(U8)[:, 2 * word : 2 * (word + P)].bitcast(FP4X4),
+                    lhsT_scale=w1_planes[:].bitcast(U8)[:, col : col + P],
+                    rhs=picked[a][:, pair * PAIR : (pair + 1) * PAIR].bitcast(FP8X4),
+                    rhs_scale=planes[:, a, :].bitcast(U8)[:, pair * PAIR : (pair + 1) * PAIR],
+                    start=(opens and t % 2 == 0),
+                    stop=(not opens and t % 2 == 1),
+                )
 
-        round_w2(0, held([P, HALF * 4], BF16, "w2_bf0", "slot_w20"))
-        site_sums(0, 0, LOW)
-        site_sums(1, 0, HIGH)
-        picked_scales2 = at([P, S], U8, "picked_scales2", table1_at + LAP)
-        nc.vector.tensor_copy(picked_scales2[:], scale_win2[:].bitcast(U8).indirect(list2[:]))
-        picked2 = [gather_half(table2, list2, 0, held([P, HALF], U32, "picked20", "slot_picked20"))]
-        w2_q = [quantize(w2_bf[0][:], HALF, "w2q0")]
-        picked2.append(gather_half(table2, list2, 1, held([P, HALF], U32, "picked21", "slot_w20")))
-        bias_col = held([P, N // P], F32, "bias_col", "slot_scale2")
-        with nc.allow_non_contiguous_dma(reason="bias onto partitions"):
-            nc.sync.dma_start(bias_col[:], bias.rearrange("(c p) -> p c", p=P))
+        def site_banks(b, pair, first_bank):
+            return [bank_tile([P, 2, PAIR], f"site_bank{b}{pair}{k}", first_bank + k) for k in range(2)]
+
+        site = {}
+
+        def copy_site(banks, b, pair):
+            if (b, pair) in site_at:
+                sums = at([P, 4, PAIR], F32, f"site{b}{pair}", site_at[b, pair])
+            else:
+                sums = held([P, 4, PAIR], F32, f"site{b}{pair}")
+            for k in range(2):
+                nc.scalar.activation(sums[:, 2 * k : 2 * k + 2, :], banks[k][:], IDENT)
+            site[b, pair] = sums
+
+        first_banks = [site_banks(0, pair, 2 * pair) for pair in range(2)]
+        for pair in range(2):
+            site_passes(first_banks[pair], 0, 0, pair, True)
+        for pair in range(2):
+            site_passes(first_banks[pair], 1, 0, pair, False)
+            copy_site(first_banks[pair], 0, pair)
+
+        def site_sums(b, pair, first_bank):
+            banks = site_banks(b, pair, first_bank)
+            for a in (1, 0):
+                site_passes(banks, a, b, pair, a == 1)
+            copy_site(banks, b, pair)
+
+        site_sums(0, 2, 4)
+        site_sums(0, 3, 6)
+
+        w2_q = {}
+
+        def quantize_w2(b, first, count, codes):
+            scales = held([P, count * P], U8, f"w2q{b}{first}_scales")
+            quantize(w2_bf[b, first][:], codes[:], scales[:])
+            for k in range(count):
+                w2_q[b, first + k] = (codes[:, k * P : (k + 1) * P], scales[:, k * P : (k + 1) * P])
+
+        quantize_w2(0, 0, 2, held([P, 2 * P], U32, "w2q00_codes"))
+        quantize_w2(0, 2, 2, at([P, 2 * P], U32, "w2q02_codes", table1_at))
+        picked2 = gather_pieces(table2, list2, (HALF, HALF), "picked2")
 
         window = {}
 
-        def window_sums(pieces, first_bank):
-            for k, (b, chunk) in enumerate(pieces):
+        def window_sums(b, chunks, first_bank):
+            for k, chunk in enumerate(chunks):
                 j0 = chunk * CHUNK
-                half, c0 = divmod(j0, HALF)
                 bank = bank_tile([P, 4, CHUNK], f"window_bank{b}{chunk}", first_bank + k)
                 for t in range(4):
                     nc.tensor.matmul_mx(
                         out=bank[:, t, :],
-                        lhsT=w2_q[b][0][:, t * P : (t + 1) * P].bitcast(FP8X4),
-                        lhsT_scale=w2_q[b][1][:, t * P : (t + 1) * P],
-                        rhs=picked2[half][:, c0 : c0 + CHUNK].bitcast(FP8X4),
-                        rhs_scale=picked_scales2[4:, j0 : j0 + CHUNK],
+                        lhsT=w2_q[b, t][0].bitcast(FP8X4),
+                        lhsT_scale=w2_q[b, t][1],
+                        rhs=picked2[:, j0 : j0 + CHUNK].bitcast(FP8X4),
+                        rhs_scale=plane2[:].bitcast(U8)[4:, j0 : j0 + CHUNK],
                         start=True,
                         stop=True,
                     )
                 window[b, chunk] = bank
 
-        def match(b, chunk, dst):
-            half, c0 = divmod(chunk * CHUNK, HALF)
+        h_bf = {}
+        h_codes = [held([P, S], U32, f"h_codes{b}") for b in range(2)]
+        h_scales = [held([P, S], U8, f"h_scales{b}") for b in range(2)]
+
+        def match(b, chunk):
+            pair, k = divmod(chunk, 2)
+            if k == 0:
+                if (b, pair) in h_at:
+                    h_bf[b, pair] = at([P, 4 * PAIR], BF16, f"h{b}{pair}", h_at[b, pair])
+                else:
+                    h_bf[b, pair] = held([P, 4 * PAIR], BF16, f"h{b}{pair}")
+            dst = h_bf[b, pair][:, k * 4 * CHUNK : (k + 1) * 4 * CHUNK]
             nc.vector.tensor_tensor(
                 dst.rearrange("p (g i t) -> p g t i", i=2, t=4),
                 window[b, chunk][:].rearrange("p t (g i) -> p g t i", i=2),
-                site[b, half][:, :, c0 : c0 + CHUNK].rearrange("p t (g i) -> p g t i", i=2),
+                site[b, pair][:, :, k * CHUNK : (k + 1) * CHUNK].rearrange("p t (g i) -> p g t i", i=2),
                 MULT,
             )
 
-        h_q = {}
+        def quantize_h(b, j0, width):
+            pair, c0 = divmod(j0, PAIR)
+            values = h_bf[b, pair][:, 4 * c0 : 4 * (c0 + width)]
+            quantize(values, h_codes[b][:, j0 : j0 + width], h_scales[b][:, j0 : j0 + width])
+
         out_rows = out.rearrange("(c p) j -> p c j", p=P)
 
-        def score(j0, width, first_bank):
-            blocks = 1 if width == HALF else 2
-            for c0 in range(0, N // P, blocks):
+        def score(j0, width, bank_numbers, on_vector=()):
+            blocks = N // P // len(bank_numbers)
+            for g, number in enumerate(bank_numbers):
+                c0 = g * blocks
                 res = held([P, blocks, width], F32, f"res{j0}_{c0}")
-                bank = bank_tile([P, blocks, width], f"score_bank{j0}_{c0}", first_bank + c0 // blocks)
+                bank = bank_tile([P, blocks, width], f"score_bank{j0}_{c0}", number)
                 for b in range(2):
                     for k in range(blocks):
                         c = c0 + k
@@ -250,69 +290,63 @@ def tile_list_guide_cleavage_scores_kernel(
                             out=bank[:, k, :],
                             lhsT=w3_q[b][0][:, c * P : (c + 1) * P].bitcast(FP8X4),
                             lhsT_scale=w3_q[b][1][:, c * P : (c + 1) * P],
-                            rhs=h_q[b, j0][0][:, :width].bitcast(FP8X4),
-                            rhs_scale=h_q[b, j0][1][:, :width],
+                            rhs=h_codes[b][:, j0 : j0 + width].bitcast(FP8X4),
+                            rhs_scale=h_scales[b][:, j0 : j0 + width],
                             start=(b == 0 and k == 0),
                             stop=(b == 1 and k == blocks - 1),
                         )
-                for k in range(blocks):
-                    c = c0 + k
-                    if j0 == S - CHUNK and c0:
-                        nc.vector.tensor_scalar_add(res[:, k, :], bank[:, k, :], bias_col[:, c : c + 1])
-                    else:
+                if g in on_vector:
+                    spread = bias_col[:, c0 : c0 + blocks].unsqueeze(2).to_broadcast([P, blocks, width])
+                    nc.vector.tensor_tensor(res[:], bank[:], spread, ADD)
+                else:
+                    for k in range(blocks):
+                        c = c0 + k
                         nc.scalar.activation(res[:, k, :], bank[:, k, :], IDENT, bias=bias_col[:, c : c + 1])
                 nc.sync.dma_start(out_rows[:, c0 : c0 + blocks, j0 : j0 + width], res[:])
 
-        def h_tile(name, entries, tag=None):
-            return held([P, entries * 4], BF16, name, tag)
+        window_sums(0, range(6), 0)
+        w2_bf[1, 0] = round_w2(1, 0, 4, held([P, 4 * HALF], BF16, "w2_bf1"))
+        for chunk in range(6):
+            match(0, chunk)
+            if chunk in (2, 4):
+                quantize_h(0, (chunk - 2) * CHUNK, PAIR)
+        site_sums(1, 0, 0)
+        site_sums(1, 1, 2)
+        quantize_w2(1, 0, 4, held([P, HALF], U32, "w2q10_codes"))
+        quantize_h(0, 2 * PAIR, PAIR)
+        window_sums(1, (0, 1), 6)
+        w3_bf = [round_w3(w3_raw[0], at([P, 4 * N], BF16, "w3_bf0", w3_bf_at[0]), 2)]
+        w3_bf.append(round_w3(w3_raw[1], at([P, 4 * N], BF16, "w3_bf1", w3_bf_at[1]), 4))
+        window_sums(1, (2, 3), 0)
+        site_sums(1, 2, 4)
+        window_sums(1, (4, 5), 2)
+        match(1, 0)
+        match(1, 1)
+        site_sums(1, 3, 6)
+        match(1, 2)
+        quantize_h(1, 0, PAIR)
+        match(1, 3)
+        w3_q = [quantize_weight(w3_bf[0], held([P, N], U32, "w3q0_codes"), "w3q0")]
+        quantize_h(1, PAIR, PAIR)
+        w3_q.append(quantize_weight(w3_bf[1], held([P, N], U32, "w3q1_codes"), "w3q1"))
+        score(0, PAIR, (0, 1))
+        score(PAIR, PAIR, (4, 5))
+        match(1, 4)
+        match(1, 5)
 
-        def part(h_bf, k):
-            return h_bf[:, k * CHUNK * 4 : (k + 1) * CHUNK * 4]
-
-        def quantize_h(h_bf, pieces, tag=None, offset=None):
-            width = h_bf.shape[1] // 4
-            codes, scales = quantize(h_bf[:], width, "h%d_%d" % pieces[0], tag, offset)
-            for k, key in enumerate(pieces):
-                c0 = k * width // len(pieces)
-                h_q[key] = (codes[:, c0:], scales[:, c0:])
-
-        third_pieces = [(0, 4), (0, 5), (1, 4), (1, 5)]
-        last_pieces = [(0, 6), (1, 6), (0, 7), (1, 7)]
-
-        first = [h_tile(f"h_first{b}", HALF) for b in range(2)]
-        window_sums([(0, k) for k in range(4)], HIGH)
-        for k in range(4):
-            match(0, k, part(first[0], k))
-        round_w2(1, held([P, HALF * 4], BF16, "w2_bf1"))
-        site_sums(0, 1, HIGH)
-        w3_bf[0] = round_on_gpsimd(w3_raw[0], held([P, N * 4], BF16, "w3_bf0"), 4)
-        w2_q.append(quantize(w2_bf[1][:], HALF, "w2q1", None, w2a_at + N * 8))
-        quantize_h(first[0], [(0, 0)])
-        window_sums([(1, k) for k in range(4)], LOW)
-        round_w3(1, nc.scalar.copy, 4, held([P, N * 4], BF16, "w3_bf1", "slot_w31"))
-        site_sums(1, 1, LOW)
-        for k in range(4):
-            match(1, k, part(first[1], k))
-        w3_q = [quantize(w3_bf[0][:], N, "w3q0", "slot_picked20")]
-        quantize_h(first[1], [(1, 0)])
-        w3_q.append(quantize(w3_bf[1][:], N, "w3q1"))
-        window_sums(third_pieces, HIGH)
-        score(0, HALF, LOW)
-
-        third = h_tile("h_third", 2 * PAIR, "slot_w31")
-        for k, (b, chunk) in enumerate(third_pieces):
-            match(b, chunk, part(third, k))
-        window_sums(last_pieces, HIGH)
-        sixth = h_tile("h_sixth", 2 * CHUNK)
-        match(0, 6, part(sixth, 0))
-        quantize_h(third, [(0, HALF), (1, HALF)])
-        score(HALF, PAIR, LOW)
-        match(1, 6, part(sixth, 1))
-        last = [h_tile(f"h_last{b}", CHUNK) for b in range(2)]
-        match(0, 7, part(last[0], 0))
-        quantize_h(sixth, [(0, 6 * CHUNK), (1, 6 * CHUNK)])
-        score(6 * CHUNK, CHUNK, LOW + 2)
-        quantize_h(last[0], [(0, 7 * CHUNK)])
-        match(1, 7, part(last[1], 0))
-        quantize_h(last[1], [(1, 7 * CHUNK)])
-        score(7 * CHUNK, CHUNK, HIGH)
+        for b in range(2):
+            window_sums(b, (6,), 6 + b)
+        match(0, 6)
+        quantize_h(1, 2 * PAIR, PAIR)
+        score(2 * PAIR, PAIR, (0, 1))
+        for b in range(2):
+            window_sums(b, (7,), 2 + b)
+        match(1, 6)
+        quantize_h(0, 6 * CHUNK, CHUNK)
+        match(0, 7)
+        quantize_h(1, 6 * CHUNK, CHUNK)
+        score(6 * CHUNK, CHUNK, (4,))
+        match(1, 7)
+        quantize_h(0, 7 * CHUNK, CHUNK)
+        quantize_h(1, 7 * CHUNK, CHUNK)
+        score(7 * CHUNK, CHUNK, (5, 6), on_vector=(1,))

@@ -44,19 +44,20 @@ def tile_list_guide_cleavage_scores_kernel(
             return psum.tile(shape, F32, name=name, offset=bank * BANK_BYTES)
 
         big_bytes = 4 * T
-        table1_at = 0
-        w2b_at = table1_at + big_bytes
+        table2_at = 0
+        w2b_at = table2_at + big_bytes
         w3_bf_at = [w2b_at + big_bytes + b * big_bytes // 2 for b in range(2)]
-        site00_at = w3_bf_at[1] + big_bytes // 2
-        w1a_at = site00_at + big_bytes // 2
-        site_at = {(0, 0): site00_at, (1, 0): w2b_at, (1, 1): w2b_at + big_bytes // 2}
+        w3b_at = w3_bf_at[1] + big_bytes // 2
+        w2a_at = w3b_at + big_bytes
+        site_at = {(0, 3): w2a_at, (1, 2): w2b_at, (1, 3): w3b_at}
         h_at = {(1, 2): w3_bf_at[1] - big_bytes // 8}
 
         def load_table(words, tile):
             nc.sync.dma_start(tile[:], words.rearrange("p t i -> p (t i)").bitcast(I32))
             return tile
 
-        def load_w1(b, raw):
+        def load_w1(b):
+            raw = held([P, 2, HALF // 2], I32, f"w1_raw{b}")
             nc.sync.dma_start(raw[:], w1_words.rearrange("a p n -> p a n")[:, :, b * H : (b + 1) * H].bitcast(I32))
             return raw
 
@@ -64,8 +65,7 @@ def tile_list_guide_cleavage_scores_kernel(
             nc.sync.dma_start(raw[:], w2.rearrange("(p s) n -> p s n", s=4)[:, :, b * HALF : (b + 1) * HALF])
             return raw
 
-        def load_w3(b):
-            raw = held([P, 4, N], F32, f"w3_raw{b}")
+        def load_w3(b, raw):
             by_t = w3[b * HALF : (b + 1) * HALF, :].rearrange("(u t i) n -> t u i n", t=4, i=8)
             for t in range(4):
                 nc.sync.dma_start(raw[:, t, :], by_t[t])
@@ -77,10 +77,9 @@ def tile_list_guide_cleavage_scores_kernel(
         scale_win2 = held([P, T // 4], I32, "scale_win2")
         w1s_raw = held([P, 2, H // 4], I32, "w1s_raw")
         planes = held([P, 2, S // 4], I32, "planes")
-        plane2 = held([P, S // 4], I32, "plane2")
         nc.gpsimd.memset(scale_win[:], 0)
         w1_planes = held([P, 2 * H // 4], I32, "w1_planes")
-        for tile in (scale_win2, w1_planes, planes, plane2):
+        for tile in (scale_win2, w1_planes, planes):
             nc.vector.memset(tile[:], 0)
         nc.sync.dma_start(list1[:], offs)
         nc.sync.dma_start(list2[:], offs2)
@@ -89,29 +88,18 @@ def tile_list_guide_cleavage_scores_kernel(
             nc.scalar.dma_start(w1s_raw[32 * d : 32 * d + 4], rows.bitcast(I32))
         nc.sync.dma_start(scale_win[::4], tab_scales.rearrange("a q t -> q a t").bitcast(I32))
         table0 = load_table(tab_words[0], held([P, T], I32, "table0"))
-        nc.sync.dma_start(scale_win2[::8], tab2_scales[0].bitcast(I32))
-        w2_raw = [load_w2(0, held([P, 4, HALF], F32, "w2_raw0"))]
-        w1_raw = [load_w1(0, at([P, 2, HALF // 2], I32, "w1_raw0", w1a_at))]
+        for e in range(4):
+            nc.gpsimd.dma_start(scale_win2[4 + e :: 32], tab2_scales[0, e::4, :].bitcast(I32))
+        w1_raw = [load_w1(0)]
+        table1 = load_table(tab_words[1], held([P, T], I32, "table1"))
 
         picked_scales = held([P, S], U8, "picked_scales")
         nc.vector.tensor_copy(picked_scales[:], scale_win[:].bitcast(U8).indirect(list1[:]))
         for d in QUADRANTS:
             nc.sync.dma_start(planes[32 * d : 32 * d + 4], picked_scales[32 * d : 32 * d + 32 : 4].bitcast(I32))
-        table1 = load_table(tab_words[1], at([P, T], I32, "table1", table1_at))
-        w1_raw.append(load_w1(1, at([P, 2, HALF // 2], I32, "w1_raw1", site00_at)))
-        table2 = load_table(tab2_words[0], held([P, T], I32, "table2"))
-
-        picked0 = held([P, S], U32, "picked0")
-        nc.vector.tensor_copy(picked0[:], table0[:].bitcast(U32).indirect(list1[:]))
-        picked_scales2 = held([P, S], U8, "picked_scales2")
-        nc.vector.tensor_copy(picked_scales2[:], scale_win2[:].bitcast(U8).indirect(list2[:]))
-        for d in QUADRANTS:
-            nc.sync.dma_start(plane2[32 * d + 4 : 32 * d + 8], picked_scales2[32 * d : 32 * d + 32 : 8].bitcast(I32))
-        w2_raw.append(load_w2(1, at([P, 4, HALF], F32, "w2_raw1", w2b_at)))
-        w3_raw = [load_w3(b) for b in range(2)]
-        bias_col = held([P, N // P], F32, "bias_col")
-        with nc.allow_non_contiguous_dma(reason="bias onto partitions"):
-            nc.sync.dma_start(bias_col[:], bias.rearrange("(c p) -> p c", p=P))
+        table2 = load_table(tab2_words[0], at([P, T], I32, "table2", table2_at))
+        w1_raw.append(load_w1(1))
+        w2_raw = [load_w2(0, at([P, 4, HALF], F32, "w2_raw0", w2a_at))]
 
         def gather_pieces(window, offsets, widths, name):
             picked = held([P, S], U32, name)
@@ -122,6 +110,14 @@ def tile_list_guide_cleavage_scores_kernel(
                 j0 = j0 + width
             return picked
 
+        picked = [gather_pieces(table0, list1, (S,), "picked0")]
+        picked.append(gather_pieces(table1, list1, (PAIR, PAIR, HALF), "picked1"))
+        w2_raw.append(load_w2(1, at([P, 4, HALF], F32, "w2_raw1", w2b_at)))
+        w3_raw = [load_w3(0, held([P, 4, N], F32, "w3_raw0")), load_w3(1, at([P, 4, N], F32, "w3_raw1", w3b_at))]
+        bias_col = held([P, N // P], F32, "bias_col")
+        with nc.allow_non_contiguous_dma(reason="bias onto partitions"):
+            nc.sync.dma_start(bias_col[:], bias.rearrange("(c p) -> p c", p=P))
+
         for d in QUADRANTS:
             rows = slice(32 * d, 32 * d + 4)
             nc.scalar.copy(
@@ -129,26 +125,20 @@ def tile_list_guide_cleavage_scores_kernel(
                 w1s_raw[rows].bitcast(U32).rearrange("p a (b u t i) -> p (a b) t u i", b=2, t=4, i=2),
             )
 
-        def order_w1(b, copy, ordered):
-            copy(
+        def order_w1(b):
+            ordered = held([P, HALF], U32, f"w1_ord{b}")
+            nc.scalar.copy(
                 ordered[:].rearrange("p (a t u i) -> p a t u i", a=2, t=4, i=4),
                 w1_raw[b][:].bitcast(U32).rearrange("p a (u t i) -> p a t u i", t=4, i=4),
             )
             return ordered
 
-        def round_w2(b, first, count, rounded):
-            dst = rounded[:].rearrange("p (t u h i s) -> p t u h s i", t=count, h=2, i=4, s=4)
+        def round_w2(b, copies):
+            rounded = held([P, 4 * HALF], BF16, f"w2_bf{b}")
+            dst = rounded[:].rearrange("p (t u h i s) -> p t u h s i", t=4, h=2, i=4, s=4)
             src = w2_raw[b][:].rearrange("p s (u t h i) -> p t u h s i", t=4, h=2, i=4)
-            for k in range(count):
-                t = first + k
-                if (b, t) == (0, 0):
-                    nc.scalar.activation(
-                        rounded[:].rearrange("p (t u i s) -> p t u i s", t=count, i=8, s=4)[:, k],
-                        w2_raw[b][:].rearrange("p s (u t i) -> p t u i s", t=4, i=8)[:, t],
-                        IDENT,
-                    )
-                else:
-                    nc.scalar.copy(dst[:, k], src[:, t])
+            for t, copy in enumerate(copies):
+                copy(dst[:, t], src[:, t])
             return rounded
 
         def round_w3(raw, rounded, on_gpsimd):
@@ -171,11 +161,7 @@ def tile_list_guide_cleavage_scores_kernel(
             quantize(rounded[:], codes[:], scales[:])
             return codes, scales
 
-        w1_ord = [order_w1(0, nc.scalar.copy, held([P, HALF], U32, "w1_ord0"))]
-        w2_bf = {(0, 0): round_w2(0, 0, 2, held([P, 2 * HALF], BF16, "w2_bf00"))}
-        w2_bf[0, 2] = round_w2(0, 2, 2, at([P, 2 * HALF], BF16, "w2_bf02", w1a_at))
-        picked = [picked0, gather_pieces(table1, list1, (PAIR, PAIR, HALF), "picked1")]
-        w1_ord.append(order_w1(1, nc.scalar.copy, held([P, HALF], U32, "w1_ord1")))
+        w1_ord = [order_w1(0)]
 
         def site_passes(banks, a, b, pair, opens):
             for t in range(4):
@@ -219,19 +205,16 @@ def tile_list_guide_cleavage_scores_kernel(
             copy_site(banks, b, pair)
 
         site_sums(0, 2, 4)
-        site_sums(0, 3, 6)
+        w1_ord.append(order_w1(1))
 
-        w2_q = {}
-
-        def quantize_w2(b, first, count, codes):
-            scales = held([P, count * P], U8, f"w2q{b}{first}_scales")
-            quantize(w2_bf[b, first][:], codes[:], scales[:])
-            for k in range(count):
-                w2_q[b, first + k] = (codes[:, k * P : (k + 1) * P], scales[:, k * P : (k + 1) * P])
-
-        quantize_w2(0, 0, 2, held([P, 2 * P], U32, "w2q00_codes"))
-        quantize_w2(0, 2, 2, at([P, 2 * P], U32, "w2q02_codes", table1_at))
         picked2 = gather_pieces(table2, list2, (HALF, HALF), "picked2")
+        picked_scales2 = at([P, S], U8, "picked_scales2", table2_at)
+        nc.vector.tensor_copy(picked_scales2[:], scale_win2[:].bitcast(U8).indirect(list2[:]))
+        w2_bf = [round_w2(0, 2 * [nc.scalar.copy] + 2 * [nc.vector.tensor_copy])]
+        w2_q = [quantize_weight(w2_bf[0], held([P, HALF], U32, "w2q0_codes"), "w2q0")]
+        site_sums(0, 3, 6)
+        site_sums(1, 0, 0)
+        site_sums(1, 1, 2)
 
         window = {}
 
@@ -242,10 +225,10 @@ def tile_list_guide_cleavage_scores_kernel(
                 for t in range(4):
                     nc.tensor.matmul_mx(
                         out=bank[:, t, :],
-                        lhsT=w2_q[b, t][0].bitcast(FP8X4),
-                        lhsT_scale=w2_q[b, t][1],
+                        lhsT=w2_q[b][0][:, t * P : (t + 1) * P].bitcast(FP8X4),
+                        lhsT_scale=w2_q[b][1][:, t * P : (t + 1) * P],
                         rhs=picked2[:, j0 : j0 + CHUNK].bitcast(FP8X4),
-                        rhs_scale=plane2[:].bitcast(U8)[4:, j0 : j0 + CHUNK],
+                        rhs_scale=picked_scales2[4:, j0 : j0 + CHUNK],
                         start=True,
                         stop=True,
                     )
@@ -304,25 +287,29 @@ def tile_list_guide_cleavage_scores_kernel(
                         nc.scalar.activation(res[:, k, :], bank[:, k, :], IDENT, bias=bias_col[:, c : c + 1])
                 nc.sync.dma_start(out_rows[:, c0 : c0 + blocks, j0 : j0 + width], res[:])
 
-        window_sums(0, range(6), 0)
-        w2_bf[1, 0] = round_w2(1, 0, 4, held([P, 4 * HALF], BF16, "w2_bf1"))
-        for chunk in range(6):
-            match(0, chunk)
-            if chunk in (2, 4):
-                quantize_h(0, (chunk - 2) * CHUNK, PAIR)
-        site_sums(1, 0, 0)
-        site_sums(1, 1, 2)
-        quantize_w2(1, 0, 4, held([P, HALF], U32, "w2q10_codes"))
+        window_sums(0, (0, 1), 4)
+        window_sums(0, (2, 3), 6)
+        w2_bf.append(round_w2(1, 4 * [nc.scalar.copy]))
+        match(0, 0)
+        match(0, 1)
+        window_sums(0, (4, 5), 4)
+        site_sums(1, 2, 0)
+        match(0, 2)
+        quantize_h(0, 0, PAIR)
+        match(0, 3)
+        match(0, 4)
+        quantize_h(0, PAIR, PAIR)
+        match(0, 5)
+        w2_q.append(quantize_weight(w2_bf[1], held([P, HALF], U32, "w2q1_codes"), "w2q1"))
         quantize_h(0, 2 * PAIR, PAIR)
         window_sums(1, (0, 1), 6)
-        w3_bf = [round_w3(w3_raw[0], at([P, 4 * N], BF16, "w3_bf0", w3_bf_at[0]), 2)]
-        w3_bf.append(round_w3(w3_raw[1], at([P, 4 * N], BF16, "w3_bf1", w3_bf_at[1]), 4))
-        window_sums(1, (2, 3), 0)
-        site_sums(1, 2, 4)
-        window_sums(1, (4, 5), 2)
+        window_sums(1, (2, 3), 4)
+        w3_bf = [round_w3(w3_raw[0], at([P, 4 * N], BF16, "w3_bf0", w3_bf_at[0]), 4)]
+        w3_bf.append(round_w3(w3_raw[1], at([P, 4 * N], BF16, "w3_bf1", w3_bf_at[1]), 0))
+        site_sums(1, 3, 2)
         match(1, 0)
         match(1, 1)
-        site_sums(1, 3, 6)
+        window_sums(1, (4, 5), 6)
         match(1, 2)
         quantize_h(1, 0, PAIR)
         match(1, 3)
@@ -330,23 +317,23 @@ def tile_list_guide_cleavage_scores_kernel(
         quantize_h(1, PAIR, PAIR)
         w3_q.append(quantize_weight(w3_bf[1], held([P, N], U32, "w3q1_codes"), "w3q1"))
         score(0, PAIR, (0, 1))
-        score(PAIR, PAIR, (4, 5))
+        score(PAIR, PAIR, (2, 3))
         match(1, 4)
         match(1, 5)
 
         for b in range(2):
-            window_sums(b, (6,), 6 + b)
+            window_sums(b, (6,), 4 + b)
         match(0, 6)
         quantize_h(1, 2 * PAIR, PAIR)
         score(2 * PAIR, PAIR, (0, 1))
         for b in range(2):
-            window_sums(b, (7,), 2 + b)
+            window_sums(b, (7,), 6 + b)
         match(1, 6)
         quantize_h(0, 6 * CHUNK, CHUNK)
         match(0, 7)
         quantize_h(1, 6 * CHUNK, CHUNK)
-        score(6 * CHUNK, CHUNK, (4,))
+        score(6 * CHUNK, CHUNK, (2,))
         match(1, 7)
         quantize_h(0, 7 * CHUNK, CHUNK)
         quantize_h(1, 7 * CHUNK, CHUNK)
-        score(7 * CHUNK, CHUNK, (5, 6), on_vector=(1,))
+        score(7 * CHUNK, CHUNK, (3, 4), on_vector=(1,))

@@ -49,8 +49,11 @@ def tile_list_guide_cleavage_scores_kernel(
         w3_bf_at = [w2b_at + big_bytes + b * big_bytes // 2 for b in range(2)]
         w3b_at = w3_bf_at[1] + big_bytes // 2
         w2a_at = w3b_at + big_bytes
-        site_at = {(0, 3): w2a_at, (1, 2): w2b_at, (1, 3): w3b_at}
-        h_at = {(1, 2): w3_bf_at[1] - big_bytes // 8}
+        w2a_bf_at = w2a_at + big_bytes
+        site_at = {(0, 2): w2a_at, (0, 3): w2a_at + big_bytes // 2, (1, 3): w3b_at}
+        site_at[1, 0], site_at[1, 1] = w2b_at, w2b_at + big_bytes // 2
+        site_at[1, 2] = w2a_bf_at + big_bytes // 2
+        h_at = {(1, HALF): w3_bf_at[1]}
 
         def load_table(words, tile):
             nc.sync.dma_start(tile[:], words.rearrange("p t i -> p (t i)").bitcast(I32))
@@ -133,10 +136,20 @@ def tile_list_guide_cleavage_scores_kernel(
             )
             return ordered
 
-        def round_w2(b, copies):
-            rounded = held([P, 4 * HALF], BF16, f"w2_bf{b}")
-            dst = rounded[:].rearrange("p (t u h i s) -> p t u h s i", t=4, h=2, i=4, s=4)
-            src = w2_raw[b][:].rearrange("p s (u t h i) -> p t u h s i", t=4, h=2, i=4)
+        def on_scalar(dst, src):
+            nc.scalar.copy(dst.rearrange("p u (h i) s -> p u h s i", i=4), src.rearrange("p u (h i) s -> p u h s i", i=4))
+
+        def on_vector(dst, src):
+            nc.vector.tensor_copy(
+                dst.rearrange("p u (h i) s -> p u h s i", i=4), src.rearrange("p u (h i) s -> p u h s i", i=4)
+            )
+
+        def on_gpsimd(dst, src):
+            nc.gpsimd.tensor_scalar(dst, src, 1.0, 0.0, MULT, ADD)
+
+        def round_w2(b, copies, rounded):
+            dst = rounded[:].rearrange("p (t u i s) -> p t u i s", t=4, i=8, s=4)
+            src = w2_raw[b][:].rearrange("p s (u t i) -> p t u i s", t=4, i=8)
             for t, copy in enumerate(copies):
                 copy(dst[:, t], src[:, t])
             return rounded
@@ -204,17 +217,21 @@ def tile_list_guide_cleavage_scores_kernel(
                 site_passes(banks, a, b, pair, a == 1)
             copy_site(banks, b, pair)
 
-        site_sums(0, 2, 4)
         w1_ord.append(order_w1(1))
 
         picked2 = gather_pieces(table2, list2, (HALF, HALF), "picked2")
-        picked_scales2 = at([P, S], U8, "picked_scales2", table2_at)
-        nc.vector.tensor_copy(picked_scales2[:], scale_win2[:].bitcast(U8).indirect(list2[:]))
-        w2_bf = [round_w2(0, 2 * [nc.scalar.copy] + 2 * [nc.vector.tensor_copy])]
+
+        def gather_plane2(half, offset):
+            plane = at([P, HALF], U8, f"plane2{half}", offset)
+            cols = slice(half * HALF // 16, (half + 1) * HALF // 16)
+            nc.vector.tensor_copy(plane[:], scale_win2[:].bitcast(U8).indirect(list2[:, cols]))
+            return plane
+
+        plane2 = [gather_plane2(0, table2_at)]
+        copies = 2 * [on_scalar] + 2 * [on_vector]
+        w2_bf = [round_w2(0, copies, at([P, 4 * HALF], BF16, "w2_bf0", w2a_bf_at))]
         w2_q = [quantize_weight(w2_bf[0], held([P, HALF], U32, "w2q0_codes"), "w2q0")]
-        site_sums(0, 3, 6)
-        site_sums(1, 0, 0)
-        site_sums(1, 1, 2)
+        plane2.append(gather_plane2(1, w2a_bf_at))
 
         window = {}
 
@@ -228,39 +245,43 @@ def tile_list_guide_cleavage_scores_kernel(
                         lhsT=w2_q[b][0][:, t * P : (t + 1) * P].bitcast(FP8X4),
                         lhsT_scale=w2_q[b][1][:, t * P : (t + 1) * P],
                         rhs=picked2[:, j0 : j0 + CHUNK].bitcast(FP8X4),
-                        rhs_scale=picked_scales2[4:, j0 : j0 + CHUNK],
+                        rhs_scale=plane2[j0 // HALF][4:, j0 % HALF : j0 % HALF + CHUNK],
                         start=True,
                         stop=True,
                     )
                 window[b, chunk] = bank
 
-        h_bf = {}
-        h_codes = [held([P, S], U32, f"h_codes{b}") for b in range(2)]
-        h_scales = [held([P, S], U8, f"h_scales{b}") for b in range(2)]
+        h_bf, h_q = {}, {}
+        segments = ((0, HALF), (HALF, PAIR), (6 * CHUNK, CHUNK), (7 * CHUNK, CHUNK))
 
         def match(b, chunk):
             pair, k = divmod(chunk, 2)
-            if k == 0:
-                if (b, pair) in h_at:
-                    h_bf[b, pair] = at([P, 4 * PAIR], BF16, f"h{b}{pair}", h_at[b, pair])
+            j0, width = [seg for seg in segments if seg[0] <= chunk * CHUNK][-1]
+            if (b, j0) not in h_bf:
+                if (b, j0) in h_at:
+                    h_bf[b, j0] = at([P, 4 * width], BF16, f"h{b}_{j0}", h_at[b, j0])
                 else:
-                    h_bf[b, pair] = held([P, 4 * PAIR], BF16, f"h{b}{pair}")
-            dst = h_bf[b, pair][:, k * 4 * CHUNK : (k + 1) * 4 * CHUNK]
+                    h_bf[b, j0] = held([P, 4 * width], BF16, f"h{b}_{j0}")
+            c0 = 4 * (chunk * CHUNK - j0)
             nc.vector.tensor_tensor(
-                dst.rearrange("p (g i t) -> p g t i", i=2, t=4),
+                h_bf[b, j0][:, c0 : c0 + 4 * CHUNK].rearrange("p (g i t) -> p g t i", i=2, t=4),
                 window[b, chunk][:].rearrange("p t (g i) -> p g t i", i=2),
                 site[b, pair][:, :, k * CHUNK : (k + 1) * CHUNK].rearrange("p t (g i) -> p g t i", i=2),
                 MULT,
             )
 
-        def quantize_h(b, j0, width):
-            pair, c0 = divmod(j0, PAIR)
-            values = h_bf[b, pair][:, 4 * c0 : 4 * (c0 + width)]
-            quantize(values, h_codes[b][:, j0 : j0 + width], h_scales[b][:, j0 : j0 + width])
+        def quantize_h(b, j0, width, offset=None):
+            if offset is None:
+                codes = held([P, width], U32, f"h_codes{b}_{j0}")
+            else:
+                codes = at([P, width], U32, f"h_codes{b}_{j0}", offset)
+            scales = held([P, width], U8, f"h_scales{b}_{j0}")
+            quantize(h_bf[b, j0][:], codes[:], scales[:])
+            h_q[b, j0] = (codes, scales)
 
         out_rows = out.rearrange("(c p) j -> p c j", p=P)
 
-        def score(j0, width, bank_numbers, on_vector=()):
+        def score(j0, width, bank_numbers, by_vector=()):
             blocks = N // P // len(bank_numbers)
             for g, number in enumerate(bank_numbers):
                 c0 = g * blocks
@@ -273,12 +294,12 @@ def tile_list_guide_cleavage_scores_kernel(
                             out=bank[:, k, :],
                             lhsT=w3_q[b][0][:, c * P : (c + 1) * P].bitcast(FP8X4),
                             lhsT_scale=w3_q[b][1][:, c * P : (c + 1) * P],
-                            rhs=h_codes[b][:, j0 : j0 + width].bitcast(FP8X4),
-                            rhs_scale=h_scales[b][:, j0 : j0 + width],
+                            rhs=h_q[b, j0][0][:].bitcast(FP8X4),
+                            rhs_scale=h_q[b, j0][1][:],
                             start=(b == 0 and k == 0),
                             stop=(b == 1 and k == blocks - 1),
                         )
-                if g in on_vector:
+                if g in by_vector:
                     spread = bias_col[:, c0 : c0 + blocks].unsqueeze(2).to_broadcast([P, blocks, width])
                     nc.vector.tensor_tensor(res[:], bank[:], spread, ADD)
                 else:
@@ -287,53 +308,53 @@ def tile_list_guide_cleavage_scores_kernel(
                         nc.scalar.activation(res[:, k, :], bank[:, k, :], IDENT, bias=bias_col[:, c : c + 1])
                 nc.sync.dma_start(out_rows[:, c0 : c0 + blocks, j0 : j0 + width], res[:])
 
-        window_sums(0, (0, 1), 4)
-        window_sums(0, (2, 3), 6)
-        w2_bf.append(round_w2(1, 4 * [nc.scalar.copy]))
+        window_sums(0, (0, 1, 2, 3), 0)
+        site_sums(0, 2, 4)
+        site_sums(0, 3, 6)
+        w2_bf.append(round_w2(1, 2 * [on_gpsimd] + 2 * [on_scalar], held([P, 4 * HALF], BF16, "w2_bf1")))
         match(0, 0)
         match(0, 1)
-        window_sums(0, (4, 5), 4)
-        site_sums(1, 2, 0)
+        window_sums(0, (4, 5), 0)
+        site_sums(1, 0, 4)
+        site_sums(1, 1, 6)
         match(0, 2)
-        quantize_h(0, 0, PAIR)
         match(0, 3)
-        match(0, 4)
-        quantize_h(0, PAIR, PAIR)
-        match(0, 5)
         w2_q.append(quantize_weight(w2_bf[1], held([P, HALF], U32, "w2q1_codes"), "w2q1"))
-        quantize_h(0, 2 * PAIR, PAIR)
-        window_sums(1, (0, 1), 6)
-        window_sums(1, (2, 3), 4)
+        match(0, 4)
+        match(0, 5)
+        window_sums(1, (0, 1), 2)
+        window_sums(1, (2, 3), 0)
+        site_sums(1, 2, 4)
         w3_bf = [round_w3(w3_raw[0], at([P, 4 * N], BF16, "w3_bf0", w3_bf_at[0]), 4)]
-        w3_bf.append(round_w3(w3_raw[1], at([P, 4 * N], BF16, "w3_bf1", w3_bf_at[1]), 0))
-        site_sums(1, 3, 2)
+        w3_bf.append(round_w3(w3_raw[1], at([P, 4 * N], BF16, "w3_bf1", w3_bf_at[1]), 2))
+        site_sums(1, 3, 6)
         match(1, 0)
         match(1, 1)
-        window_sums(1, (4, 5), 6)
+        window_sums(1, (4, 5), 2)
         match(1, 2)
-        quantize_h(1, 0, PAIR)
         match(1, 3)
-        w3_q = [quantize_weight(w3_bf[0], held([P, N], U32, "w3q0_codes"), "w3q0")]
-        quantize_h(1, PAIR, PAIR)
+        w3_q = [quantize_weight(w3_bf[0], at([P, N], U32, "w3q0_codes", site_at[1, 1]), "w3q0")]
+        quantize_h(0, 0, HALF, w3_bf_at[0])
+        quantize_h(1, 0, HALF)
         w3_q.append(quantize_weight(w3_bf[1], held([P, N], U32, "w3q1_codes"), "w3q1"))
-        score(0, PAIR, (0, 1))
-        score(PAIR, PAIR, (2, 3))
         match(1, 4)
         match(1, 5)
+        score(0, HALF, (0, 1, 4, 5))
 
         for b in range(2):
-            window_sums(b, (6,), 4 + b)
+            window_sums(b, (6,), 6 + b)
+        quantize_h(0, HALF, PAIR, site_at[1, 2])
+        quantize_h(1, HALF, PAIR)
         match(0, 6)
-        quantize_h(1, 2 * PAIR, PAIR)
-        score(2 * PAIR, PAIR, (0, 1))
         for b in range(2):
-            window_sums(b, (7,), 6 + b)
+            window_sums(b, (7,), 2 + b)
+        score(HALF, PAIR, (0, 1))
         match(1, 6)
         quantize_h(0, 6 * CHUNK, CHUNK)
         match(0, 7)
         quantize_h(1, 6 * CHUNK, CHUNK)
-        score(6 * CHUNK, CHUNK, (2,))
+        score(6 * CHUNK, CHUNK, (4,))
         match(1, 7)
         quantize_h(0, 7 * CHUNK, CHUNK)
         quantize_h(1, 7 * CHUNK, CHUNK)
-        score(7 * CHUNK, CHUNK, (3, 4), on_vector=(1,))
+        score(7 * CHUNK, CHUNK, (5, 6), by_vector=(1,))

@@ -139,11 +139,6 @@ def tile_list_guide_cleavage_scores_kernel(
         def on_scalar(dst, src):
             nc.scalar.copy(dst.rearrange("p u (h i) s -> p u h s i", i=4), src.rearrange("p u (h i) s -> p u h s i", i=4))
 
-        def on_vector(dst, src):
-            nc.vector.tensor_copy(
-                dst.rearrange("p u (h i) s -> p u h s i", i=4), src.rearrange("p u (h i) s -> p u h s i", i=4)
-            )
-
         def on_gpsimd(dst, src):
             nc.gpsimd.tensor_scalar(dst, src, 1.0, 0.0, MULT, ADD)
 
@@ -221,17 +216,17 @@ def tile_list_guide_cleavage_scores_kernel(
 
         picked2 = gather_pieces(table2, list2, (HALF, HALF), "picked2")
 
-        def gather_plane2(half, offset):
-            plane = at([P, HALF], U8, f"plane2{half}", offset)
-            cols = slice(half * HALF // 16, (half + 1) * HALF // 16)
+        def gather_plane2(j0, width, offset):
+            plane = at([P, width], U8, f"plane2_{j0}", offset)
+            cols = slice(j0 // 16, (j0 + width) // 16)
             nc.vector.tensor_copy(plane[:], scale_win2[:].bitcast(U8).indirect(list2[:, cols]))
-            return plane
+            return [plane[4:, c0 : c0 + CHUNK] for c0 in range(0, width, CHUNK)]
 
-        plane2 = [gather_plane2(0, table2_at)]
-        copies = 2 * [on_scalar] + 2 * [on_vector]
+        plane2 = gather_plane2(0, S - PAIR, table2_at)
+        copies = 2 * [on_scalar] + 2 * [on_gpsimd]
         w2_bf = [round_w2(0, copies, at([P, 4 * HALF], BF16, "w2_bf0", w2a_bf_at))]
         w2_q = [quantize_weight(w2_bf[0], held([P, HALF], U32, "w2q0_codes"), "w2q0")]
-        plane2.append(gather_plane2(1, w2a_bf_at))
+        plane2.extend(gather_plane2(S - PAIR, PAIR, w2a_bf_at))
 
         window = {}
 
@@ -245,7 +240,7 @@ def tile_list_guide_cleavage_scores_kernel(
                         lhsT=w2_q[b][0][:, t * P : (t + 1) * P].bitcast(FP8X4),
                         lhsT_scale=w2_q[b][1][:, t * P : (t + 1) * P],
                         rhs=picked2[:, j0 : j0 + CHUNK].bitcast(FP8X4),
-                        rhs_scale=plane2[j0 // HALF][4:, j0 % HALF : j0 % HALF + CHUNK],
+                        rhs_scale=plane2[chunk],
                         start=True,
                         stop=True,
                     )

@@ -48,11 +48,9 @@ def tile_list_guide_cleavage_scores_kernel(
         w2b_at = table2_at + big_bytes
         w3_bf_at = [w2b_at + big_bytes + b * big_bytes // 2 for b in range(2)]
         w3b_at = w3_bf_at[1] + big_bytes // 2
-        w2a_at = w3b_at + big_bytes
-        w2a_bf_at = w2a_at + big_bytes
-        site_at = {(0, 2): w2a_at, (0, 3): w2a_at + big_bytes // 2, (1, 3): w3b_at}
+        w2a_at = w3b_at + big_bytes + big_bytes // 4
+        site_at = {(0, 2): w2a_at - big_bytes // 4, (0, 3): w2a_at + big_bytes // 2, (1, 3): w3b_at}
         site_at[1, 0], site_at[1, 1] = w2b_at, w2b_at + big_bytes // 2
-        site_at[1, 2] = w2a_bf_at + big_bytes // 2
         h_at = {(1, HALF): w3_bf_at[1]}
 
         def load_table(words, tile):
@@ -101,7 +99,6 @@ def tile_list_guide_cleavage_scores_kernel(
         for d in QUADRANTS:
             nc.sync.dma_start(planes[32 * d : 32 * d + 4], picked_scales[32 * d : 32 * d + 32 : 4].bitcast(I32))
         table2 = load_table(tab2_words[0], at([P, T], I32, "table2", table2_at))
-        w1_raw.append(load_w1(1))
         w2_raw = [load_w2(0, at([P, 4, HALF], F32, "w2_raw0", w2a_at))]
 
         def gather_pieces(window, offsets, widths, name):
@@ -115,6 +112,7 @@ def tile_list_guide_cleavage_scores_kernel(
 
         picked = [gather_pieces(table0, list1, (S,), "picked0")]
         picked.append(gather_pieces(table1, list1, (PAIR, PAIR, HALF), "picked1"))
+        w1_raw.append(load_w1(1))
         w2_raw.append(load_w2(1, at([P, 4, HALF], F32, "w2_raw1", w2b_at)))
         w3_raw = [load_w3(0, held([P, 4, N], F32, "w3_raw0")), load_w3(1, at([P, 4, N], F32, "w3_raw1", w3b_at))]
         bias_col = held([P, N // P], F32, "bias_col")
@@ -212,8 +210,6 @@ def tile_list_guide_cleavage_scores_kernel(
                 site_passes(banks, a, b, pair, a == 1)
             copy_site(banks, b, pair)
 
-        w1_ord.append(order_w1(1))
-
         picked2 = gather_pieces(table2, list2, (HALF, HALF), "picked2")
 
         def gather_plane2(j0, width, offset):
@@ -224,9 +220,9 @@ def tile_list_guide_cleavage_scores_kernel(
 
         plane2 = gather_plane2(0, S - PAIR, table2_at)
         copies = 2 * [on_scalar] + 2 * [on_gpsimd]
-        w2_bf = [round_w2(0, copies, at([P, 4 * HALF], BF16, "w2_bf0", w2a_bf_at))]
+        w2_bf = [round_w2(0, copies, held([P, 4 * HALF], BF16, "w2_bf0"))]
         w2_q = [quantize_weight(w2_bf[0], held([P, HALF], U32, "w2q0_codes"), "w2q0")]
-        plane2.extend(gather_plane2(S - PAIR, PAIR, w2a_bf_at))
+        plane2.extend(gather_plane2(S - PAIR, PAIR, w2a_at + big_bytes // 4))
 
         window = {}
 
@@ -304,6 +300,7 @@ def tile_list_guide_cleavage_scores_kernel(
                 nc.sync.dma_start(out_rows[:, c0 : c0 + blocks, j0 : j0 + width], res[:])
 
         window_sums(0, (0, 1, 2, 3), 0)
+        w1_ord.append(order_w1(1))
         site_sums(0, 2, 4)
         site_sums(0, 3, 6)
         w2_bf.append(round_w2(1, 2 * [on_gpsimd] + 2 * [on_scalar], held([P, 4 * HALF], BF16, "w2_bf1")))
@@ -328,17 +325,17 @@ def tile_list_guide_cleavage_scores_kernel(
         window_sums(1, (4, 5), 2)
         match(1, 2)
         match(1, 3)
-        w3_q = [quantize_weight(w3_bf[0], at([P, N], U32, "w3q0_codes", site_at[1, 1]), "w3q0")]
-        quantize_h(0, 0, HALF, w3_bf_at[0])
-        quantize_h(1, 0, HALF)
+        w3_q = [quantize_weight(w3_bf[0], at([P, N], U32, "w3q0_codes", site_at[1, 0]), "w3q0")]
+        quantize_h(0, 0, HALF, site_at[1, 0] + big_bytes // 4)
         w3_q.append(quantize_weight(w3_bf[1], held([P, N], U32, "w3q1_codes"), "w3q1"))
+        quantize_h(1, 0, HALF)
         match(1, 4)
         match(1, 5)
         score(0, HALF, (0, 1, 4, 5))
 
         for b in range(2):
             window_sums(b, (6,), 6 + b)
-        quantize_h(0, HALF, PAIR, site_at[1, 2])
+        quantize_h(0, HALF, PAIR, w3_bf_at[0])
         quantize_h(1, HALF, PAIR)
         match(0, 6)
         for b in range(2):

@@ -49,7 +49,8 @@ def tile_list_guide_cleavage_scores_kernel(
         w3_bf_at = [w2b_at + big_bytes + b * big_bytes // 2 for b in range(2)]
         w3b_at = w3_bf_at[1] + big_bytes // 2
         w2a_at = w3b_at + big_bytes + big_bytes // 4
-        site_at = {(0, 2): w2a_at - big_bytes // 4, (0, 3): w2a_at + big_bytes // 2, (1, 3): w3b_at}
+        site_at = {(0, 2): w2a_at - big_bytes // 4, (0, 3): w2a_at + big_bytes // 2}
+        site_at[1, 2], site_at[1, 3] = w3b_at, w3b_at + big_bytes // 2
         site_at[1, 0], site_at[1, 1] = w2b_at, w2b_at + big_bytes // 2
         h_at = {(1, HALF): w3_bf_at[1]}
 
@@ -316,9 +317,9 @@ def tile_list_guide_cleavage_scores_kernel(
         match(0, 5)
         window_sums(1, (0, 1), 2)
         window_sums(1, (2, 3), 0)
-        site_sums(1, 2, 4)
         w3_bf = [round_w3(w3_raw[0], at([P, 4 * N], BF16, "w3_bf0", w3_bf_at[0]), 4)]
-        w3_bf.append(round_w3(w3_raw[1], at([P, 4 * N], BF16, "w3_bf1", w3_bf_at[1]), 2))
+        w3_bf.append(round_w3(w3_raw[1], at([P, 4 * N], BF16, "w3_bf1", w3_bf_at[1]), 0))
+        site_sums(1, 2, 4)
         site_sums(1, 3, 6)
         match(1, 0)
         match(1, 1)

@@ -148,70 +148,54 @@ def tile_list_guide_cleavage_scores_kernel(
                 copy(dst[:, t], src[:, t])
             return rounded
 
-        def round_w3(raw, rounded, on_gpsimd):
-            for c in range(4):
-                if c < on_gpsimd:
-                    dst = rounded[:].rearrange("p (c n t) -> p c n t", c=4, t=4)[:, c]
-                    src = raw[:].rearrange("p t (c n) -> p c n t", c=4)[:, c]
-                    nc.gpsimd.tensor_scalar(dst, src, 1.0, 0.0, MULT, ADD)
-                else:
-                    dst = rounded[:].rearrange("p (c g i t) -> p c g t i", c=4, i=4, t=4)[:, c]
-                    src = raw[:].rearrange("p t (c g i) -> p c g t i", c=4, i=4)[:, c]
-                    nc.scalar.copy(dst, src)
+        def round_w3(raw, first, copies, rounded):
+            dst = rounded[:].rearrange("p (c u i t) -> p c u i t", u=16, i=8, t=4)
+            src = raw[:].rearrange("p t (c u i) -> p c u i t", u=16, i=8)
+            for k, copy in enumerate(copies):
+                copy(dst[:, k], src[:, first + k])
             return rounded
 
         def quantize(values, codes, scales):
             nc.vector.quantize_mx(out=codes.bitcast(FP8X4), scales=scales, in_=values)
 
-        def quantize_weight(rounded, codes, name):
+        def quantize_weight(parts, codes, name):
             scales = held([P, HALF], U8, name + "_scales")
-            quantize(rounded[:], codes[:], scales[:])
+            width = HALF // len(parts)
+            for k, rounded in enumerate(parts):
+                quantize(rounded[:], codes[:, k * width : (k + 1) * width], scales[:, k * width : (k + 1) * width])
             return codes, scales
 
         w1_ord = [order_w1(0)]
 
-        def site_passes(banks, a, b, pair, opens):
-            for t in range(4):
-                word = a * HALF + t * P
-                col = a * H + b * HALF + t * P
-                nc.tensor.matmul_mx(
-                    out=banks[t // 2][:, t % 2, :],
-                    lhsT=w1_ord[b][:].bitcast(U8)[:, 2 * word : 2 * (word + P)].bitcast(FP4X4),
-                    lhsT_scale=w1_planes[:].bitcast(U8)[:, col : col + P],
-                    rhs=picked[a][:, pair * PAIR : (pair + 1) * PAIR].bitcast(FP8X4),
-                    rhs_scale=planes[:, a, :].bitcast(U8)[:, pair * PAIR : (pair + 1) * PAIR],
-                    start=(opens and t % 2 == 0),
-                    stop=(not opens and t % 2 == 1),
-                )
-
-        def site_banks(b, pair, first_bank):
-            return [bank_tile([P, 2, PAIR], f"site_bank{b}{pair}{k}", first_bank + k) for k in range(2)]
-
         site = {}
 
-        def copy_site(banks, b, pair):
+        def site_sums(b, pair, first_bank):
             if (b, pair) in site_at:
                 sums = at([P, 4, PAIR], F32, f"site{b}{pair}", site_at[b, pair])
             else:
                 sums = held([P, 4, PAIR], F32, f"site{b}{pair}")
             for k in range(2):
-                nc.scalar.activation(sums[:, 2 * k : 2 * k + 2, :], banks[k][:], IDENT)
+                bank = bank_tile([P, 2, PAIR], f"site_bank{b}{pair}{k}", first_bank + k)
+                for a in range(2):
+                    for e in range(2):
+                        word = a * HALF + (2 * k + e) * P
+                        col = a * H + b * HALF + (2 * k + e) * P
+                        nc.tensor.matmul_mx(
+                            out=bank[:, e, :],
+                            lhsT=w1_ord[b][:].bitcast(U8)[:, 2 * word : 2 * (word + P)].bitcast(FP4X4),
+                            lhsT_scale=w1_planes[:].bitcast(U8)[:, col : col + P],
+                            rhs=picked[a][:, pair * PAIR : (pair + 1) * PAIR].bitcast(FP8X4),
+                            rhs_scale=planes[:, a, :].bitcast(U8)[:, pair * PAIR : (pair + 1) * PAIR],
+                            start=(a == 0 and e == 0),
+                            stop=(a == 1 and e == 1),
+                        )
+                nc.scalar.activation(sums[:, 2 * k : 2 * k + 2, :], bank[:], IDENT)
             site[b, pair] = sums
 
-        first_banks = [site_banks(0, pair, 2 * pair) for pair in range(2)]
-        for pair in range(2):
-            site_passes(first_banks[pair], 0, 0, pair, True)
-        for pair in range(2):
-            site_passes(first_banks[pair], 1, 0, pair, False)
-            copy_site(first_banks[pair], 0, pair)
+        site_sums(0, 0, 0)
+        site_sums(0, 1, 2)
 
-        def site_sums(b, pair, first_bank):
-            banks = site_banks(b, pair, first_bank)
-            for a in (1, 0):
-                site_passes(banks, a, b, pair, a == 1)
-            copy_site(banks, b, pair)
-
-        picked2 = gather_pieces(table2, list2, (HALF, HALF), "picked2")
+        picked2 = gather_pieces(table2, list2, (S,), "picked2")
 
         def gather_plane2(j0, width, offset):
             plane = at([P, width], U8, f"plane2_{j0}", offset)
@@ -222,7 +206,7 @@ def tile_list_guide_cleavage_scores_kernel(
         plane2 = gather_plane2(0, S - PAIR, table2_at)
         copies = 2 * [on_scalar] + 2 * [on_gpsimd]
         w2_bf = [round_w2(0, copies, held([P, 4 * HALF], BF16, "w2_bf0"))]
-        w2_q = [quantize_weight(w2_bf[0], held([P, HALF], U32, "w2q0_codes"), "w2q0")]
+        w2_q = [quantize_weight([w2_bf[0]], held([P, HALF], U32, "w2q0_codes"), "w2q0")]
         plane2.extend(gather_plane2(S - PAIR, PAIR, w2a_at + big_bytes // 4))
 
         window = {}
@@ -312,13 +296,18 @@ def tile_list_guide_cleavage_scores_kernel(
         site_sums(1, 1, 6)
         match(0, 2)
         match(0, 3)
-        w2_q.append(quantize_weight(w2_bf[1], held([P, HALF], U32, "w2q1_codes"), "w2q1"))
+        w2_q.append(quantize_weight([w2_bf[1]], held([P, HALF], U32, "w2q1_codes"), "w2q1"))
         match(0, 4)
         match(0, 5)
         window_sums(1, (0, 1), 2)
         window_sums(1, (2, 3), 0)
-        w3_bf = [round_w3(w3_raw[0], at([P, 4 * N], BF16, "w3_bf0", w3_bf_at[0]), 4)]
-        w3_bf.append(round_w3(w3_raw[1], at([P, 4 * N], BF16, "w3_bf1", w3_bf_at[1]), 0))
+        w3_bf = [
+            [
+                round_w3(w3_raw[0], 0, 2 * [on_gpsimd], at([P, 2 * N], BF16, "w3_bf00", w3_bf_at[0])),
+                round_w3(w3_raw[0], 2, 2 * [on_scalar], at([P, 2 * N], BF16, "w3_bf02", site_at[0, 2])),
+            ],
+            [round_w3(w3_raw[1], 0, [on_gpsimd] + 3 * [on_scalar], at([P, 4 * N], BF16, "w3_bf1", w3_bf_at[1]))],
+        ]
         site_sums(1, 2, 4)
         site_sums(1, 3, 6)
         match(1, 0)

@@ -204,7 +204,7 @@ def tile_list_guide_cleavage_scores_kernel(
             return [plane[4:, c0 : c0 + CHUNK] for c0 in range(0, width, CHUNK)]
 
         plane2 = gather_plane2(0, S - PAIR, table2_at)
-        copies = 2 * [on_scalar] + 2 * [on_gpsimd]
+        copies = 3 * [on_scalar] + [on_gpsimd]
         w2_bf = [round_w2(0, copies, held([P, 4 * HALF], BF16, "w2_bf0"))]
         w2_q = [quantize_weight([w2_bf[0]], held([P, HALF], U32, "w2q0_codes"), "w2q0")]
         plane2.extend(gather_plane2(S - PAIR, PAIR, w2a_at + big_bytes // 4))

from contextlib import ExitStack

import concourse.mybir as mybir

K, K2, H, N, T, S = 1024, 512, 1024, 512, 2048, 1024
FLOPS = 2 * S * (K * H + K2 * H + H * N)

F32 = mybir.dt.float32
BF16 = mybir.dt.bfloat16
I32 = mybir.dt.int32
U32 = mybir.dt.uint32
U16 = mybir.dt.uint16
U8 = mybir.dt.uint8
FP8X4 = mybir.dt.float8_e4m3fn_x4
FP4X4 = mybir.dt.float4_e2m1fn_x4
MULT = mybir.AluOpType.mult
ADD = mybir.AluOpType.add
IDENT = mybir.ActivationFunctionType.Identity

P = 128
HALF = 512
CHUNK = 128
PAIR = 2 * CHUNK
BANK_BYTES = 2048
QUADRANTS = (0, 2, 1, 3)


def tile_list_guide_cleavage_scores_kernel(
    tc, tab_words, tab_scales, offs, tab2_words, tab2_scales, offs2, w1_words, w1_scales, w2, w3, bias, out
):
    nc = tc.nc
    with ExitStack() as ctx:
        keep = ctx.enter_context(tc.tile_pool(name="keep", bufs=1))
        placed = ctx.enter_context(tc.tile_pool(name="placed", bufs=1))
        psum = ctx.enter_context(tc.psum_pool(name="psum", bufs=1))

        def held(shape, dtype, name):
            return keep.tile(shape, dtype, name=name, align_bytes=64)

        def at(shape, dtype, name, offset):
            return placed.tile(shape, dtype, name=name, offset=offset, align_bytes=64)

        def bank_tile(shape, name, bank):
            return psum.tile(shape, F32, name=name, offset=bank * BANK_BYTES)

        big_bytes = 4 * T
        table2_at = 0
        w2b_at = table2_at + big_bytes
        w3_bf_at = [w2b_at + big_bytes + b * big_bytes // 2 for b in range(2)]
        w3b_at = w3_bf_at[1] + big_bytes // 2
        w2a_at = w3b_at + big_bytes + big_bytes // 4
        site_at = {(0, 2): w2a_at - big_bytes // 4, (0, 3): w2a_at + big_bytes // 2}
        site_at[1, 2], site_at[1, 3] = w3b_at, w3b_at + big_bytes // 2
        site_at[1, 0], site_at[1, 1] = w2b_at, w2b_at + big_bytes // 2
        h_at = {(1, HALF): w3_bf_at[1]}

        def load_table(words, tile):
            nc.sync.dma_start(tile[:], words.rearrange("p t i -> p (t i)").bitcast(I32))
            return tile

        def load_w1(b):
            raw = held([P, 2, HALF // 2], I32, f"w1_raw{b}")
            nc.sync.dma_start(raw[:], w1_words.rearrange("a p n -> p a n")[:, :, b * H : (b + 1) * H].bitcast(I32))
            return raw

        def load_w2(b, raw):
            nc.sync.dma_start(raw[:], w2.rearrange("(p s) n -> p s n", s=4)[:, :, b * HALF : (b + 1) * HALF])
            return raw

        def load_w3(b, raw):
            by_t = w3[b * HALF : (b + 1) * HALF, :].rearrange("(u t i) n -> t u i n", t=4, i=8)
            for t in range(4):
                nc.sync.dma_start(raw[:, t, :], by_t[t])
            return raw

        list1 = keep.tile([P, S // 16], U16, name="list1")
        list2 = keep.tile([P, S // 16], U16, name="list2")
        scale_win = held([P, T // 4], I32, "scale_win")
        scale_win2 = held([P, T // 4], I32, "scale_win2")
        w1s_raw = held([P, 2, H // 4], I32, "w1s_raw")
        planes = held([P, 2, S // 4], I32, "planes")
        nc.gpsimd.memset(scale_win[:], 0)
        w1_planes = held([P, 2 * H // 4], I32, "w1_planes")
        for tile in (scale_win2, w1_planes, planes):
            nc.vector.memset(tile[:], 0)
        nc.sync.dma_start(list1[:], offs)
        nc.sync.dma_start(list2[:], offs2)
        for d in QUADRANTS:
            rows = w1_scales[:, 4 * d : 4 * d + 4, :].rearrange("a e n -> e a n")
            nc.scalar.dma_start(w1s_raw[32 * d : 32 * d + 4], rows.bitcast(I32))
        nc.sync.dma_start(scale_win[::4], tab_scales.rearrange("a q t -> q a t").bitcast(I32))
        table0 = load_table(tab_words[0], held([P, T], I32, "table0"))
        for e in range(4):
            nc.gpsimd.dma_start(scale_win2[4 + e :: 32], tab2_scales[0, e::4, :].bitcast(I32))
        w1_raw = [load_w1(0)]
        table1 = load_table(tab_words[1], held([P, T], I32, "table1"))

        picked_scales = held([P, S], U8, "picked_scales")
        nc.vector.tensor_copy(picked_scales[:], scale_win[:].bitcast(U8).indirect(list1[:]))
        for d in QUADRANTS:
            nc.sync.dma_start(planes[32 * d : 32 * d + 4], picked_scales[32 * d : 32 * d + 32 : 4].bitcast(I32))
        table2 = load_table(tab2_words[0], at([P, T], I32, "table2", table2_at))
        w2_raw = [load_w2(0, at([P, 4, HALF], F32, "w2_raw0", w2a_at))]

        def gather_pieces(window, offsets, widths, name):
            picked = held([P, S], U32, name)
            j0 = 0
            for width in widths:
                cols = slice(j0 // 16, (j0 + width) // 16)
                nc.vector.tensor_copy(picked[:, j0 : j0 + width], window[:].bitcast(U32).indirect(offsets[:, cols]))
                j0 = j0 + width
            return picked

        picked = [gather_pieces(table0, list1, (S,), "picked0")]
        picked.append(gather_pieces(table1, list1, (PAIR, PAIR, HALF), "picked1"))
        w1_raw.append(load_w1(1))
        w2_raw.append(load_w2(1, at([P, 4, HALF], F32, "w2_raw1", w2b_at)))
        w3_raw = [load_w3(0, held([P, 4, N], F32, "w3_raw0")), load_w3(1, at([P, 4, N], F32, "w3_raw1", w3b_at))]
        bias_col = held([P, N // P], F32, "bias_col")
        with nc.allow_non_contiguous_dma(reason="bias onto partitions"):
            nc.sync.dma_start(bias_col[:], bias.rearrange("(c p) -> p c", p=P))

        for d in QUADRANTS:
            rows = slice(32 * d, 32 * d + 4)
            nc.scalar.copy(
                w1_planes[rows].bitcast(U32).rearrange("p (g t u i) -> p g t u i", g=4, t=4, i=2),
                w1s_raw[rows].bitcast(U32).rearrange("p a (b u t i) -> p (a b) t u i", b=2, t=4, i=2),
            )

        def order_w1(b):
            ordered = held([P, HALF], U32, f"w1_ord{b}")
            nc.scalar.copy(
                ordered[:].rearrange("p (a t u i) -> p a t u i", a=2, t=4, i=4),
                w1_raw[b][:].bitcast(U32).rearrange("p a (u t i) -> p a t u i", t=4, i=4),
            )
            return ordered

        def on_scalar(dst, src):
            nc.scalar.copy(dst.rearrange("p u (h i) s -> p u h s i", i=4), src.rearrange("p u (h i) s -> p u h s i", i=4))

        def on_gpsimd(dst, src):
            nc.gpsimd.tensor_scalar(dst, src, 1.0, 0.0, MULT, ADD)

        def round_w2(b, copies, rounded):
            dst = rounded[:].rearrange("p (t u i s) -> p t u i s", t=4, i=8, s=4)
            src = w2_raw[b][:].rearrange("p s (u t i) -> p t u i s", t=4, i=8)
            for t, copy in enumerate(copies):
                copy(dst[:, t], src[:, t])
            return rounded

        def round_w3(raw, first, copies, rounded):
            dst = rounded[:].rearrange("p (c u i t) -> p c u i t", u=16, i=8, t=4)
            src = raw[:].rearrange("p t (c u i) -> p c u i t", u=16, i=8)
            for k, copy in enumerate(copies):
                copy(dst[:, k], src[:, first + k])
            return rounded

        def quantize(values, codes, scales):
            nc.vector.quantize_mx(out=codes.bitcast(FP8X4), scales=scales, in_=values)

        def quantize_weight(parts, codes, name):
            scales = held([P, HALF], U8, name + "_scales")
            width = HALF // len(parts)
            for k, rounded in enumerate(parts):
                quantize(rounded[:], codes[:, k * width : (k + 1) * width], scales[:, k * width : (k + 1) * width])
            return codes, scales

        w1_ord = [order_w1(0)]

        site = {}

        def site_sums(b, pair, first_bank):
            if (b, pair) in site_at:
                sums = at([P, 4, PAIR], F32, f"site{b}{pair}", site_at[b, pair])
            else:
                sums = held([P, 4, PAIR], F32, f"site{b}{pair}")
            for k in range(2):
                bank = bank_tile([P, 2, PAIR], f"site_bank{b}{pair}{k}", first_bank + k)
                for a in range(2):
                    for e in range(2):
                        word = a * HALF + (2 * k + e) * P
                        col = a * H + b * HALF + (2 * k + e) * P
                        nc.tensor.matmul_mx(
                            out=bank[:, e, :],
                            lhsT=w1_ord[b][:].bitcast(U8)[:, 2 * word : 2 * (word + P)].bitcast(FP4X4),
                            lhsT_scale=w1_planes[:].bitcast(U8)[:, col : col + P],
                            rhs=picked[a][:, pair * PAIR : (pair + 1) * PAIR].bitcast(FP8X4),
                            rhs_scale=planes[:, a, :].bitcast(U8)[:, pair * PAIR : (pair + 1) * PAIR],
                            start=(a == 0 and e == 0),
                            stop=(a == 1 and e == 1),
                        )
                nc.scalar.activation(sums[:, 2 * k : 2 * k + 2, :], bank[:], IDENT)
            site[b, pair] = sums

        site_sums(0, 0, 0)
        site_sums(0, 1, 2)

        picked2 = gather_pieces(table2, list2, (S,), "picked2")

        def gather_plane2(j0, width, offset):
            plane = at([P, width], U8, f"plane2_{j0}", offset)
            cols = slice(j0 // 16, (j0 + width) // 16)
            nc.vector.tensor_copy(plane[:], scale_win2[:].bitcast(U8).indirect(list2[:, cols]))
            return [plane[4:, c0 : c0 + CHUNK] for c0 in range(0, width, CHUNK)]

        plane2 = gather_plane2(0, S - PAIR, table2_at)
        copies = 3 * [on_scalar] + [on_gpsimd]
        w2_bf = [round_w2(0, copies, held([P, 4 * HALF], BF16, "w2_bf0"))]
        w2_q = [quantize_weight([w2_bf[0]], held([P, HALF], U32, "w2q0_codes"), "w2q0")]
        plane2.extend(gather_plane2(S - PAIR, PAIR, w2a_at + big_bytes // 4))

        window = {}

        def window_sums(b, chunks, first_bank):
            for k, chunk in enumerate(chunks):
                j0 = chunk * CHUNK
                bank = bank_tile([P, 4, CHUNK], f"window_bank{b}{chunk}", first_bank + k)
                for t in range(4):
                    nc.tensor.matmul_mx(
                        out=bank[:, t, :],
                        lhsT=w2_q[b][0][:, t * P : (t + 1) * P].bitcast(FP8X4),
                        lhsT_scale=w2_q[b][1][:, t * P : (t + 1) * P],
                        rhs=picked2[:, j0 : j0 + CHUNK].bitcast(FP8X4),
                        rhs_scale=plane2[chunk],
                        start=True,
                        stop=True,
                    )
                window[b, chunk] = bank

        h_bf, h_q = {}, {}
        segments = ((0, HALF), (HALF, PAIR), (6 * CHUNK, CHUNK), (7 * CHUNK, CHUNK))

        def match(b, chunk):
            pair, k = divmod(chunk, 2)
            j0, width = [seg for seg in segments if seg[0] <= chunk * CHUNK][-1]
            if (b, j0) not in h_bf:
                if (b, j0) in h_at:
                    h_bf[b, j0] = at([P, 4 * width], BF16, f"h{b}_{j0}", h_at[b, j0])
                else:
                    h_bf[b, j0] = held([P, 4 * width], BF16, f"h{b}_{j0}")
            c0 = 4 * (chunk * CHUNK - j0)
            nc.vector.tensor_tensor(
                h_bf[b, j0][:, c0 : c0 + 4 * CHUNK].rearrange("p (g i t) -> p g t i", i=2, t=4),
                window[b, chunk][:].rearrange("p t (g i) -> p g t i", i=2),
                site[b, pair][:, :, k * CHUNK : (k + 1) * CHUNK].rearrange("p t (g i) -> p g t i", i=2),
                MULT,
            )

        def quantize_h(b, j0, width, offset=None):
            if offset is None:
                codes = held([P, width], U32, f"h_codes{b}_{j0}")
            else:
                codes = at([P, width], U32, f"h_codes{b}_{j0}", offset)
            scales = held([P, width], U8, f"h_scales{b}_{j0}")
            quantize(h_bf[b, j0][:], codes[:], scales[:])
            h_q[b, j0] = (codes, scales)

        out_rows = out.rearrange("(c p) j -> p c j", p=P)

        def score(j0, width, bank_numbers, by_vector=()):
            blocks = N // P // len(bank_numbers)
            for g, number in enumerate(bank_numbers):
                c0 = g * blocks
                res = held([P, blocks, width], F32, f"res{j0}_{c0}")
                bank = bank_tile([P, blocks, width], f"score_bank{j0}_{c0}", number)
                for b in range(2):
                    for k in range(blocks):
                        c = c0 + k
                        nc.tensor.matmul_mx(
                            out=bank[:, k, :],
                            lhsT=w3_q[b][0][:, c * P : (c + 1) * P].bitcast(FP8X4),
                            lhsT_scale=w3_q[b][1][:, c * P : (c + 1) * P],
                            rhs=h_q[b, j0][0][:].bitcast(FP8X4),
                            rhs_scale=h_q[b, j0][1][:],
                            start=(b == 0 and k == 0),
                            stop=(b == 1 and k == blocks - 1),
                        )
                if g in by_vector:
                    spread = bias_col[:, c0 : c0 + blocks].unsqueeze(2).to_broadcast([P, blocks, width])
                    nc.vector.tensor_tensor(res[:], bank[:], spread, ADD)
                else:
                    for k in range(blocks):
                        c = c0 + k
                        nc.scalar.activation(res[:, k, :], bank[:, k, :], IDENT, bias=bias_col[:, c : c + 1])
                nc.sync.dma_start(out_rows[:, c0 : c0 + blocks, j0 : j0 + width], res[:])

        window_sums(0, (0, 1, 2, 3), 0)
        w1_ord.append(order_w1(1))
        site_sums(0, 2, 4)
        site_sums(0, 3, 6)
        w2_bf.append(round_w2(1, 2 * [on_gpsimd] + 2 * [on_scalar], held([P, 4 * HALF], BF16, "w2_bf1")))
        match(0, 0)
        match(0, 1)
        window_sums(0, (4, 5), 0)
        site_sums(1, 0, 4)
        site_sums(1, 1, 6)
        match(0, 2)
        match(0, 3)
        w2_q.append(quantize_weight([w2_bf[1]], held([P, HALF], U32, "w2q1_codes"), "w2q1"))
        match(0, 4)
        match(0, 5)
        window_sums(1, (0, 1), 2)
        window_sums(1, (2, 3), 0)
        w3_bf = [
            [
                round_w3(w3_raw[0], 0, 2 * [on_gpsimd], at([P, 2 * N], BF16, "w3_bf00", w3_bf_at[0])),
                round_w3(w3_raw[0], 2, 2 * [on_scalar], at([P, 2 * N], BF16, "w3_bf02", site_at[0, 2])),
            ],
            [round_w3(w3_raw[1], 0, [on_gpsimd] + 3 * [on_scalar], at([P, 4 * N], BF16, "w3_bf1", w3_bf_at[1]))],
        ]
        site_sums(1, 2, 4)
        site_sums(1, 3, 6)
        match(1, 0)
        match(1, 1)
        window_sums(1, (4, 5), 2)
        match(1, 2)
        match(1, 3)
        w3_q = [quantize_weight(w3_bf[0], at([P, N], U32, "w3q0_codes", site_at[1, 0]), "w3q0")]
        quantize_h(0, 0, HALF, site_at[1, 0] + big_bytes // 4)
        w3_q.append(quantize_weight(w3_bf[1], held([P, N], U32, "w3q1_codes"), "w3q1"))
        quantize_h(1, 0, HALF)
        match(1, 4)
        match(1, 5)
        score(0, HALF, (0, 1, 4, 5))

        for b in range(2):
            window_sums(b, (6,), 6 + b)
        quantize_h(0, HALF, PAIR, w3_bf_at[0])
        quantize_h(1, HALF, PAIR)
        match(0, 6)
        for b in range(2):
            window_sums(b, (7,), 2 + b)
        score(HALF, PAIR, (0, 1))
        match(1, 6)
        quantize_h(0, 6 * CHUNK, CHUNK)
        match(0, 7)
        quantize_h(1, 6 * CHUNK, CHUNK)
        score(6 * CHUNK, CHUNK, (4,))
        match(1, 7)
        quantize_h(0, 7 * CHUNK, CHUNK)
        quantize_h(1, 7 * CHUNK, CHUNK)
        score(7 * CHUNK, CHUNK, (5, 6), by_vector=(1,))
